import numpy as np
import ml_dtypes


def mxq(x, axis, fmt="e4m3"):
    dtype, down = {"e4m3": (ml_dtypes.float8_e4m3fn, 7), "e5m2": (ml_dtypes.float8_e5m2, 14)}[fmt]
    v = np.moveaxis(np.asarray(x, np.float32).astype(ml_dtypes.bfloat16).astype(np.float64), axis, -1)
    blocks = v.reshape(v.shape[:-1] + (-1, 32))
    amax = np.abs(blocks).max(-1, keepdims=True)
    byte = np.maximum(np.where(amax > 0, np.frexp(amax)[1] - 1 + 127, 0) - down, 1)
    scale = np.exp2(byte - 127.0)
    codes = (blocks / scale).astype(np.float32).astype(dtype).astype(np.float64)
    return np.moveaxis((codes * scale).reshape(v.shape), -1, axis)


WIDE = False


def mx_kscale(k):
    if not WIDE:
        return np.ones(k)
    levels = np.array([10, -10, 5, -5, 0])
    if k % 512:
        return np.exp2(np.random.permutation(np.resize(levels, k // 32))).repeat(32)
    a = np.empty((k // 512, 16))
    for p in range(k // 512):
        a[p, :8] = np.random.permutation(np.resize(levels, 8))
        for g in range(8):
            far = levels[np.abs(levels - a[p, g]) >= 10]
            a[p, g + 8] = far[np.random.randint(len(far))]
    return np.exp2(a.ravel()).repeat(32)


def f64(x):
    return np.asarray(x).astype(np.float64)


def striped(idx):
    return np.tile(idx.reshape(-1, 16).T, (8, 1)).astype(np.uint16)


def unstriped(offs):
    return offs[:16].T.reshape(-1).astype(np.int64)


E2M1 = np.array([0.0, 0.5, 1.0, 1.5, 2.0, 3.0, 4.0, 6.0, -0.0, -0.5, -1.0, -1.5, -2.0, -3.0, -4.0, -6.0])


def pack_weight(w, fmt):
    k, n = w.shape
    w = f64(np.asarray(w, np.float32).astype(ml_dtypes.bfloat16)).reshape(k // 32, 32, n)
    amax = np.abs(w).max(1)
    if fmt == "e4m3":
        byte = np.frexp(amax)[1] - 1 + 127 - 7
    else:
        mant, ex = np.frexp(amax / 6.0)
        byte = np.where(mant > 0.5, ex, ex - 1) + 127
    byte = np.clip(np.where(amax > 0, byte, 1), 1, 254)
    scaled = (w * np.exp2(127.0 - byte)[:, None, :]).reshape(k, n).astype(np.float32)
    by_word = np.ascontiguousarray(scaled.reshape(k // 512, 128, 4, n).transpose(0, 1, 3, 2))
    if fmt == "e4m3":
        words = by_word.astype(ml_dtypes.float8_e4m3fn).view(np.uint8)
    else:
        c = by_word.astype(ml_dtypes.float4_e2m1fn).view(np.uint8) & 0xF
        words = (c[..., 0::2] | (c[..., 1::2] << 4)).reshape(k // 512, 128, 2 * n)
    return np.ascontiguousarray(words), np.ascontiguousarray(byte.astype(np.uint8).reshape(k // 512, 16, n))


def unpack_weight(words, scales, fmt):
    g, _, n = scales.shape
    words = np.ascontiguousarray(words).reshape(g, 128, n, -1)
    if fmt == "e4m3":
        vals = words.view(ml_dtypes.float8_e4m3fn).astype(np.float64)
    else:
        nib = np.empty((g, 128, n, 4), np.uint8)
        nib[..., 0::2] = words & 0xF
        nib[..., 1::2] = words >> 4
        vals = E2M1[nib]
    vals = vals * np.repeat(np.exp2(scales.astype(np.float64) - 127.0), 8, axis=1)[..., None]
    return vals.transpose(0, 1, 3, 2).reshape(g * 512, n)


def silu(v):
    return v / (1.0 + np.exp(-np.maximum(v, -700.0)))


K, M, T, S = 512, 512, 4096, 2048


def setup_inputs():
    n = np.random.standard_normal
    s = mx_kscale(K)[:, None]
    s2 = mx_kscale(512)[:, None]
    v = pack_weight(n((K, T)) * s, "e4m3")
    p_w4 = pack_weight(n((K, M)) / np.sqrt(K) / s, "e2m1")
    return {
        "tab_words": v[0],
        "tab_scales": v[1],
        "w4_words": p_w4[0],
        "w4_scales": p_w4[1],
        "c": (n((512, S)) * s2).astype(np.float32),
        "u": (n((512, M)) / np.sqrt(512) / s2).astype(np.float32),
        "ts": np.tile(np.exp(0.5 * n(T)), (128, 1)).astype(np.float32),
        "b": (0.3 * n(512)).astype(np.float32),
        "offs": striped(np.random.permutation(T)[:S]),
    }


def reference(tab_words, tab_scales, w4_words, w4_scales, c, u, ts, b, offs):
    tab_ = unpack_weight(tab_words, tab_scales, "e4m3")[:, unstriped(offs)]
    w4_ = unpack_weight(w4_words, w4_scales, "e2m1")
    c_ = mxq(f64(c), 0, "e4m3")
    u_ = mxq(f64(u), 0, "e4m3")
    y = w4_.T @ tab_ + u_.T @ c_
    y = y * f64(ts)[0][unstriped(offs)]
    return silu(y + f64(b)[:, None])

@@ -1,0 +1,218 @@
+from contextlib import ExitStack
+
+import concourse.mybir as mybir
+from concourse.masks import make_identity
+
+K, M, T, S = 512, 512, 4096, 2048
+FLOPS = 2 * 2 * K * M * S
+
+F32 = mybir.dt.float32
+BF16 = mybir.dt.bfloat16
+I32 = mybir.dt.int32
+U32 = mybir.dt.uint32
+U16 = mybir.dt.uint16
+U8 = mybir.dt.uint8
+FP8X4 = mybir.dt.float8_e4m3fn_x4
+FP4X4 = mybir.dt.float4_e2m1fn_x4
+ACT = mybir.ActivationFunctionType
+ALU = mybir.AluOpType
+
+P = 128
+PACK = 4
+CHUNK = 512
+N_CHUNKS = S // CHUNK
+N_TILES = M // P
+BLOCKS = CHUNK // P
+IL = {"u": "vector", 0: "gpsimd", 1: "gpsimd", 2: "gpsimd", 3: "gpsimd"}
+SCALE_TILES = 3
+
+
+def tile_list_tabts_silu_kernel(tc, tab_words, tab_scales, w4_words, w4_scales, c, u, ts, b, offs, out):
+    nc = tc.nc
+    with ExitStack() as ctx:
+        keep = ctx.enter_context(tc.tile_pool(name="keep", bufs=1))
+        work = ctx.enter_context(tc.tile_pool(name="work", bufs=4))
+        acc_pool = ctx.enter_context(tc.psum_pool(name="acc", bufs=4))
+        turn_pool = ctx.enter_context(tc.psum_pool(name="turn", bufs=4))
+
+        offsets = keep.tile([P, S // 16], U16, name="offsets")
+        tab_s = keep.tile([P, T // 4], I32, name="tab_s", align_bytes=64)
+        ts_rows = keep.tile([P, P], F32, name="ts_rows", tag="c_rows", align_bytes=64)
+        ts_cols = [keep.tile([P, T // P // 2], F32, name="ts_cols%d" % h, tag=tag, align_bytes=64) for h, tag in enumerate(("table", "w4"))]
+        ts_all = keep.tile([P, T], F32, name="ts_all", align_bytes=64)
+        bias = keep.tile([P, N_TILES], F32, name="bias")
+        ident = keep.tile([P, P], F32, name="ident")
+        warm = keep.tile([P, 1], F32, name="warm")
+        u_raw = keep.tile([P, PACK, M], F32, name="u_raw", tag="u_rows", align_bytes=64)
+
+        nc.vector.memset(tab_s[:], 0)
+        make_identity(nc, ident[:])
+        nc.scalar.activation(warm[:], ident[:, 0:1], ACT.Silu)
+
+        nc.sync.dma_start(offsets[:], offs)
+        nc.sync.dma_start(ts_rows[:], ts[0:PACK, :].rearrange("r (a p) -> (r a) p", p=P))
+        nc.sync.dma_start(u_raw[:], u.rearrange("(p i) n -> p i n", i=PACK))
+        for q in range(4):
+            nc.sync.dma_start(tab_s[32 * q : 32 * q + 4, :], tab_scales[0, 4 * q : 4 * q + 4, :].bitcast(I32))
+
+        half = T // P // 2
+        turned = turn_pool.tile([P, CHUNK], F32, name="turned")
+        nc.tensor.transpose(turned[:, 0:P], ts_rows[:], ident[:])
+        for h in range(2):
+            nc.scalar.copy(ts_cols[h][:], turned[:, h * half : (h + 1) * half])
+        c_rows = keep.tile([P, 2, PACK, CHUNK], F32, name="c_rows", tag="c_rows", align_bytes=64)
+        c_raw = [c_rows[:, i % 2] for i in range(N_CHUNKS)]
+
+        def load_c(i):
+            nc.sync.dma_start(c_raw[i], c[:, i * CHUNK : (i + 1) * CHUNK].rearrange("(p i) j -> p i j", i=PACK))
+
+        load_c(0)
+        load_c(1)
+        for g in range(T // CHUNK):
+            turned = turn_pool.tile([P, CHUNK], F32, name="turned")
+            for a in range(BLOCKS):
+                col = g * BLOCKS + a
+                nc.tensor.transpose(turned[:, a * P : (a + 1) * P], ts_cols[col // half][:, col % half : col % half + 1].to_broadcast([P, P]), ident[:])
+            nc.scalar.copy(ts_all[:, g * CHUNK : (g + 1) * CHUNK], turned[:])
+        tab_w = keep.tile([P, T], I32, name="tab_w", tag="table", align_bytes=64)
+        nc.sync.dma_start(tab_w[:], tab_words[0].rearrange("p t i -> p (t i)").bitcast(I32))
+        w4 = keep.tile([P, 3 * M // 4], I32, name="w4", tag="w4", align_bytes=64)
+        w4_w = w4[:, 0 : 2 * M // 4]
+        w4_s = w4[:, 2 * M // 4 : 3 * M // 4]
+        nc.sync.dma_start(w4_w, w4_words[0].bitcast(I32))
+        nc.gpsimd.memset(w4_s, 0)
+        for q in range(4):
+            nc.sync.dma_start(w4[32 * q : 32 * q + 4, 2 * M // 4 : 3 * M // 4], w4_scales[0, 4 * q : 4 * q + 4, :].bitcast(I32))
+
+        def load_bias():
+            b_rows = keep.tile([P, P], F32, name="b_rows")
+            nc.gpsimd.memset(b_rows[:], 0.0)
+            nc.sync.dma_start(b_rows[0:N_TILES, :], b.rearrange("(m p) -> m p", p=P))
+            turned = turn_pool.tile([P, CHUNK], F32, name="turned")
+            nc.tensor.transpose(turned[:, 0:P], b_rows[:], ident[:])
+            nc.scalar.copy(bias[:], turned[:, 0:N_TILES])
+
+        picked_w = [keep.tile([P, CHUNK], U32, name="picked_w%d" % i, align_bytes=64) for i in range(N_CHUNKS)]
+        picked_s = {}
+        picked_t = {}
+        blocks = [[keep.tile([P, M], F32, name="block%d_%d" % (i, a), align_bytes=64) for a in range(BLOCKS)] for i in range(2)]
+        u_bf = keep.tile([P, M, PACK], BF16, name="u_bf", align_bytes=64)
+        c_bf = [u_bf] * N_CHUNKS
+        c_w = [keep.tile([P, CHUNK], U32, name="c_w%d" % i, tag="c_w%d" % i, align_bytes=64) for i in range(N_CHUNKS)]
+        c_s = [keep.tile([P, CHUNK], U8, name="c_s%d" % i, align_bytes=64) for i in range(N_CHUNKS)]
+        u_w = keep.tile([P, M], U32, name="u_w", align_bytes=64)
+        u_s = keep.tile([P, M], U8, name="u_s", align_bytes=64)
+        ts_col = [keep.tile([P, BLOCKS], F32, name="ts_col%d" % i) for i in range(2)]
+
+        def listed(i):
+            return offsets[:, i * (CHUNK // 16) : (i + 1) * (CHUNK // 16)]
+
+        def pick_scales(i):
+            nc.vector.tensor_copy(picked_s[i % SCALE_TILES], tab_s[:].bitcast(U8).indirect(listed(i)))
+
+        def pick_words(i):
+            nc.vector.tensor_copy(picked_w[i][:], tab_w[:].bitcast(U32).indirect(listed(i)))
+
+        def pick_ts(i, tag):
+            picked_t[i] = keep.tile([P, CHUNK], F32, name="picked_t%d" % i, tag=tag, align_bytes=64)
+            nc.vector.tensor_copy(picked_t[i][:], ts_all[:].indirect(listed(i)))
+
+        def interleave(grouped, raw, engine):
+            dst = grouped[:].rearrange("p (g e) i -> p g i e", e=4)
+            src = raw.rearrange("p i (g e) -> p g i e", e=4)
+            if engine == "scalar":
+                nc.scalar.copy(dst, src)
+            elif engine == "vector":
+                nc.vector.tensor_copy(dst, src)
+            else:
+                nc.gpsimd.tensor_scalar(grouped[:], raw.rearrange("p i w -> p w i"), 1.0, 0.0, ALU.mult, ALU.add)
+
+        def quantize(words, scales, grouped):
+            nc.vector.quantize_mx(out=words[:].bitcast(FP8X4), scales=scales[:], in_=grouped[:].rearrange("p w i -> p (w i)"))
+
+        def il_c(i):
+            interleave(c_bf[i], c_raw[i], IL[i])
+
+        def q_c(i):
+            quantize(c_w[i], c_s[i], c_bf[i])
+
+        w4_bytes = w4_w.bitcast(U8)
+        w4_plane = w4_s.bitcast(U8)
+
+        def finish(i, m, src):
+            result = work.tile([P, CHUNK], F32, name="result", bufs=16)
+            nc.scalar.activation(result[:], src, ACT.Silu, bias=bias[:, m : m + 1])
+            nc.sync.dma_start(out[m * P : (m + 1) * P, i * CHUNK : (i + 1) * CHUNK], result[:])
+
+        def direct(i, m):
+            cols = slice(m * P, (m + 1) * P)
+            acc = acc_pool.tile([P, CHUNK], F32, name="acc")
+            nc.tensor.matmul_mx(out=acc[:], lhsT=w4_bytes[:, 2 * m * P : 2 * (m + 1) * P].bitcast(FP4X4), lhsT_scale=w4_plane[:, cols],
+                                rhs=picked_w[i][:].bitcast(FP8X4), rhs_scale=picked_s[i % SCALE_TILES], start=True, stop=False)
+            nc.tensor.matmul_mx(out=acc[:], lhsT=u_w[:, cols].bitcast(FP8X4), lhsT_scale=u_s[:, cols],
+                                rhs=c_w[i][:].bitcast(FP8X4), rhs_scale=c_s[i][:], start=False, stop=True)
+            scaled = work.tile([P, CHUNK], F32, name="scaled", bufs=8)
+            nc.vector.tensor_tensor(scaled[:], acc[:], picked_t[i][:], ALU.mult)
+            finish(i, m, scaled[:])
+
+        def ts_to_partitions(i):
+            turned = turn_pool.tile([P, CHUNK], F32, name="turned")
+            for a in range(BLOCKS):
+                nc.tensor.transpose(turned[:, a * P : (a + 1) * P], picked_t[i][:, a * P : (a + 1) * P], ident[:])
+            nc.scalar.copy(ts_col[i][:], turned[:, 0:CHUNK:P])
+
+        def turned_sums(i):
+            for a in range(BLOCKS):
+                cols = slice(a * P, (a + 1) * P)
+                acc = acc_pool.tile([P, M], F32, name="acc")
+                nc.tensor.matmul_mx(out=acc[:], lhsT=picked_w[i][:, cols].bitcast(FP8X4), lhsT_scale=picked_s[i % SCALE_TILES][:, cols],
+                                    rhs=w4_bytes.bitcast(FP4X4), rhs_scale=w4_plane, start=True, stop=False)
+                nc.tensor.matmul_mx(out=acc[:], lhsT=c_w[i][:, cols].bitcast(FP8X4), lhsT_scale=c_s[i][:, cols],
+                                    rhs=u_w[:].bitcast(FP8X4), rhs_scale=u_s[:], start=False, stop=True)
+                nc.scalar.activation(blocks[i][a][:], acc[:], ACT.Copy, scale=ts_col[i][:, a : a + 1])
+
+        def turn_back(i):
+            for m in range(N_TILES):
+                turned = turn_pool.tile([P, CHUNK], F32, name="turned")
+                for a in range(BLOCKS):
+                    nc.tensor.transpose(turned[:, a * P : (a + 1) * P], blocks[i][a][:, m * P : (m + 1) * P], ident[:])
+                finish(i, m, turned[:])
+
+        load_bias()
+        interleave(u_bf, u_raw[:], IL["u"])
+        planes = keep.tile([P, SCALE_TILES, CHUNK], U8, name="planes", tag="u_rows", align_bytes=64)
+        for i in range(SCALE_TILES):
+            picked_s[i] = planes[:, i, :]
+        pick_scales(0)
+        quantize(u_w, u_s, u_bf)
+        il_c(0)
+        load_c(2)
+        pick_scales(1)
+        pick_ts(0, "ts0")
+        ts_to_partitions(0)
+        q_c(0)
+        il_c(1)
+        load_c(3)
+        pick_words(0)
+        turned_sums(0)
+        pick_ts(1, "ts1")
+        ts_to_partitions(1)
+        q_c(1)
+        il_c(2)
+        pick_words(1)
+        pick_scales(2)
+        turned_sums(1)
+        turn_back(0)
+        pick_words(2)
+        q_c(2)
+        il_c(3)
+        pick_ts(2, "c_w0")
+        pick_scales(3)
+        pick_words(3)
+        q_c(3)
+        for m in range(N_TILES):
+            direct(2, m)
+        turn_back(1)
+        pick_ts(3, "c_w1")
+        for m in range(N_TILES):
+            direct(3, m)

@@ -1,7 +1,6 @@
 from contextlib import ExitStack
 
 import concourse.mybir as mybir
-from concourse.masks import make_identity
 
 K, M, T, S = 512, 512, 4096, 2048
 FLOPS = 2 * 2 * K * M * S
@@ -23,137 +22,150 @@ CHUNK = 512
 N_CHUNKS = S // CHUNK
 N_TILES = M // P
 BLOCKS = CHUNK // P
-IL = {"u": "vector", 0: "gpsimd", 1: "gpsimd", 2: "gpsimd", 3: "gpsimd"}
-SCALE_TILES = 3
+TS_PER_PARTITION = T // P
 
 
 def tile_list_tabts_silu_kernel(tc, tab_words, tab_scales, w4_words, w4_scales, c, u, ts, b, offs, out):
     nc = tc.nc
     with ExitStack() as ctx:
         keep = ctx.enter_context(tc.tile_pool(name="keep", bufs=1))
-        work = ctx.enter_context(tc.tile_pool(name="work", bufs=4))
+        work = ctx.enter_context(tc.tile_pool(name="work", bufs=1))
         acc_pool = ctx.enter_context(tc.psum_pool(name="acc", bufs=4))
         turn_pool = ctx.enter_context(tc.psum_pool(name="turn", bufs=4))
 
-        offsets = keep.tile([P, S // 16], U16, name="offsets")
-        tab_s = keep.tile([P, T // 4], I32, name="tab_s", align_bytes=64)
-        ts_rows = keep.tile([P, P], F32, name="ts_rows", tag="c_rows", align_bytes=64)
-        ts_cols = [keep.tile([P, T // P // 2], F32, name="ts_cols%d" % h, tag=tag, align_bytes=64) for h, tag in enumerate(("table", "w4"))]
-        ts_all = keep.tile([P, T], F32, name="ts_all", align_bytes=64)
-        bias = keep.tile([P, N_TILES], F32, name="bias")
-        ident = keep.tile([P, P], F32, name="ident")
-        warm = keep.tile([P, 1], F32, name="warm")
-        u_raw = keep.tile([P, PACK, M], F32, name="u_raw", tag="u_rows", align_bytes=64)
+        def kept(shape, dtype, name, tag=None):
+            return keep.tile(shape, dtype, name=name, tag=tag or name, align_bytes=64)
+
+        offsets = kept([P, S // 16], U16, "offsets")
+        tab_s = kept([P, T // 4], I32, "tab_s")
+        ts_cols = kept([P, TS_PER_PARTITION], F32, "ts_cols", "first_bf")
+        ts_all = kept([P, T], F32, "ts_all")
+        b_rows = kept([P, P], F32, "b_rows", "c_bf1")
+        bias = kept([P, N_TILES], F32, "bias")
+        zeros = kept([P, P], F32, "zeros", "rows")
+        ident = kept([P, P], F32, "ident")
+        warm = kept([P, 1], F32, "warm", "table")
+        warm_bias = kept([P, 1], F32, "warm_bias", "w4")
 
         nc.vector.memset(tab_s[:], 0)
-        make_identity(nc, ident[:])
-        nc.scalar.activation(warm[:], ident[:, 0:1], ACT.Silu)
+        nc.vector.memset(b_rows[:], 0.0)
+        nc.gpsimd.memset(zeros[:], 0.0)
+        nc.gpsimd.memset(warm_bias[:], 0.0)
+        nc.gpsimd.affine_select(
+            out=ident[:], in_=zeros[:], compare_op=ALU.not_equal, fill=1.0, base=0, pattern=[[-1, P]], channel_multiplier=1
+        )
+        nc.scalar.activation(warm[:], ident[:, 0:1], ACT.Silu, bias=warm_bias[:])
 
+        nc.sync.dma_start(ts_cols[:], ts[0].rearrange("(p a) -> p a", p=P))
         nc.sync.dma_start(offsets[:], offs)
-        nc.sync.dma_start(ts_rows[:], ts[0:PACK, :].rearrange("r (a p) -> (r a) p", p=P))
-        nc.sync.dma_start(u_raw[:], u.rearrange("(p i) n -> p i n", i=PACK))
-        for q in range(4):
-            nc.sync.dma_start(tab_s[32 * q : 32 * q + 4, :], tab_scales[0, 4 * q : 4 * q + 4, :].bitcast(I32))
+        for r in range(4):
+            nc.sync.dma_start(tab_s[r:P:32, :], tab_scales[0, r:16:4, :].bitcast(I32))
+        rows = kept([P, 3, PACK, CHUNK], F32, "rows")
+        u_raw = rows[:, 2]
+        c_raw = [rows[:, i % 3] for i in range(N_CHUNKS)]
 
-        half = T // P // 2
-        turned = turn_pool.tile([P, CHUNK], F32, name="turned")
-        nc.tensor.transpose(turned[:, 0:P], ts_rows[:], ident[:])
-        for h in range(2):
-            nc.scalar.copy(ts_cols[h][:], turned[:, h * half : (h + 1) * half])
-        c_rows = keep.tile([P, 2, PACK, CHUNK], F32, name="c_rows", tag="c_rows", align_bytes=64)
-        c_raw = [c_rows[:, i % 2] for i in range(N_CHUNKS)]
+        def load_rows(dst, src):
+            nc.sync.dma_start(dst, src.rearrange("(p i) j -> p i j", i=PACK))
 
         def load_c(i):
-            nc.sync.dma_start(c_raw[i], c[:, i * CHUNK : (i + 1) * CHUNK].rearrange("(p i) j -> p i j", i=PACK))
+            load_rows(c_raw[i], c[:, i * CHUNK : (i + 1) * CHUNK])
 
+        tab_w = kept([P, T], I32, "tab_w", "table")
+
+        def load_words():
+            nc.sync.dma_start(tab_w[:], tab_words[0].rearrange("p t i -> p (t i)").bitcast(I32))
+
+        nc.sync.dma_start(b_rows[0:N_TILES, :], b.rearrange("(m p) -> m p", p=P))
+        load_rows(u_raw, u)
         load_c(0)
         load_c(1)
+        load_words()
+        w4 = kept([P, 3 * M // 4], I32, "w4")
+        nc.sync.dma_start(w4[:, 0 : 2 * M // 4], w4_words[0].bitcast(I32))
+        nc.gpsimd.memset(w4[:, 2 * M // 4 : 3 * M // 4], 0)
+        for r in range(4):
+            nc.sync.dma_start(w4[r:P:32, 2 * M // 4 : 3 * M // 4], w4_scales[0, r:16:4, :].bitcast(I32))
+        w4_bytes = w4[:, 0 : 2 * M // 4].bitcast(U8)
+        w4_plane = w4[:, 2 * M // 4 : 3 * M // 4].bitcast(U8)
+
         for g in range(T // CHUNK):
             turned = turn_pool.tile([P, CHUNK], F32, name="turned")
             for a in range(BLOCKS):
                 col = g * BLOCKS + a
-                nc.tensor.transpose(turned[:, a * P : (a + 1) * P], ts_cols[col // half][:, col % half : col % half + 1].to_broadcast([P, P]), ident[:])
-            nc.scalar.copy(ts_all[:, g * CHUNK : (g + 1) * CHUNK], turned[:])
-        tab_w = keep.tile([P, T], I32, name="tab_w", tag="table", align_bytes=64)
-        nc.sync.dma_start(tab_w[:], tab_words[0].rearrange("p t i -> p (t i)").bitcast(I32))
-        w4 = keep.tile([P, 3 * M // 4], I32, name="w4", tag="w4", align_bytes=64)
-        w4_w = w4[:, 0 : 2 * M // 4]
-        w4_s = w4[:, 2 * M // 4 : 3 * M // 4]
-        nc.sync.dma_start(w4_w, w4_words[0].bitcast(I32))
-        nc.gpsimd.memset(w4_s, 0)
-        for q in range(4):
-            nc.sync.dma_start(w4[32 * q : 32 * q + 4, 2 * M // 4 : 3 * M // 4], w4_scales[0, 4 * q : 4 * q + 4, :].bitcast(I32))
+                nc.tensor.transpose(turned[:, a * P : (a + 1) * P], ts_cols[:, col : col + 1].to_broadcast([P, P]), ident[:])
+            nc.scalar.copy(
+                ts_all[:].rearrange("q (p a) -> q p a", p=P)[:, :, g * BLOCKS : (g + 1) * BLOCKS],
+                turned[:].rearrange("q (a p) -> q p a", p=P),
+            )
+        turned = turn_pool.tile([P, CHUNK], F32, name="turned")
+        nc.tensor.transpose(turned[:, 0:P], b_rows[:], ident[:])
+        nc.scalar.copy(bias[:], turned[:, 0:N_TILES])
 
-        def load_bias():
-            b_rows = keep.tile([P, P], F32, name="b_rows")
-            nc.gpsimd.memset(b_rows[:], 0.0)
-            nc.sync.dma_start(b_rows[0:N_TILES, :], b.rearrange("(m p) -> m p", p=P))
-            turned = turn_pool.tile([P, CHUNK], F32, name="turned")
-            nc.tensor.transpose(turned[:, 0:P], b_rows[:], ident[:])
-            nc.scalar.copy(bias[:], turned[:, 0:N_TILES])
-
-        picked_w = [keep.tile([P, CHUNK], U32, name="picked_w%d" % i, align_bytes=64) for i in range(N_CHUNKS)]
-        picked_s = {}
+        planes = kept([P, S], U8, "planes")
+        picked_s = [planes[:, i * CHUNK : (i + 1) * CHUNK] for i in range(N_CHUNKS)]
         picked_t = {}
-        blocks = [[keep.tile([P, M], F32, name="block%d_%d" % (i, a), align_bytes=64) for a in range(BLOCKS)] for i in range(2)]
-        u_bf = keep.tile([P, M, PACK], BF16, name="u_bf", align_bytes=64)
-        c_bf = [u_bf] * N_CHUNKS
-        c_w = [keep.tile([P, CHUNK], U32, name="c_w%d" % i, tag="c_w%d" % i, align_bytes=64) for i in range(N_CHUNKS)]
-        c_s = [keep.tile([P, CHUNK], U8, name="c_s%d" % i, align_bytes=64) for i in range(N_CHUNKS)]
-        u_w = keep.tile([P, M], U32, name="u_w", align_bytes=64)
-        u_s = keep.tile([P, M], U8, name="u_s", align_bytes=64)
-        ts_col = [keep.tile([P, BLOCKS], F32, name="ts_col%d" % i) for i in range(2)]
+        blocks = [[kept([P, M], F32, "block%d_%d" % (i, a)) for a in range(BLOCKS)] for i in range(2)]
+        first_bf = kept([P, M + CHUNK, PACK], BF16, "first_bf")
+        first_w = kept([P, M + CHUNK], U32, "first_w")
+        first_s = kept([P, M + CHUNK], U8, "first_s")
+        c_bf = [first_bf[:, M : M + CHUNK, :]] + [kept([P, CHUNK, PACK], BF16, "c_bf%d" % i, "c_bf%d" % (1 if i == 2 else i)) for i in range(1, N_CHUNKS)]
+        c_w = [first_w[:, M : M + CHUNK]] + [kept([P, CHUNK], U32, "c_w%d" % i) for i in range(1, N_CHUNKS)]
+        c_s = [first_s[:, M : M + CHUNK]] + [kept([P, CHUNK], U8, "c_s%d" % i) for i in range(1, N_CHUNKS)]
+        u_bf = first_bf[:, 0:M, :]
+        u_w = first_w[:, 0:M]
+        u_s = first_s[:, 0:M]
+        ts_col = [kept([P, BLOCKS], F32, "ts_col%d" % i) for i in range(2)]
 
-        def listed(i):
-            return offsets[:, i * (CHUNK // 16) : (i + 1) * (CHUNK // 16)]
+        def listed(i, n):
+            return offsets[:, i * (CHUNK // 16) : (i + n) * (CHUNK // 16)]
 
-        def pick_scales(i):
-            nc.vector.tensor_copy(picked_s[i % SCALE_TILES], tab_s[:].bitcast(U8).indirect(listed(i)))
+        def pick_scales(i, n):
+            nc.vector.tensor_copy(planes[:, i * CHUNK : (i + n) * CHUNK], tab_s[:].bitcast(U8).indirect(listed(i, n)))
 
-        def pick_words(i):
-            nc.vector.tensor_copy(picked_w[i][:], tab_w[:].bitcast(U32).indirect(listed(i)))
+        def pick_words(i, n=1):
+            nc.vector.tensor_copy(word_pair[:, (i % 2) * CHUNK : (i % 2 + n) * CHUNK], tab_w[:].bitcast(U32).indirect(listed(i, n)))
 
-        def pick_ts(i, tag):
-            picked_t[i] = keep.tile([P, CHUNK], F32, name="picked_t%d" % i, tag=tag, align_bytes=64)
-            nc.vector.tensor_copy(picked_t[i][:], ts_all[:].indirect(listed(i)))
+        def pick_ts(i, n, tag=None):
+            picked = kept([P, n * CHUNK], F32, "picked_t%d" % i, tag)
+            for k in range(n):
+                picked_t[i + k] = picked[:, k * CHUNK : (k + 1) * CHUNK]
+            nc.vector.tensor_copy(picked[:], ts_all[:].indirect(listed(i, n)))
 
-        def interleave(grouped, raw, engine):
-            dst = grouped[:].rearrange("p (g e) i -> p g i e", e=4)
-            src = raw.rearrange("p i (g e) -> p g i e", e=4)
-            if engine == "scalar":
-                nc.scalar.copy(dst, src)
-            elif engine == "vector":
-                nc.vector.tensor_copy(dst, src)
-            else:
-                nc.gpsimd.tensor_scalar(grouped[:], raw.rearrange("p i w -> p w i"), 1.0, 0.0, ALU.mult, ALU.add)
+        def interleave(copy, grouped, raw):
+            copy(grouped.rearrange("p (g e) i -> p g i e", e=4), raw.rearrange("p i (g e) -> p g i e", e=4))
+
+        def on_gpsimd(i, lo=0, hi=CHUNK):
+            nc.gpsimd.tensor_scalar(c_bf[i][:, lo:hi, :], c_raw[i][:, :, lo:hi].rearrange("p i w -> p w i"), 1.0, 0.0, ALU.mult, ALU.add)
+
+        def il_c(i, copy, lo=0, hi=CHUNK):
+            interleave(copy, c_bf[i][:, lo:hi, :], c_raw[i][:, :, lo:hi])
 
         def quantize(words, scales, grouped):
             nc.vector.quantize_mx(out=words[:].bitcast(FP8X4), scales=scales[:], in_=grouped[:].rearrange("p w i -> p (w i)"))
 
-        def il_c(i):
-            interleave(c_bf[i], c_raw[i], IL[i])
-
         def q_c(i):
             quantize(c_w[i], c_s[i], c_bf[i])
 
-        w4_bytes = w4_w.bitcast(U8)
-        w4_plane = w4_s.bitcast(U8)
-
-        def finish(i, m, src):
-            result = work.tile([P, CHUNK], F32, name="result", bufs=16)
+        def finish(i, m, src, lo=0, hi=CHUNK):
+            result = work.tile([P, hi - lo], F32, name="result", bufs=18)
             nc.scalar.activation(result[:], src, ACT.Silu, bias=bias[:, m : m + 1])
-            nc.sync.dma_start(out[m * P : (m + 1) * P, i * CHUNK : (i + 1) * CHUNK], result[:])
+            nc.sync.dma_start(out[m * P : (m + 1) * P, i * CHUNK + lo : i * CHUNK + hi], result[:])
 
-        def direct(i, m):
+        def open_sum(i, m):
             cols = slice(m * P, (m + 1) * P)
             acc = acc_pool.tile([P, CHUNK], F32, name="acc")
             nc.tensor.matmul_mx(out=acc[:], lhsT=w4_bytes[:, 2 * m * P : 2 * (m + 1) * P].bitcast(FP4X4), lhsT_scale=w4_plane[:, cols],
-                                rhs=picked_w[i][:].bitcast(FP8X4), rhs_scale=picked_s[i % SCALE_TILES], start=True, stop=False)
+                                rhs=word_pair[:, (i % 2) * CHUNK : (i % 2 + 1) * CHUNK].bitcast(FP8X4), rhs_scale=picked_s[i], start=True, stop=False)
+            return acc
+
+        def close_sum(i, m, acc, cuts=(0, CHUNK)):
+            cols = slice(m * P, (m + 1) * P)
             nc.tensor.matmul_mx(out=acc[:], lhsT=u_w[:, cols].bitcast(FP8X4), lhsT_scale=u_s[:, cols],
                                 rhs=c_w[i][:].bitcast(FP8X4), rhs_scale=c_s[i][:], start=False, stop=True)
-            scaled = work.tile([P, CHUNK], F32, name="scaled", bufs=8)
-            nc.vector.tensor_tensor(scaled[:], acc[:], picked_t[i][:], ALU.mult)
-            finish(i, m, scaled[:])
+            for lo, hi in zip(cuts, cuts[1:]):
+                scaled = work.tile([P, hi - lo], F32, name="scaled", bufs=10)
+                nc.vector.tensor_tensor(scaled[:], acc[:, lo:hi], picked_t[i][:, lo:hi], ALU.mult)
+                finish(i, m, scaled[:], lo, hi)
 
         def ts_to_partitions(i):
             turned = turn_pool.tile([P, CHUNK], F32, name="turned")
@@ -161,15 +173,18 @@ def tile_list_tabts_silu_kernel(tc, tab_words, tab_scales, w4_words, w4_scales, 
                 nc.tensor.transpose(turned[:, a * P : (a + 1) * P], picked_t[i][:, a * P : (a + 1) * P], ident[:])
             nc.scalar.copy(ts_col[i][:], turned[:, 0:CHUNK:P])
 
-        def turned_sums(i):
+        def turned_sums(i, on_vector=0):
             for a in range(BLOCKS):
                 cols = slice(a * P, (a + 1) * P)
                 acc = acc_pool.tile([P, M], F32, name="acc")
-                nc.tensor.matmul_mx(out=acc[:], lhsT=picked_w[i][:, cols].bitcast(FP8X4), lhsT_scale=picked_s[i % SCALE_TILES][:, cols],
-                                    rhs=w4_bytes.bitcast(FP4X4), rhs_scale=w4_plane, start=True, stop=False)
                 nc.tensor.matmul_mx(out=acc[:], lhsT=c_w[i][:, cols].bitcast(FP8X4), lhsT_scale=c_s[i][:, cols],
-                                    rhs=u_w[:].bitcast(FP8X4), rhs_scale=u_s[:], start=False, stop=True)
-                nc.scalar.activation(blocks[i][a][:], acc[:], ACT.Copy, scale=ts_col[i][:, a : a + 1])
+                                    rhs=u_w[:].bitcast(FP8X4), rhs_scale=u_s[:], start=True, stop=False)
+                nc.tensor.matmul_mx(out=acc[:], lhsT=word_pair[:, (i % 2) * CHUNK + a * P : (i % 2) * CHUNK + (a + 1) * P].bitcast(FP8X4), lhsT_scale=picked_s[i][:, cols],
+                                    rhs=w4_bytes.bitcast(FP4X4), rhs_scale=w4_plane, start=False, stop=True)
+                if a >= BLOCKS - on_vector:
+                    nc.vector.tensor_scalar(blocks[i][a][:], acc[:], ts_col[i][:, a : a + 1], None, ALU.mult)
+                else:
+                    nc.scalar.activation(blocks[i][a][:], acc[:], ACT.Copy, scale=ts_col[i][:, a : a + 1])
 
         def turn_back(i):
             for m in range(N_TILES):
@@ -178,41 +193,35 @@ def tile_list_tabts_silu_kernel(tc, tab_words, tab_scales, w4_words, w4_scales, 
                     nc.tensor.transpose(turned[:, a * P : (a + 1) * P], blocks[i][a][:, m * P : (m + 1) * P], ident[:])
                 finish(i, m, turned[:])
 
-        load_bias()
-        interleave(u_bf, u_raw[:], IL["u"])
-        planes = keep.tile([P, SCALE_TILES, CHUNK], U8, name="planes", tag="u_rows", align_bytes=64)
-        for i in range(SCALE_TILES):
-            picked_s[i] = planes[:, i, :]
-        pick_scales(0)
-        quantize(u_w, u_s, u_bf)
-        il_c(0)
+        interleave(nc.scalar.copy, u_bf[:], u_raw)
         load_c(2)
-        pick_scales(1)
-        pick_ts(0, "ts0")
-        ts_to_partitions(0)
-        q_c(0)
-        il_c(1)
+        il_c(0, nc.scalar.copy)
         load_c(3)
+        il_c(1, nc.scalar.copy)
+        pick_scales(0, N_CHUNKS)
+        pick_ts(0, 3)
+        ts_to_partitions(0)
+        ts_to_partitions(1)
+        quantize(first_w, first_s, first_bf)
+        word_pair = kept([P, 2 * CHUNK], U32, "word_pair", "first_bf")
         pick_words(0)
         turned_sums(0)
-        pick_ts(1, "ts1")
-        ts_to_partitions(1)
         q_c(1)
-        il_c(2)
         pick_words(1)
-        pick_scales(2)
         turned_sums(1)
         turn_back(0)
+        il_c(2, nc.vector.tensor_copy)
         pick_words(2)
-        q_c(2)
-        il_c(3)
-        pick_ts(2, "c_w0")
-        pick_scales(3)
-        pick_words(3)
-        q_c(3)
-        for m in range(N_TILES):
-            direct(2, m)
+        sums = [open_sum(2, m) for m in range(4)]
         turn_back(1)
-        pick_ts(3, "c_w1")
+        sums += [open_sum(2, m) for m in range(4, N_TILES)]
+        q_c(2)
+        pick_ts(3, 1, "ts_col0")
+        il_c(3, nc.vector.tensor_copy)
+        q_c(3)
+        pick_words(3)
         for m in range(N_TILES):
-            direct(3, m)
+            close_sum(2, m, sums[m])
+        for m in range(N_TILES - 1):
+            close_sum(3, m, open_sum(3, m))
+        close_sum(3, N_TILES - 1, open_sum(3, N_TILES - 1), (0, 256, 512))

@@ -199,7 +199,7 @@ def tile_list_tabts_silu_kernel(tc, tab_words, tab_scales, w4_words, w4_scales, 
         load_c(3)
         il_c(1, nc.scalar.copy)
         pick_scales(0, N_CHUNKS)
-        pick_ts(0, 3)
+        pick_ts(0, 4)
         ts_to_partitions(0)
         ts_to_partitions(1)
         quantize(first_w, first_s, first_bf)
@@ -216,7 +216,6 @@ def tile_list_tabts_silu_kernel(tc, tab_words, tab_scales, w4_words, w4_scales, 
         turn_back(1)
         sums += [open_sum(2, m) for m in range(4, N_TILES)]
         q_c(2)
-        pick_ts(3, 1, "ts_col0")
         il_c(3, nc.vector.tensor_copy)
         q_c(3)
         pick_words(3)

@@ -23,204 +23,233 @@ N_CHUNKS = S // CHUNK
 N_TILES = M // P
 BLOCKS = CHUNK // P
 TS_PER_PARTITION = T // P
+VECTOR_TILES = 28
+SCALAR_TILES = 24
 
 
 def tile_list_tabts_silu_kernel(tc, tab_words, tab_scales, w4_words, w4_scales, c, u, ts, b, offs, out):
     nc = tc.nc
     with ExitStack() as ctx:
         keep = ctx.enter_context(tc.tile_pool(name="keep", bufs=1))
-        work = ctx.enter_context(tc.tile_pool(name="work", bufs=1))
-        acc_pool = ctx.enter_context(tc.psum_pool(name="acc", bufs=4))
-        turn_pool = ctx.enter_context(tc.psum_pool(name="turn", bufs=4))
+        banks = ctx.enter_context(tc.psum_pool(name="banks", bufs=8))
 
         def kept(shape, dtype, name, tag=None):
             return keep.tile(shape, dtype, name=name, tag=tag or name, align_bytes=64)
 
+        def by_vector(shape, dtype, name):
+            return keep.tile(shape, dtype, name=name, tag="by_vector", bufs=VECTOR_TILES, align_bytes=64)
+
+        def by_scalar(shape, dtype, name):
+            return keep.tile(shape, dtype, name=name, tag="by_scalar", bufs=SCALAR_TILES, align_bytes=64)
+
+        def bank(name):
+            return banks.tile([P, CHUNK], F32, name=name, tag="bank")
+
         offsets = kept([P, S // 16], U16, "offsets")
         tab_s = kept([P, T // 4], I32, "tab_s")
-        ts_cols = kept([P, TS_PER_PARTITION], F32, "ts_cols", "first_bf")
+        ts_cols = kept([P, TS_PER_PARTITION], F32, "ts_cols")
         ts_all = kept([P, T], F32, "ts_all")
-        b_rows = kept([P, P], F32, "b_rows", "c_bf1")
-        bias = kept([P, N_TILES], F32, "bias")
-        zeros = kept([P, P], F32, "zeros", "rows")
+        b_rows = kept([P, P], F32, "b_rows")
+        ones = kept([P, P], F32, "ones")
+        ramp = kept([P, P], F32, "ramp")
+        lane = kept([P, 32], F32, "lane")
+        quadrant = kept([P, 1], F32, "quadrant")
         ident = kept([P, P], F32, "ident")
-        warm = kept([P, 1], F32, "warm", "table")
-        warm_bias = kept([P, 1], F32, "warm_bias", "w4")
+        warm = kept([P, 1], F32, "warm")
+        w4_w = kept([P, 2 * M // 4], I32, "w4_w")
+        w4_s = kept([P, M // 4], I32, "w4_s")
+        tab_w = kept([P, T], I32, "tab_w")
+        u_raw = kept([P, PACK, M], F32, "u_raw")
+        c_raw = [kept([P, PACK, CHUNK], F32, "c_raw%d" % i) for i in range(N_CHUNKS)]
+        u_bf = kept([P, M, PACK], BF16, "u_bf")
+        c_bf = [kept([P, CHUNK, PACK], BF16, "c_bf%d" % i, "ts_cols" if i == 0 else None) for i in range(N_CHUNKS)]
+        w4_bytes = w4_w[:].bitcast(U8)
+        w4_plane = w4_s[:].bitcast(U8)
+        codes, scales, words, picked_s, picked_t, ts_col, blocks, small, sums = {}, {}, {}, {}, {}, {}, {}, {}, {}
 
-        nc.vector.memset(tab_s[:], 0)
-        nc.vector.memset(b_rows[:], 0.0)
-        nc.gpsimd.memset(zeros[:], 0.0)
-        nc.gpsimd.memset(warm_bias[:], 0.0)
-        nc.gpsimd.affine_select(
-            out=ident[:], in_=zeros[:], compare_op=ALU.not_equal, fill=1.0, base=0, pattern=[[-1, P]], channel_multiplier=1
-        )
-        nc.scalar.activation(warm[:], ident[:, 0:1], ACT.Silu, bias=warm_bias[:])
-
-        nc.sync.dma_start(ts_cols[:], ts[0].rearrange("(p a) -> p a", p=P))
-        nc.sync.dma_start(offsets[:], offs)
-        for r in range(4):
-            nc.sync.dma_start(tab_s[r:P:32, :], tab_scales[0, r:16:4, :].bitcast(I32))
-        rows = kept([P, 3, PACK, CHUNK], F32, "rows")
-        u_raw = rows[:, 2]
-        c_raw = [rows[:, i % 3] for i in range(N_CHUNKS)]
+        def identity():
+            nc.gpsimd.memset(ones[:], 1.0)
+            for q in range(4):
+                nc.gpsimd.memset(quadrant[32 * q : 32 * (q + 1), :], 32.0 * q)
+            nc.vector.tensor_tensor_scan(ramp[:], ones[:], ones[:], 0.0, ALU.mult, ALU.add)
+            nc.vector.transpose(lane[:], ramp[:, 0:32])
+            nc.vector.tensor_scalar(ident[:], ramp[:], lane[:, 0:1], quadrant[:], ALU.subtract, ALU.is_equal)
 
         def load_rows(dst, src):
-            nc.sync.dma_start(dst, src.rearrange("(p i) j -> p i j", i=PACK))
+            nc.sync.dma_start(dst[:], src.rearrange("(p i) j -> p i j", i=PACK))
 
         def load_c(i):
             load_rows(c_raw[i], c[:, i * CHUNK : (i + 1) * CHUNK])
 
-        tab_w = kept([P, T], I32, "tab_w", "table")
+        def load_planes(queue, plane, rows):
+            for r in range(4):
+                queue.dma_start(plane[r:P:32, :], rows[r:16:4, :].bitcast(I32))
 
         def load_words():
             nc.sync.dma_start(tab_w[:], tab_words[0].rearrange("p t i -> p (t i)").bitcast(I32))
 
-        nc.sync.dma_start(b_rows[0:N_TILES, :], b.rearrange("(m p) -> m p", p=P))
-        load_rows(u_raw, u)
-        load_c(0)
-        load_c(1)
-        load_words()
-        w4 = kept([P, 3 * M // 4], I32, "w4")
-        nc.sync.dma_start(w4[:, 0 : 2 * M // 4], w4_words[0].bitcast(I32))
-        nc.gpsimd.memset(w4[:, 2 * M // 4 : 3 * M // 4], 0)
-        for r in range(4):
-            nc.sync.dma_start(w4[r:P:32, 2 * M // 4 : 3 * M // 4], w4_scales[0, r:16:4, :].bitcast(I32))
-        w4_bytes = w4[:, 0 : 2 * M // 4].bitcast(U8)
-        w4_plane = w4[:, 2 * M // 4 : 3 * M // 4].bitcast(U8)
+        def ts_window():
+            for g in range(T // CHUNK):
+                turned = bank("turned")
+                for a in range(BLOCKS):
+                    col = g * BLOCKS + a
+                    nc.tensor.transpose(turned[:, a * P : (a + 1) * P], ts_cols[:, col : col + 1].to_broadcast([P, P]), ident[:])
+                nc.scalar.copy(
+                    ts_all[:].rearrange("q (p a) -> q p a", p=P)[:, :, g * BLOCKS : (g + 1) * BLOCKS],
+                    turned[:].rearrange("q (a p) -> q p a", p=P),
+                )
 
-        for g in range(T // CHUNK):
-            turned = turn_pool.tile([P, CHUNK], F32, name="turned")
-            for a in range(BLOCKS):
-                col = g * BLOCKS + a
-                nc.tensor.transpose(turned[:, a * P : (a + 1) * P], ts_cols[:, col : col + 1].to_broadcast([P, P]), ident[:])
-            nc.scalar.copy(
-                ts_all[:].rearrange("q (p a) -> q p a", p=P)[:, :, g * BLOCKS : (g + 1) * BLOCKS],
-                turned[:].rearrange("q (a p) -> q p a", p=P),
-            )
-        turned = turn_pool.tile([P, CHUNK], F32, name="turned")
-        nc.tensor.transpose(turned[:, 0:P], b_rows[:], ident[:])
-        nc.scalar.copy(bias[:], turned[:, 0:N_TILES])
-
-        planes = kept([P, S], U8, "planes")
-        picked_s = [planes[:, i * CHUNK : (i + 1) * CHUNK] for i in range(N_CHUNKS)]
-        picked_t = {}
-        blocks = [[kept([P, M], F32, "block%d_%d" % (i, a)) for a in range(BLOCKS)] for i in range(2)]
-        first_bf = kept([P, M + CHUNK, PACK], BF16, "first_bf")
-        first_w = kept([P, M + CHUNK], U32, "first_w")
-        first_s = kept([P, M + CHUNK], U8, "first_s")
-        c_bf = [first_bf[:, M : M + CHUNK, :]] + [kept([P, CHUNK, PACK], BF16, "c_bf%d" % i, "c_bf%d" % (1 if i == 2 else i)) for i in range(1, N_CHUNKS)]
-        c_w = [first_w[:, M : M + CHUNK]] + [kept([P, CHUNK], U32, "c_w%d" % i) for i in range(1, N_CHUNKS)]
-        c_s = [first_s[:, M : M + CHUNK]] + [kept([P, CHUNK], U8, "c_s%d" % i) for i in range(1, N_CHUNKS)]
-        u_bf = first_bf[:, 0:M, :]
-        u_w = first_w[:, 0:M]
-        u_s = first_s[:, 0:M]
-        ts_col = [kept([P, BLOCKS], F32, "ts_col%d" % i) for i in range(2)]
-
-        def listed(i, n):
+        def listed(i, n=1):
             return offsets[:, i * (CHUNK // 16) : (i + n) * (CHUNK // 16)]
 
         def pick_scales(i, n):
-            nc.vector.tensor_copy(planes[:, i * CHUNK : (i + n) * CHUNK], tab_s[:].bitcast(U8).indirect(listed(i, n)))
-
-        def pick_words(i, n=1):
-            nc.vector.tensor_copy(word_pair[:, (i % 2) * CHUNK : (i % 2 + n) * CHUNK], tab_w[:].bitcast(U32).indirect(listed(i, n)))
-
-        def pick_ts(i, n, tag=None):
-            picked = kept([P, n * CHUNK], F32, "picked_t%d" % i, tag)
+            plane = by_vector([P, n * CHUNK], U8, "plane%d" % i)
+            nc.vector.tensor_copy(plane[:], tab_s[:].bitcast(U8).indirect(listed(i, n)))
             for k in range(n):
-                picked_t[i + k] = picked[:, k * CHUNK : (k + 1) * CHUNK]
-            nc.vector.tensor_copy(picked[:], ts_all[:].indirect(listed(i, n)))
+                picked_s[i + k] = plane[:, k * CHUNK : (k + 1) * CHUNK]
+            return plane
 
-        def interleave(copy, grouped, raw):
-            copy(grouped.rearrange("p (g e) i -> p g i e", e=4), raw.rearrange("p i (g e) -> p g i e", e=4))
+        def pick_words(i):
+            words[i] = by_vector([P, CHUNK], U32, "words%d" % i)
+            nc.vector.tensor_copy(words[i][:], tab_w[:].bitcast(U32).indirect(listed(i)))
 
-        def on_gpsimd(i, lo=0, hi=CHUNK):
-            nc.gpsimd.tensor_scalar(c_bf[i][:, lo:hi, :], c_raw[i][:, :, lo:hi].rearrange("p i w -> p w i"), 1.0, 0.0, ALU.mult, ALU.add)
+        def pick_ts(i):
+            picked_t[i] = by_vector([P, CHUNK], F32, "picked%d" % i)
+            nc.vector.tensor_copy(picked_t[i][:], ts_all[:].indirect(listed(i)))
 
-        def il_c(i, copy, lo=0, hi=CHUNK):
-            interleave(copy, c_bf[i][:, lo:hi, :], c_raw[i][:, :, lo:hi])
+        def interleave(copy, grouped, raw, lo=0, hi=CHUNK):
+            copy(grouped[:, lo:hi, :].rearrange("p (g e) i -> p g i e", e=4), raw[:, :, lo:hi].rearrange("p i (g e) -> p g i e", e=4))
 
-        def quantize(words, scales, grouped):
-            nc.vector.quantize_mx(out=words[:].bitcast(FP8X4), scales=scales[:], in_=grouped[:].rearrange("p w i -> p (w i)"))
+        def on_gpsimd(grouped, raw, lo=0, hi=CHUNK):
+            nc.gpsimd.tensor_copy(grouped[:, lo:hi, :], raw[:, :, lo:hi].rearrange("p i w -> p w i"))
 
-        def q_c(i):
-            quantize(c_w[i], c_s[i], c_bf[i])
+        def quantize(key, grouped):
+            codes[key] = by_vector([P, CHUNK], U32, "codes_%s" % key)
+            scales[key] = kept([P, CHUNK], U8, "scales_%s" % key)
+            nc.vector.quantize_mx(out=codes[key][:].bitcast(FP8X4), scales=scales[key][:], in_=grouped[:].rearrange("p w i -> p (w i)"))
 
         def finish(i, m, src, lo=0, hi=CHUNK):
-            result = work.tile([P, hi - lo], F32, name="result", bufs=18)
-            nc.scalar.activation(result[:], src, ACT.Silu, bias=bias[:, m : m + 1])
+            result = by_scalar([P, hi - lo], F32, "result")
+            nc.scalar.activation(result[:], src, ACT.Silu, bias=small["bias"][:, m : m + 1])
             nc.sync.dma_start(out[m * P : (m + 1) * P, i * CHUNK + lo : i * CHUNK + hi], result[:])
 
-        def open_sum(i, m):
+        def table_pass(i, m, acc, first):
             cols = slice(m * P, (m + 1) * P)
-            acc = acc_pool.tile([P, CHUNK], F32, name="acc")
             nc.tensor.matmul_mx(out=acc[:], lhsT=w4_bytes[:, 2 * m * P : 2 * (m + 1) * P].bitcast(FP4X4), lhsT_scale=w4_plane[:, cols],
-                                rhs=word_pair[:, (i % 2) * CHUNK : (i % 2 + 1) * CHUNK].bitcast(FP8X4), rhs_scale=picked_s[i], start=True, stop=False)
-            return acc
+                                rhs=words[i][:].bitcast(FP8X4), rhs_scale=picked_s[i], start=first, stop=not first)
 
-        def close_sum(i, m, acc, cuts=(0, CHUNK)):
+        def dense_pass(i, m, acc, first):
             cols = slice(m * P, (m + 1) * P)
-            nc.tensor.matmul_mx(out=acc[:], lhsT=u_w[:, cols].bitcast(FP8X4), lhsT_scale=u_s[:, cols],
-                                rhs=c_w[i][:].bitcast(FP8X4), rhs_scale=c_s[i][:], start=False, stop=True)
-            for lo, hi in zip(cuts, cuts[1:]):
-                scaled = work.tile([P, hi - lo], F32, name="scaled", bufs=10)
-                nc.vector.tensor_tensor(scaled[:], acc[:, lo:hi], picked_t[i][:, lo:hi], ALU.mult)
-                finish(i, m, scaled[:], lo, hi)
+            nc.tensor.matmul_mx(out=acc[:], lhsT=codes["u"][:, cols].bitcast(FP8X4), lhsT_scale=scales["u"][:, cols],
+                                rhs=codes[i][:].bitcast(FP8X4), rhs_scale=scales[i][:], start=first, stop=not first)
+
+        def turned_table_pass(i, a, acc, first):
+            cols = slice(a * P, (a + 1) * P)
+            nc.tensor.matmul_mx(out=acc[:], lhsT=words[i][:, cols].bitcast(FP8X4), lhsT_scale=picked_s[i][:, cols],
+                                rhs=w4_bytes.bitcast(FP4X4), rhs_scale=w4_plane, start=first, stop=not first)
+
+        def turned_dense_pass(i, a, acc, first):
+            cols = slice(a * P, (a + 1) * P)
+            nc.tensor.matmul_mx(out=acc[:], lhsT=codes[i][:, cols].bitcast(FP8X4), lhsT_scale=scales[i][:, cols],
+                                rhs=codes["u"][:].bitcast(FP8X4), rhs_scale=scales["u"][:], start=first, stop=not first)
+
+        def open_sums(one_pass, i, tiles=range(N_TILES)):
+            for m in tiles:
+                sums[i, m] = bank("acc")
+                one_pass(i, m, sums[i, m], True)
+
+        def close_sums(one_pass, i, tiles=range(N_TILES)):
+            for m in tiles:
+                one_pass(i, m, sums[i, m], False)
+
+        def scale_direct(i, m, acc, lo=0, hi=CHUNK):
+            scaled = by_vector([P, hi - lo], F32, "scaled")
+            nc.vector.tensor_tensor(scaled[:], acc[:, lo:hi], picked_t[i][:, lo:hi], ALU.mult)
+            return scaled
 
         def ts_to_partitions(i):
-            turned = turn_pool.tile([P, CHUNK], F32, name="turned")
+            turned = bank("turned")
             for a in range(BLOCKS):
                 nc.tensor.transpose(turned[:, a * P : (a + 1) * P], picked_t[i][:, a * P : (a + 1) * P], ident[:])
+            ts_col[i] = by_scalar([P, BLOCKS], F32, "ts_col%d" % i)
             nc.scalar.copy(ts_col[i][:], turned[:, 0:CHUNK:P])
 
-        def turned_sums(i, on_vector=0):
-            for a in range(BLOCKS):
-                cols = slice(a * P, (a + 1) * P)
-                acc = acc_pool.tile([P, M], F32, name="acc")
-                nc.tensor.matmul_mx(out=acc[:], lhsT=c_w[i][:, cols].bitcast(FP8X4), lhsT_scale=c_s[i][:, cols],
-                                    rhs=u_w[:].bitcast(FP8X4), rhs_scale=u_s[:], start=True, stop=False)
-                nc.tensor.matmul_mx(out=acc[:], lhsT=word_pair[:, (i % 2) * CHUNK + a * P : (i % 2) * CHUNK + (a + 1) * P].bitcast(FP8X4), lhsT_scale=picked_s[i][:, cols],
-                                    rhs=w4_bytes.bitcast(FP4X4), rhs_scale=w4_plane, start=False, stop=True)
-                if a >= BLOCKS - on_vector:
-                    nc.vector.tensor_scalar(blocks[i][a][:], acc[:], ts_col[i][:, a : a + 1], None, ALU.mult)
-                else:
-                    nc.scalar.activation(blocks[i][a][:], acc[:], ACT.Copy, scale=ts_col[i][:, a : a + 1])
+        def turn_bias():
+            turned = bank("turned")
+            nc.tensor.transpose(turned[:, 0:P], b_rows[:], ident[:])
+            small["bias"] = by_scalar([P, N_TILES], F32, "bias")
+            nc.scalar.copy(small["bias"][:], turned[:, 0:N_TILES])
 
-        def turn_back(i):
-            for m in range(N_TILES):
-                turned = turn_pool.tile([P, CHUNK], F32, name="turned")
-                for a in range(BLOCKS):
-                    nc.tensor.transpose(turned[:, a * P : (a + 1) * P], blocks[i][a][:, m * P : (m + 1) * P], ident[:])
-                finish(i, m, turned[:])
+        def scale_turned(i, a, acc):
+            blocks[i, a] = by_scalar([P, M], F32, "block%d_%d" % (i, a))
+            nc.scalar.activation(blocks[i, a][:], acc[:], ACT.Copy, scale=ts_col[i][:, a : a + 1])
 
-        interleave(nc.scalar.copy, u_bf[:], u_raw)
+        def scale_turned_on_vector(i, a, acc):
+            blocks[i, a] = by_vector([P, M], F32, "block%d_%d" % (i, a))
+            nc.vector.tensor_scalar(blocks[i, a][:], acc[:], ts_col[i][:, a : a + 1], None, ALU.mult)
+
+        def turn_back(i, m):
+            turned = bank("turned")
+            for a in reversed(range(BLOCKS)):
+                nc.tensor.transpose(turned[:, a * P : (a + 1) * P], blocks[i, a][:, m * P : (m + 1) * P], ident[:])
+            return turned
+
+        nc.vector.memset(tab_s[:], 0)
+        identity()
+        nc.gpsimd.memset(w4_s[:], 0)
+        nc.gpsimd.memset(b_rows[:], 0.0)
+        nc.scalar.activation(warm[:], ones[:, 0:1], ACT.Silu, bias=ones[:, 1:2])
+        nc.sync.dma_start(offsets[:], offs)
+        nc.sync.dma_start(ts_cols[:], ts[0].rearrange("(p a) -> p a", p=P))
+        nc.sync.dma_start(w4_w[:], w4_words[0].bitcast(I32))
+        load_planes(nc.sync, tab_s, tab_scales[0])
+        load_rows(u_raw, u)
+        load_c(0)
+        load_words()
+        load_planes(nc.sync, w4_s, w4_scales[0])
+        nc.sync.dma_start(b_rows[0:N_TILES, :], b.rearrange("(m p) -> m p", p=P))
+        load_c(1)
         load_c(2)
-        il_c(0, nc.scalar.copy)
         load_c(3)
-        il_c(1, nc.scalar.copy)
-        pick_scales(0, N_CHUNKS)
-        pick_ts(0, 4)
+        ts_window()
+        on_gpsimd(u_bf, u_raw)
+        interleave(nc.scalar.copy, c_bf[0], c_raw[0])
+        pick_scales(0, 4)
+        pick_ts(0)
+        pick_ts(1)
+        quantize("u", u_bf)
+        quantize(0, c_bf[0])
+        open_sums(turned_dense_pass, 0)
         ts_to_partitions(0)
-        ts_to_partitions(1)
-        quantize(first_w, first_s, first_bf)
-        word_pair = kept([P, 2 * CHUNK], U32, "word_pair", "first_bf")
+        pick_ts(2)
         pick_words(0)
-        turned_sums(0)
-        q_c(1)
+        close_sums(turned_table_pass, 0)
+        for a in range(BLOCKS):
+            scale_turned(0, a, sums[0, a])
+        turn_bias()
         pick_words(1)
-        turned_sums(1)
-        turn_back(0)
-        il_c(2, nc.vector.tensor_copy)
-        pick_words(2)
-        sums = [open_sum(2, m) for m in range(4)]
-        turn_back(1)
-        sums += [open_sum(2, m) for m in range(4, N_TILES)]
-        q_c(2)
-        il_c(3, nc.vector.tensor_copy)
-        q_c(3)
-        pick_words(3)
+        open_sums(table_pass, 1, range(2))
+        interleave(nc.vector.tensor_copy, c_bf[1], c_raw[1])
+        pick_ts(3)
+        quantize(1, c_bf[1])
+        on_gpsimd(c_bf[2], c_raw[2])
         for m in range(N_TILES):
-            close_sum(2, m, sums[m])
-        for m in range(N_TILES - 1):
-            close_sum(3, m, open_sum(3, m))
-        close_sum(3, N_TILES - 1, open_sum(3, N_TILES - 1), (0, 256, 512))
+            finish(0, m, turn_back(0, m)[:])
+        open_sums(table_pass, 1, range(2, 4))
+        close_sums(dense_pass, 1)
+        pick_words(2)
+        open_sums(table_pass, 2)
+        for m in range(N_TILES):
+            finish(1, m, scale_direct(1, m, sums[1, m])[:])
+        interleave(nc.scalar.copy, c_bf[3], c_raw[3])
+        quantize(2, c_bf[2])
+        close_sums(dense_pass, 2)
+        pick_words(3)
+        open_sums(table_pass, 3)
+        for m in range(N_TILES):
+            finish(2, m, scale_direct(2, m, sums[2, m])[:])
+        quantize(3, c_bf[3])
+        close_sums(dense_pass, 3)
+        for m in range(N_TILES):
+            for lo, hi in ((0, CHUNK),) if m < N_TILES - 1 else ((0, 256), (256, 512)):
+                finish(3, m, scale_direct(3, m, sums[3, m], lo, hi)[:], lo, hi)

@@ -121,7 +121,7 @@ def tile_list_tabts_silu_kernel(tc, tab_words, tab_scales, w4_words, w4_scales, 
             copy(grouped[:, lo:hi, :].rearrange("p (g e) i -> p g i e", e=4), raw[:, :, lo:hi].rearrange("p i (g e) -> p g i e", e=4))
 
         def on_gpsimd(grouped, raw, lo=0, hi=CHUNK):
-            nc.gpsimd.tensor_copy(grouped[:, lo:hi, :], raw[:, :, lo:hi].rearrange("p i w -> p w i"))
+            nc.gpsimd.tensor_scalar(grouped[:, lo:hi, :], raw[:, :, lo:hi].rearrange("p i w -> p w i"), 1.0, 0.0, ALU.mult, ALU.add)
 
         def quantize(key, grouped):
             codes[key] = by_vector([P, CHUNK], U32, "codes_%s" % key)

@@ -62,7 +62,7 @@ def tile_list_tabts_silu_kernel(tc, tab_words, tab_scales, w4_words, w4_scales, 
         u_raw = kept([P, PACK, M], F32, "u_raw")
         c_raw = [kept([P, PACK, CHUNK], F32, "c_raw%d" % i) for i in range(N_CHUNKS)]
         u_bf = kept([P, M, PACK], BF16, "u_bf")
-        c_bf = [kept([P, CHUNK, PACK], BF16, "c_bf%d" % i, "ts_cols" if i == 0 else None) for i in range(N_CHUNKS)]
+        c_bf = [kept([P, CHUNK, PACK], BF16, "c_bf%d" % i, ("ts_cols", "c_bf1", "c_bf1", None)[i]) for i in range(N_CHUNKS)]
         w4_bytes = w4_w[:].bitcast(U8)
         w4_plane = w4_s[:].bitcast(U8)
         codes, scales, words, picked_s, picked_t, ts_col, blocks, small, sums = {}, {}, {}, {}, {}, {}, {}, {}, {}

@@ -22,9 +22,12 @@ CHUNK = 512
 N_CHUNKS = S // CHUNK
 N_TILES = M // P
 BLOCKS = CHUNK // P
+HALF = CHUNK // 2
 TS_PER_PARTITION = T // P
 VECTOR_TILES = 28
-SCALAR_TILES = 24
+SCALAR_TILES = 28
+VECTOR_WIDE_TILES = 1
+SCALAR_WIDE_TILES = 1
 
 
 def tile_list_tabts_silu_kernel(tc, tab_words, tab_scales, w4_words, w4_scales, c, u, ts, b, offs, out):
@@ -36,11 +39,13 @@ def tile_list_tabts_silu_kernel(tc, tab_words, tab_scales, w4_words, w4_scales, 
         def kept(shape, dtype, name, tag=None):
             return keep.tile(shape, dtype, name=name, tag=tag or name, align_bytes=64)
 
-        def by_vector(shape, dtype, name):
-            return keep.tile(shape, dtype, name=name, tag="by_vector", bufs=VECTOR_TILES, align_bytes=64)
+        def by_vector(shape, dtype, name, wide=False):
+            tag, bufs = ("by_vector_wide", VECTOR_WIDE_TILES) if wide else ("by_vector", VECTOR_TILES)
+            return keep.tile(shape, dtype, name=name, tag=tag, bufs=bufs, align_bytes=64)
 
-        def by_scalar(shape, dtype, name):
-            return keep.tile(shape, dtype, name=name, tag="by_scalar", bufs=SCALAR_TILES, align_bytes=64)
+        def by_scalar(shape, dtype, name, wide=False):
+            tag, bufs = ("by_scalar_wide", SCALAR_WIDE_TILES) if wide else ("by_scalar", SCALAR_TILES)
+            return keep.tile(shape, dtype, name=name, tag=tag, bufs=bufs, align_bytes=64)
 
         def bank(name):
             return banks.tile([P, CHUNK], F32, name=name, tag="bank")
@@ -58,14 +63,13 @@ def tile_list_tabts_silu_kernel(tc, tab_words, tab_scales, w4_words, w4_scales, 
         warm = kept([P, 1], F32, "warm")
         w4_w = kept([P, 2 * M // 4], I32, "w4_w")
         w4_s = kept([P, M // 4], I32, "w4_s")
+        planes = kept([P, S // 4], I32, "planes")
         tab_w = kept([P, T], I32, "tab_w")
         u_raw = kept([P, PACK, M], F32, "u_raw")
         c_raw = [kept([P, PACK, CHUNK], F32, "c_raw%d" % i) for i in range(N_CHUNKS)]
-        u_bf = kept([P, M, PACK], BF16, "u_bf")
-        c_bf = [kept([P, CHUNK, PACK], BF16, "c_bf%d" % i, ("ts_cols", "c_bf1", "c_bf1", None)[i]) for i in range(N_CHUNKS)]
         w4_bytes = w4_w[:].bitcast(U8)
         w4_plane = w4_s[:].bitcast(U8)
-        codes, scales, words, picked_s, picked_t, ts_col, blocks, small, sums = {}, {}, {}, {}, {}, {}, {}, {}, {}
+        codes, scales, words, picked_s, picked_t, ts_col, blocks, small, sums, rounded = {}, {}, {}, {}, {}, {}, {}, {}, {}, {}
 
         def identity():
             nc.gpsimd.memset(ones[:], 1.0)
@@ -103,35 +107,60 @@ def tile_list_tabts_silu_kernel(tc, tab_words, tab_scales, w4_words, w4_scales, 
             return offsets[:, i * (CHUNK // 16) : (i + n) * (CHUNK // 16)]
 
         def pick_scales(i, n):
-            plane = by_vector([P, n * CHUNK], U8, "plane%d" % i)
-            nc.vector.tensor_copy(plane[:], tab_s[:].bitcast(U8).indirect(listed(i, n)))
-            for k in range(n):
-                picked_s[i + k] = plane[:, k * CHUNK : (k + 1) * CHUNK]
-            return plane
+            rows = by_vector([P, n * CHUNK], U8, "picked_rows%d" % i)
+            nc.vector.tensor_copy(rows[:], tab_s[:].bitcast(U8).indirect(listed(i, n)))
+            for r in range(4):
+                nc.sync.dma_start(planes[r:P:32, i * CHUNK // 4 : (i + n) * CHUNK // 4], rows[8 * r : P : 32, :].bitcast(I32))
+            for k in range(i, i + n):
+                picked_s[k] = planes[:].bitcast(U8)[:, k * CHUNK : (k + 1) * CHUNK]
 
-        def pick_words(i):
-            words[i] = by_vector([P, CHUNK], U32, "words%d" % i)
+        def pick_words(i, wide=False):
+            words[i] = by_vector([P, CHUNK], U32, "words%d" % i, wide)
             nc.vector.tensor_copy(words[i][:], tab_w[:].bitcast(U32).indirect(listed(i)))
 
-        def pick_ts(i):
-            picked_t[i] = by_vector([P, CHUNK], F32, "picked%d" % i)
+        def pick_ts(i, wide=False):
+            picked_t[i] = by_vector([P, CHUNK], F32, "picked%d" % i, wide)
             nc.vector.tensor_copy(picked_t[i][:], ts_all[:].indirect(listed(i)))
 
-        def interleave(copy, grouped, raw, lo=0, hi=CHUNK):
-            copy(grouped[:, lo:hi, :].rearrange("p (g e) i -> p g i e", e=4), raw[:, :, lo:hi].rearrange("p i (g e) -> p g i e", e=4))
+        def raw_rows(key):
+            return u_raw if key == "u" else c_raw[key]
 
-        def on_gpsimd(grouped, raw, lo=0, hi=CHUNK):
-            nc.gpsimd.tensor_scalar(grouped[:, lo:hi, :], raw[:, :, lo:hi].rearrange("p i w -> p w i"), 1.0, 0.0, ALU.mult, ALU.add)
+        def round_on_gpsimd(key, lo=0, hi=CHUNK, tag=None):
+            part = kept([P, hi - lo, PACK], BF16, "rounded_%s_%d" % (key, lo), tag)
+            nc.gpsimd.tensor_scalar(part[:], raw_rows(key)[:, :, lo:hi].rearrange("p i w -> p w i"), 1.0, 0.0, ALU.mult, ALU.add)
+            rounded.setdefault(key, []).append((lo, hi, part))
 
-        def quantize(key, grouped):
+        def round_half(make, copy, key, h):
+            lo, hi = h * HALF, (h + 1) * HALF
+            part = make([P, HALF, PACK], BF16, "rounded_%s_%d" % (key, lo))
+            copy(part[:].rearrange("p (g e) i -> p g i e", e=4), raw_rows(key)[:, :, lo:hi].rearrange("p i (g e) -> p g i e", e=4))
+            rounded.setdefault(key, []).append((lo, hi, part))
+
+        def round_on_vector(key, halves=(0, 1), tag=None):
+            for h in halves:
+                make = by_vector if tag is None or h != halves[-1] else (lambda shape, dtype, name: kept(shape, dtype, name, tag))
+                round_half(make, nc.vector.tensor_copy, key, h)
+
+        def round_on_scalar(key, halves=(0, 1)):
+            for h in halves:
+                round_half(by_scalar, nc.scalar.copy, key, h)
+
+        def quantize(key, tag=None):
             codes[key] = by_vector([P, CHUNK], U32, "codes_%s" % key)
-            scales[key] = kept([P, CHUNK], U8, "scales_%s" % key)
-            nc.vector.quantize_mx(out=codes[key][:].bitcast(FP8X4), scales=scales[key][:], in_=grouped[:].rearrange("p w i -> p (w i)"))
+            scales[key] = kept([P, CHUNK], U8, "scales_%s" % key, tag)
+            for lo, hi, part in rounded[key]:
+                nc.vector.quantize_mx(out=codes[key][:, lo:hi].bitcast(FP8X4), scales=scales[key][:, lo:hi], in_=part[:].rearrange("p w i -> p (w i)"))
 
         def finish(i, m, src, lo=0, hi=CHUNK):
             result = by_scalar([P, hi - lo], F32, "result")
             nc.scalar.activation(result[:], src, ACT.Silu, bias=small["bias"][:, m : m + 1])
             nc.sync.dma_start(out[m * P : (m + 1) * P, i * CHUNK + lo : i * CHUNK + hi], result[:])
+
+        def finish_pair(i, m, left, right):
+            result = by_scalar([P, 2 * CHUNK], F32, "pair", True)
+            for k, src in enumerate((left, right)):
+                nc.scalar.activation(result[:, k * CHUNK : (k + 1) * CHUNK], src, ACT.Silu, bias=small["bias"][:, m : m + 1])
+            nc.sync.dma_start(out[m * P : (m + 1) * P, i * CHUNK : (i + 2) * CHUNK], result[:])
 
         def table_pass(i, m, acc, first):
             cols = slice(m * P, (m + 1) * P)
@@ -198,58 +227,63 @@ def tile_list_tabts_silu_kernel(tc, tab_words, tab_scales, w4_words, w4_scales, 
         identity()
         nc.gpsimd.memset(w4_s[:], 0)
         nc.gpsimd.memset(b_rows[:], 0.0)
+        load_planes(nc.gpsimd, w4_s, w4_scales[0])
+        nc.gpsimd.dma_start(b_rows[0:N_TILES, :], b.rearrange("(m p) -> m p", p=P))
+        nc.vector.memset(planes[:], 0)
         nc.scalar.activation(warm[:], ones[:, 0:1], ACT.Silu, bias=ones[:, 1:2])
         nc.sync.dma_start(offsets[:], offs)
         nc.sync.dma_start(ts_cols[:], ts[0].rearrange("(p a) -> p a", p=P))
         nc.sync.dma_start(w4_w[:], w4_words[0].bitcast(I32))
-        load_planes(nc.sync, tab_s, tab_scales[0])
+        nc.sync.dma_start(tab_s[0:P:8, :], tab_scales[0].bitcast(I32))
         load_rows(u_raw, u)
         load_c(0)
         load_words()
-        load_planes(nc.sync, w4_s, w4_scales[0])
-        nc.sync.dma_start(b_rows[0:N_TILES, :], b.rearrange("(m p) -> m p", p=P))
+        ts_window()
+        round_on_gpsimd("u")
+        pick_scales(0, 4)
         load_c(1)
         load_c(2)
         load_c(3)
-        ts_window()
-        on_gpsimd(u_bf, u_raw)
-        interleave(nc.scalar.copy, c_bf[0], c_raw[0])
-        pick_scales(0, 4)
         pick_ts(0)
         pick_ts(1)
-        quantize("u", u_bf)
-        quantize(0, c_bf[0])
-        open_sums(turned_dense_pass, 0)
+        round_on_scalar(0)
         ts_to_partitions(0)
-        pick_ts(2)
+        turn_bias()
+        quantize("u")
+        quantize(0)
+        open_sums(turned_dense_pass, 0, range(2))
         pick_words(0)
-        close_sums(turned_table_pass, 0)
+        close_sums(turned_table_pass, 0, range(2))
+        for a in range(2, BLOCKS):
+            open_sums(turned_table_pass, 0, [a])
+            close_sums(turned_dense_pass, 0, [a])
         for a in range(BLOCKS):
             scale_turned(0, a, sums[0, a])
-        turn_bias()
         pick_words(1)
-        open_sums(table_pass, 1, range(2))
-        interleave(nc.vector.tensor_copy, c_bf[1], c_raw[1])
+        open_sums(table_pass, 1)
+        pick_ts(2)
+        round_on_vector(1, tag="handed")
         pick_ts(3)
-        quantize(1, c_bf[1])
-        on_gpsimd(c_bf[2], c_raw[2])
+        quantize(1)
+        round_on_gpsimd(2, tag="handed")
         for m in range(N_TILES):
             finish(0, m, turn_back(0, m)[:])
-        open_sums(table_pass, 1, range(2, 4))
         close_sums(dense_pass, 1)
         pick_words(2)
         open_sums(table_pass, 2)
-        for m in range(N_TILES):
+        for m in range(2):
             finish(1, m, scale_direct(1, m, sums[1, m])[:])
-        interleave(nc.scalar.copy, c_bf[3], c_raw[3])
-        quantize(2, c_bf[2])
-        close_sums(dense_pass, 2)
+        round_on_scalar(3)
+        for m in range(2, N_TILES):
+            finish(1, m, scale_direct(1, m, sums[1, m])[:])
         pick_words(3)
+        quantize(2)
+        close_sums(dense_pass, 2)
         open_sums(table_pass, 3)
+        quantize(3)
+        close_sums(dense_pass, 3)
         for m in range(N_TILES):
             finish(2, m, scale_direct(2, m, sums[2, m])[:])
-        quantize(3, c_bf[3])
-        close_sums(dense_pass, 3)
         for m in range(N_TILES):
             for lo, hi in ((0, CHUNK),) if m < N_TILES - 1 else ((0, 256), (256, 512)):
                 finish(3, m, scale_direct(3, m, sums[3, m], lo, hi)[:], lo, hi)

@@ -227,8 +227,8 @@ def tile_list_tabts_silu_kernel(tc, tab_words, tab_scales, w4_words, w4_scales, 
         identity()
         nc.gpsimd.memset(w4_s[:], 0)
         nc.gpsimd.memset(b_rows[:], 0.0)
-        load_planes(nc.gpsimd, w4_s, w4_scales[0])
-        nc.gpsimd.dma_start(b_rows[0:N_TILES, :], b.rearrange("(m p) -> m p", p=P))
+        load_planes(nc.scalar, w4_s, w4_scales[0])
+        nc.scalar.dma_start(b_rows[0:N_TILES, :], b.rearrange("(m p) -> m p", p=P))
         nc.vector.memset(planes[:], 0)
         nc.scalar.activation(warm[:], ones[:, 0:1], ACT.Silu, bias=ones[:, 1:2])
         nc.sync.dma_start(offsets[:], offs)

@@ -263,7 +263,6 @@ def tile_list_tabts_silu_kernel(tc, tab_words, tab_scales, w4_words, w4_scales, 
         open_sums(table_pass, 1)
         pick_ts(2)
         round_on_vector(1, tag="handed")
-        pick_ts(3)
         quantize(1)
         round_on_gpsimd(2, tag="handed")
         for m in range(N_TILES):
@@ -276,9 +275,10 @@ def tile_list_tabts_silu_kernel(tc, tab_words, tab_scales, w4_words, w4_scales, 
         round_on_scalar(3)
         for m in range(2, N_TILES):
             finish(1, m, scale_direct(1, m, sums[1, m])[:])
-        pick_words(3)
+        pick_ts(3)
         quantize(2)
         close_sums(dense_pass, 2)
+        pick_words(3)
         open_sums(table_pass, 3)
         quantize(3)
         close_sums(dense_pass, 3)

@@ -63,7 +63,6 @@ def tile_list_tabts_silu_kernel(tc, tab_words, tab_scales, w4_words, w4_scales, 
         warm = kept([P, 1], F32, "warm")
         w4_w = kept([P, 2 * M // 4], I32, "w4_w")
         w4_s = kept([P, M // 4], I32, "w4_s")
-        planes = kept([P, S // 4], I32, "planes")
         tab_w = kept([P, T], I32, "tab_w")
         u_raw = kept([P, PACK, M], F32, "u_raw")
         c_raw = [kept([P, PACK, CHUNK], F32, "c_raw%d" % i) for i in range(N_CHUNKS)]
@@ -107,12 +106,10 @@ def tile_list_tabts_silu_kernel(tc, tab_words, tab_scales, w4_words, w4_scales, 
             return offsets[:, i * (CHUNK // 16) : (i + n) * (CHUNK // 16)]
 
         def pick_scales(i, n):
-            rows = by_vector([P, n * CHUNK], U8, "picked_rows%d" % i)
-            nc.vector.tensor_copy(rows[:], tab_s[:].bitcast(U8).indirect(listed(i, n)))
-            for r in range(4):
-                nc.sync.dma_start(planes[r:P:32, i * CHUNK // 4 : (i + n) * CHUNK // 4], rows[8 * r : P : 32, :].bitcast(I32))
-            for k in range(i, i + n):
-                picked_s[k] = planes[:].bitcast(U8)[:, k * CHUNK : (k + 1) * CHUNK]
+            plane = by_vector([P, n * CHUNK], U8, "plane%d" % i)
+            nc.vector.tensor_copy(plane[:], tab_s[:].bitcast(U8).indirect(listed(i, n)))
+            for k in range(n):
+                picked_s[i + k] = plane[:, k * CHUNK : (k + 1) * CHUNK]
 
         def pick_words(i, wide=False):
             words[i] = by_vector([P, CHUNK], U32, "words%d" % i, wide)
@@ -227,17 +224,16 @@ def tile_list_tabts_silu_kernel(tc, tab_words, tab_scales, w4_words, w4_scales, 
         identity()
         nc.gpsimd.memset(w4_s[:], 0)
         nc.gpsimd.memset(b_rows[:], 0.0)
-        load_planes(nc.scalar, w4_s, w4_scales[0])
-        nc.scalar.dma_start(b_rows[0:N_TILES, :], b.rearrange("(m p) -> m p", p=P))
-        nc.vector.memset(planes[:], 0)
         nc.scalar.activation(warm[:], ones[:, 0:1], ACT.Silu, bias=ones[:, 1:2])
         nc.sync.dma_start(offsets[:], offs)
         nc.sync.dma_start(ts_cols[:], ts[0].rearrange("(p a) -> p a", p=P))
         nc.sync.dma_start(w4_w[:], w4_words[0].bitcast(I32))
-        nc.sync.dma_start(tab_s[0:P:8, :], tab_scales[0].bitcast(I32))
+        load_planes(nc.sync, tab_s, tab_scales[0])
         load_rows(u_raw, u)
         load_c(0)
         load_words()
+        load_planes(nc.sync, w4_s, w4_scales[0])
+        nc.sync.dma_start(b_rows[0:N_TILES, :], b.rearrange("(m p) -> m p", p=P))
         ts_window()
         round_on_gpsimd("u")
         pick_scales(0, 4)
@@ -248,7 +244,6 @@ def tile_list_tabts_silu_kernel(tc, tab_words, tab_scales, w4_words, w4_scales, 
         pick_ts(1)
         round_on_scalar(0)
         ts_to_partitions(0)
-        turn_bias()
         quantize("u")
         quantize(0)
         open_sums(turned_dense_pass, 0, range(2))
@@ -259,6 +254,7 @@ def tile_list_tabts_silu_kernel(tc, tab_words, tab_scales, w4_words, w4_scales, 
             close_sums(turned_dense_pass, 0, [a])
         for a in range(BLOCKS):
             scale_turned(0, a, sums[0, a])
+        turn_bias()
         pick_words(1)
         open_sums(table_pass, 1)
         pick_ts(2)

@@ -24,9 +24,9 @@ N_TILES = M // P
 BLOCKS = CHUNK // P
 HALF = CHUNK // 2
 TS_PER_PARTITION = T // P
-VECTOR_TILES = 28
-SCALAR_TILES = 28
-VECTOR_WIDE_TILES = 1
+VECTOR_TILES = 24
+SCALAR_TILES = 24
+VECTOR_WIDE_TILES = 3
 SCALAR_WIDE_TILES = 1
 
 
@@ -106,7 +106,7 @@ def tile_list_tabts_silu_kernel(tc, tab_words, tab_scales, w4_words, w4_scales, 
             return offsets[:, i * (CHUNK // 16) : (i + n) * (CHUNK // 16)]
 
         def pick_scales(i, n):
-            plane = by_vector([P, n * CHUNK], U8, "plane%d" % i)
+            plane = by_vector([P, n * CHUNK], U8, "plane%d" % i, True)
             nc.vector.tensor_copy(plane[:], tab_s[:].bitcast(U8).indirect(listed(i, n)))
             for k in range(n):
                 picked_s[i + k] = plane[:, k * CHUNK : (k + 1) * CHUNK]
@@ -115,41 +115,35 @@ def tile_list_tabts_silu_kernel(tc, tab_words, tab_scales, w4_words, w4_scales, 
             words[i] = by_vector([P, CHUNK], U32, "words%d" % i, wide)
             nc.vector.tensor_copy(words[i][:], tab_w[:].bitcast(U32).indirect(listed(i)))
 
-        def pick_ts(i, wide=False):
-            picked_t[i] = by_vector([P, CHUNK], F32, "picked%d" % i, wide)
-            nc.vector.tensor_copy(picked_t[i][:], ts_all[:].indirect(listed(i)))
+        def pick_ts(i, n=1):
+            picked = by_vector([P, n * CHUNK], F32, "picked%d" % i, n > 1)
+            nc.vector.tensor_copy(picked[:], ts_all[:].indirect(listed(i, n)))
+            for k in range(n):
+                picked_t[i + k] = picked[:, k * CHUNK : (k + 1) * CHUNK]
 
-        def raw_rows(key):
-            return u_raw if key == "u" else c_raw[key]
+        def round_on_gpsimd(dst, raw):
+            nc.gpsimd.tensor_scalar(dst, raw.rearrange("p i w -> p w i"), 1.0, 0.0, ALU.mult, ALU.add)
 
-        def round_on_gpsimd(key, lo=0, hi=CHUNK, tag=None):
-            part = kept([P, hi - lo, PACK], BF16, "rounded_%s_%d" % (key, lo), tag)
-            nc.gpsimd.tensor_scalar(part[:], raw_rows(key)[:, :, lo:hi].rearrange("p i w -> p w i"), 1.0, 0.0, ALU.mult, ALU.add)
-            rounded.setdefault(key, []).append((lo, hi, part))
+        def round_rows(copy, dst, raw):
+            copy(dst.rearrange("p (g e) i -> p g i e", e=4), raw.rearrange("p i (g e) -> p g i e", e=4))
 
-        def round_half(make, copy, key, h):
-            lo, hi = h * HALF, (h + 1) * HALF
-            part = make([P, HALF, PACK], BF16, "rounded_%s_%d" % (key, lo))
-            copy(part[:].rearrange("p (g e) i -> p g i e", e=4), raw_rows(key)[:, :, lo:hi].rearrange("p i (g e) -> p g i e", e=4))
-            rounded.setdefault(key, []).append((lo, hi, part))
+        def quantize_part(key, rounded, lo, hi):
+            if lo == 0:
+                codes[key] = by_vector([P, CHUNK], U32, "codes_%s" % key)
+                scales[key] = kept([P, CHUNK], U8, "scales_%s" % key)
+            nc.vector.quantize_mx(out=codes[key][:, lo:hi].bitcast(FP8X4), scales=scales[key][:, lo:hi], in_=rounded[:].rearrange("p w i -> p (w i)"))
 
-        def round_on_vector(key, halves=(0, 1), tag=None):
-            for h in halves:
-                make = by_vector if tag is None or h != halves[-1] else (lambda shape, dtype, name: kept(shape, dtype, name, tag))
-                round_half(make, nc.vector.tensor_copy, key, h)
+        def quantize(keys, rounded):
+            width = CHUNK * len(keys)
+            made = by_vector([P, width], U32, "codes_%s" % keys[0], len(keys) > 1)
+            plane = kept([P, width], U8, "scales_%s" % keys[0])
+            nc.vector.quantize_mx(out=made[:].bitcast(FP8X4), scales=plane[:], in_=rounded[:].rearrange("p w i -> p (w i)"))
+            for k, key in enumerate(keys):
+                codes[key] = made[:, k * CHUNK : (k + 1) * CHUNK]
+                scales[key] = plane[:, k * CHUNK : (k + 1) * CHUNK]
 
-        def round_on_scalar(key, halves=(0, 1)):
-            for h in halves:
-                round_half(by_scalar, nc.scalar.copy, key, h)
-
-        def quantize(key, tag=None):
-            codes[key] = by_vector([P, CHUNK], U32, "codes_%s" % key)
-            scales[key] = kept([P, CHUNK], U8, "scales_%s" % key, tag)
-            for lo, hi, part in rounded[key]:
-                nc.vector.quantize_mx(out=codes[key][:, lo:hi].bitcast(FP8X4), scales=scales[key][:, lo:hi], in_=part[:].rearrange("p w i -> p (w i)"))
-
-        def finish(i, m, src, lo=0, hi=CHUNK):
-            result = by_scalar([P, hi - lo], F32, "result")
+        def finish(i, m, src, lo=0, hi=CHUNK, wide=False):
+            result = by_scalar([P, hi - lo], F32, "result", wide)
             nc.scalar.activation(result[:], src, ACT.Silu, bias=small["bias"][:, m : m + 1])
             nc.sync.dma_start(out[m * P : (m + 1) * P, i * CHUNK + lo : i * CHUNK + hi], result[:])
 
@@ -197,7 +191,7 @@ def tile_list_tabts_silu_kernel(tc, tab_words, tab_scales, w4_words, w4_scales, 
             turned = bank("turned")
             for a in range(BLOCKS):
                 nc.tensor.transpose(turned[:, a * P : (a + 1) * P], picked_t[i][:, a * P : (a + 1) * P], ident[:])
-            ts_col[i] = by_scalar([P, BLOCKS], F32, "ts_col%d" % i)
+            ts_col[i] = kept([P, BLOCKS], F32, "ts_col%d" % i, "c_raw0")
             nc.scalar.copy(ts_col[i][:], turned[:, 0:CHUNK:P])
 
         def turn_bias():
@@ -235,17 +229,16 @@ def tile_list_tabts_silu_kernel(tc, tab_words, tab_scales, w4_words, w4_scales, 
         load_planes(nc.sync, w4_s, w4_scales[0])
         nc.sync.dma_start(b_rows[0:N_TILES, :], b.rearrange("(m p) -> m p", p=P))
         ts_window()
-        round_on_gpsimd("u")
+        first = kept([P, M + CHUNK, PACK], BF16, "first")
+        round_on_gpsimd(first[:, 0:M, :], u_raw[:])
         pick_scales(0, 4)
         load_c(1)
         load_c(2)
         load_c(3)
-        pick_ts(0)
-        pick_ts(1)
-        round_on_scalar(0)
+        pick_ts(0, 3)
+        round_rows(nc.scalar.copy, first[:, M : M + CHUNK, :], c_raw[0][:])
         ts_to_partitions(0)
-        quantize("u")
-        quantize(0)
+        quantize(("u", 0), first)
         open_sums(turned_dense_pass, 0, range(2))
         pick_words(0)
         close_sums(turned_table_pass, 0, range(2))
@@ -257,28 +250,33 @@ def tile_list_tabts_silu_kernel(tc, tab_words, tab_scales, w4_words, w4_scales, 
         turn_bias()
         pick_words(1)
         open_sums(table_pass, 1)
-        pick_ts(2)
-        round_on_vector(1, tag="handed")
-        quantize(1)
-        round_on_gpsimd(2, tag="handed")
+        second = kept([P, CHUNK, PACK], BF16, "second", "handed")
+        round_rows(nc.vector.tensor_copy, second[:], c_raw[1][:])
+        quantize((1,), second)
+        third = kept([P, CHUNK, PACK], BF16, "third", "handed")
+        round_on_gpsimd(third[:], c_raw[2][:])
         for m in range(N_TILES):
             finish(0, m, turn_back(0, m)[:])
         close_sums(dense_pass, 1)
         pick_words(2)
-        open_sums(table_pass, 2)
-        for m in range(2):
-            finish(1, m, scale_direct(1, m, sums[1, m])[:])
-        round_on_scalar(3)
-        for m in range(2, N_TILES):
-            finish(1, m, scale_direct(1, m, sums[1, m])[:])
         pick_ts(3)
-        quantize(2)
+        open_sums(table_pass, 2)
+        left = by_scalar([P, HALF, PACK], BF16, "left")
+        round_rows(nc.scalar.copy, left[:], c_raw[3][:, :, 0:HALF])
+        for m in range(0, 4):
+            finish(1, m, scale_direct(1, m, sums[1, m])[:])
+        quantize_part(3, left, 0, HALF)
+        quantize((2,), third)
+        right = kept([P, HALF, PACK], BF16, "right", "handed")
+        round_on_gpsimd(right[:], c_raw[3][:, :, HALF:CHUNK])
         close_sums(dense_pass, 2)
         pick_words(3)
         open_sums(table_pass, 3)
-        quantize(3)
+        for m in range(0, 2):
+            finish(2, m, scale_direct(2, m, sums[2, m])[:])
+        quantize_part(3, right, HALF, CHUNK)
         close_sums(dense_pass, 3)
-        for m in range(N_TILES):
+        for m in range(2, 4):
             finish(2, m, scale_direct(2, m, sums[2, m])[:])
         for m in range(N_TILES):
             for lo, hi in ((0, CHUNK),) if m < N_TILES - 1 else ((0, 256), (256, 512)):

@@ -26,7 +26,7 @@ HALF = CHUNK // 2
 TS_PER_PARTITION = T // P
 VECTOR_TILES = 24
 SCALAR_TILES = 24
-VECTOR_WIDE_TILES = 3
+VECTOR_WIDE_TILES = 4
 SCALAR_WIDE_TILES = 1
 
 
@@ -34,7 +34,7 @@ def tile_list_tabts_silu_kernel(tc, tab_words, tab_scales, w4_words, w4_scales, 
     nc = tc.nc
     with ExitStack() as ctx:
         keep = ctx.enter_context(tc.tile_pool(name="keep", bufs=1))
-        banks = ctx.enter_context(tc.psum_pool(name="banks", bufs=8))
+        banks = ctx.enter_context(tc.psum_pool(name="banks", bufs=4))
 
         def kept(shape, dtype, name, tag=None):
             return keep.tile(shape, dtype, name=name, tag=tag or name, align_bytes=64)
@@ -47,8 +47,8 @@ def tile_list_tabts_silu_kernel(tc, tab_words, tab_scales, w4_words, w4_scales, 
             tag, bufs = ("by_scalar_wide", SCALAR_WIDE_TILES) if wide else ("by_scalar", SCALAR_TILES)
             return keep.tile(shape, dtype, name=name, tag=tag, bufs=bufs, align_bytes=64)
 
-        def bank(name):
-            return banks.tile([P, CHUNK], F32, name=name, tag="bank")
+        def bank(name, half="upper"):
+            return banks.tile([P, CHUNK], F32, name=name, tag=half)
 
         offsets = kept([P, S // 16], U16, "offsets")
         tab_s = kept([P, T // 4], I32, "tab_s")
@@ -115,8 +115,8 @@ def tile_list_tabts_silu_kernel(tc, tab_words, tab_scales, w4_words, w4_scales, 
             words[i] = by_vector([P, CHUNK], U32, "words%d" % i, wide)
             nc.vector.tensor_copy(words[i][:], tab_w[:].bitcast(U32).indirect(listed(i)))
 
-        def pick_ts(i, n=1):
-            picked = by_vector([P, n * CHUNK], F32, "picked%d" % i, n > 1)
+        def pick_ts(i, n=1, wide=False):
+            picked = by_vector([P, n * CHUNK], F32, "picked%d" % i, wide or n > 1)
             nc.vector.tensor_copy(picked[:], ts_all[:].indirect(listed(i, n)))
             for k in range(n):
                 picked_t[i + k] = picked[:, k * CHUNK : (k + 1) * CHUNK]
@@ -175,7 +175,7 @@ def tile_list_tabts_silu_kernel(tc, tab_words, tab_scales, w4_words, w4_scales, 
 
         def open_sums(one_pass, i, tiles=range(N_TILES)):
             for m in tiles:
-                sums[i, m] = bank("acc")
+                sums[i, m] = bank("acc", "lower" if i in (0, 3) else "upper")
                 one_pass(i, m, sums[i, m], True)
 
         def close_sums(one_pass, i, tiles=range(N_TILES)):
@@ -197,7 +197,7 @@ def tile_list_tabts_silu_kernel(tc, tab_words, tab_scales, w4_words, w4_scales, 
         def turn_bias():
             turned = bank("turned")
             nc.tensor.transpose(turned[:, 0:P], b_rows[:], ident[:])
-            small["bias"] = by_scalar([P, N_TILES], F32, "bias")
+            small["bias"] = kept([P, N_TILES], F32, "bias", "u_raw")
             nc.scalar.copy(small["bias"][:], turned[:, 0:N_TILES])
 
         def scale_turned(i, a, acc):
@@ -209,7 +209,7 @@ def tile_list_tabts_silu_kernel(tc, tab_words, tab_scales, w4_words, w4_scales, 
             nc.vector.tensor_scalar(blocks[i, a][:], acc[:], ts_col[i][:, a : a + 1], None, ALU.mult)
 
         def turn_back(i, m):
-            turned = bank("turned")
+            turned = bank("turned", "lower")
             for a in reversed(range(BLOCKS)):
                 nc.tensor.transpose(turned[:, a * P : (a + 1) * P], blocks[i, a][:, m * P : (m + 1) * P], ident[:])
             return turned
@@ -225,9 +225,9 @@ def tile_list_tabts_silu_kernel(tc, tab_words, tab_scales, w4_words, w4_scales, 
         load_planes(nc.sync, tab_s, tab_scales[0])
         load_rows(u_raw, u)
         load_c(0)
+        nc.sync.dma_start(b_rows[0:N_TILES, :], b.rearrange("(m p) -> m p", p=P))
         load_words()
         load_planes(nc.sync, w4_s, w4_scales[0])
-        nc.sync.dma_start(b_rows[0:N_TILES, :], b.rearrange("(m p) -> m p", p=P))
         ts_window()
         first = kept([P, M + CHUNK, PACK], BF16, "first")
         round_on_gpsimd(first[:, 0:M, :], u_raw[:])
@@ -235,19 +235,17 @@ def tile_list_tabts_silu_kernel(tc, tab_words, tab_scales, w4_words, w4_scales, 
         load_c(1)
         load_c(2)
         load_c(3)
-        pick_ts(0, 3)
+        pick_ts(0, 2)
         round_rows(nc.scalar.copy, first[:, M : M + CHUNK, :], c_raw[0][:])
         ts_to_partitions(0)
+        turn_bias()
         quantize(("u", 0), first)
-        open_sums(turned_dense_pass, 0, range(2))
+        open_sums(turned_dense_pass, 0)
+        pick_ts(2, wide=True)
         pick_words(0)
-        close_sums(turned_table_pass, 0, range(2))
-        for a in range(2, BLOCKS):
-            open_sums(turned_table_pass, 0, [a])
-            close_sums(turned_dense_pass, 0, [a])
+        close_sums(turned_table_pass, 0)
         for a in range(BLOCKS):
             scale_turned(0, a, sums[0, a])
-        turn_bias()
         pick_words(1)
         open_sums(table_pass, 1)
         second = kept([P, CHUNK, PACK], BF16, "second", "handed")

@@ -34,7 +34,7 @@ def tile_list_tabts_silu_kernel(tc, tab_words, tab_scales, w4_words, w4_scales, 
     nc = tc.nc
     with ExitStack() as ctx:
         keep = ctx.enter_context(tc.tile_pool(name="keep", bufs=1))
-        banks = ctx.enter_context(tc.psum_pool(name="banks", bufs=4))
+        banks = ctx.enter_context(tc.psum_pool(name="banks", bufs=8))
 
         def kept(shape, dtype, name, tag=None):
             return keep.tile(shape, dtype, name=name, tag=tag or name, align_bytes=64)
@@ -48,7 +48,7 @@ def tile_list_tabts_silu_kernel(tc, tab_words, tab_scales, w4_words, w4_scales, 
             return keep.tile(shape, dtype, name=name, tag=tag, bufs=bufs, align_bytes=64)
 
         def bank(name, half="upper"):
-            return banks.tile([P, CHUNK], F32, name=name, tag=half)
+            return banks.tile([P, CHUNK], F32, name=name, tag="bank")
 
         offsets = kept([P, S // 16], U16, "offsets")
         tab_s = kept([P, T // 4], I32, "tab_s")
@@ -128,7 +128,7 @@ def tile_list_tabts_silu_kernel(tc, tab_words, tab_scales, w4_words, w4_scales, 
             copy(dst.rearrange("p (g e) i -> p g i e", e=4), raw.rearrange("p i (g e) -> p g i e", e=4))
 
         def quantize_part(key, rounded, lo, hi):
-            if lo == 0:
+            if key not in codes:
                 codes[key] = by_vector([P, CHUNK], U32, "codes_%s" % key)
                 scales[key] = kept([P, CHUNK], U8, "scales_%s" % key)
             nc.vector.quantize_mx(out=codes[key][:, lo:hi].bitcast(FP8X4), scales=scales[key][:, lo:hi], in_=rounded[:].rearrange("p w i -> p (w i)"))
@@ -173,9 +173,28 @@ def tile_list_tabts_silu_kernel(tc, tab_words, tab_scales, w4_words, w4_scales, 
             nc.tensor.matmul_mx(out=acc[:], lhsT=codes[i][:, cols].bitcast(FP8X4), lhsT_scale=scales[i][:, cols],
                                 rhs=codes["u"][:].bitcast(FP8X4), rhs_scale=scales["u"][:], start=first, stop=not first)
 
-        def open_sums(one_pass, i, tiles=range(N_TILES)):
+        def turned_half(i, first_tile, half="upper"):
+            n0 = first_tile * P
+            for pair in range(BLOCKS // 2):
+                acc = bank("acc", half)
+                for k in range(2):
+                    cols = slice((2 * pair + k) * P, (2 * pair + k + 1) * P)
+                    at = k * 2 * P
+                    nc.tensor.matmul_mx(out=acc[:, at : at + 2 * P], lhsT=codes[i][:, cols].bitcast(FP8X4), lhsT_scale=scales[i][:, cols],
+                                        rhs=codes["u"][:, n0 : n0 + 2 * P].bitcast(FP8X4), rhs_scale=scales["u"][:, n0 : n0 + 2 * P], start=True, stop=False)
+                    for t in range(2):
+                        n = n0 + t * P
+                        nc.tensor.matmul_mx(out=acc[:, at + t * P : at + (t + 1) * P], lhsT=words[i][:, cols].bitcast(FP8X4), lhsT_scale=picked_s[i][:, cols],
+                                            rhs=w4_bytes[:, 2 * n : 2 * (n + P)].bitcast(FP4X4), rhs_scale=w4_plane[:, n : n + P], start=False, stop=t == 1)
+                both = by_scalar([P, CHUNK], F32, "half%d_%d" % (i, pair))
+                for k in range(2):
+                    a = 2 * pair + k
+                    nc.scalar.activation(both[:, k * 2 * P : (k + 1) * 2 * P], acc[:, k * 2 * P : (k + 1) * 2 * P], ACT.Copy, scale=ts_col[i][:, a : a + 1])
+                    blocks[i, a] = both[:, k * 2 * P : (k + 1) * 2 * P]
+
+        def open_sums(one_pass, i, tiles=range(N_TILES), half="upper"):
             for m in tiles:
-                sums[i, m] = bank("acc", "lower" if i in (0, 3) else "upper")
+                sums[i, m] = bank("acc", half)
                 one_pass(i, m, sums[i, m], True)
 
         def close_sums(one_pass, i, tiles=range(N_TILES)):
@@ -191,7 +210,7 @@ def tile_list_tabts_silu_kernel(tc, tab_words, tab_scales, w4_words, w4_scales, 
             turned = bank("turned")
             for a in range(BLOCKS):
                 nc.tensor.transpose(turned[:, a * P : (a + 1) * P], picked_t[i][:, a * P : (a + 1) * P], ident[:])
-            ts_col[i] = kept([P, BLOCKS], F32, "ts_col%d" % i, "c_raw0")
+            ts_col[i] = kept([P, BLOCKS], F32, "ts_col%d" % i, "c_raw0" if i == 0 else None)
             nc.scalar.copy(ts_col[i][:], turned[:, 0:CHUNK:P])
 
         def turn_bias():
@@ -208,10 +227,10 @@ def tile_list_tabts_silu_kernel(tc, tab_words, tab_scales, w4_words, w4_scales, 
             blocks[i, a] = by_vector([P, M], F32, "block%d_%d" % (i, a))
             nc.vector.tensor_scalar(blocks[i, a][:], acc[:], ts_col[i][:, a : a + 1], None, ALU.mult)
 
-        def turn_back(i, m):
-            turned = bank("turned", "lower")
+        def turn_back(i, m, first_tile=0, half="lower"):
+            turned = bank("turned", half)
             for a in reversed(range(BLOCKS)):
-                nc.tensor.transpose(turned[:, a * P : (a + 1) * P], blocks[i, a][:, m * P : (m + 1) * P], ident[:])
+                nc.tensor.transpose(turned[:, a * P : (a + 1) * P], blocks[i, a][:, (m - first_tile) * P : (m - first_tile + 1) * P], ident[:])
             return turned
 
         nc.vector.memset(tab_s[:], 0)
@@ -240,41 +259,41 @@ def tile_list_tabts_silu_kernel(tc, tab_words, tab_scales, w4_words, w4_scales, 
         ts_to_partitions(0)
         turn_bias()
         quantize(("u", 0), first)
-        open_sums(turned_dense_pass, 0)
+        open_sums(turned_dense_pass, 0, half="lower")
         pick_ts(2, wide=True)
         pick_words(0)
         close_sums(turned_table_pass, 0)
         for a in range(BLOCKS):
             scale_turned(0, a, sums[0, a])
         pick_words(1)
-        open_sums(table_pass, 1)
+        open_sums(table_pass, 1, range(1, N_TILES))
         second = kept([P, CHUNK, PACK], BF16, "second", "handed")
         round_rows(nc.vector.tensor_copy, second[:], c_raw[1][:])
         quantize((1,), second)
-        third = kept([P, CHUNK, PACK], BF16, "third", "handed")
-        round_on_gpsimd(third[:], c_raw[2][:])
+        right = kept([P, HALF, PACK], BF16, "right", "handed")
+        round_on_gpsimd(right[:], c_raw[2][:, :, HALF:CHUNK])
+        left = by_scalar([P, HALF, PACK], BF16, "left")
+        round_rows(nc.scalar.copy, left[:], c_raw[2][:, :, 0:HALF])
+        open_sums(dense_pass, 1, [0])
+        close_sums(table_pass, 1, [0])
         for m in range(N_TILES):
             finish(0, m, turn_back(0, m)[:])
-        close_sums(dense_pass, 1)
+        close_sums(dense_pass, 1, range(1, N_TILES))
         pick_words(2)
         pick_ts(3)
-        open_sums(table_pass, 2)
-        left = by_scalar([P, HALF, PACK], BF16, "left")
-        round_rows(nc.scalar.copy, left[:], c_raw[3][:, :, 0:HALF])
-        for m in range(0, 4):
+        quantize_part(2, left, 0, HALF)
+        quantize_part(2, right, HALF, CHUNK)
+        fourth = kept([P, CHUNK, PACK], BF16, "fourth", "handed")
+        round_on_gpsimd(fourth[:], c_raw[3][:])
+        for m in range(N_TILES):
             finish(1, m, scale_direct(1, m, sums[1, m])[:])
-        quantize_part(3, left, 0, HALF)
-        quantize((2,), third)
-        right = kept([P, HALF, PACK], BF16, "right", "handed")
-        round_on_gpsimd(right[:], c_raw[3][:, :, HALF:CHUNK])
-        close_sums(dense_pass, 2)
+            open_sums(table_pass, 2, [m])
+            close_sums(dense_pass, 2, [m])
         pick_words(3)
         open_sums(table_pass, 3)
-        for m in range(0, 2):
-            finish(2, m, scale_direct(2, m, sums[2, m])[:])
-        quantize_part(3, right, HALF, CHUNK)
+        quantize((3,), fourth)
         close_sums(dense_pass, 3)
-        for m in range(2, 4):
+        for m in range(0, 4):
             finish(2, m, scale_direct(2, m, sums[2, m])[:])
         for m in range(N_TILES):
             for lo, hi in ((0, CHUNK),) if m < N_TILES - 1 else ((0, 256), (256, 512)):

@@ -291,10 +291,11 @@ def tile_list_tabts_silu_kernel(tc, tab_words, tab_scales, w4_words, w4_scales, 
             close_sums(dense_pass, 2, [m])
         pick_words(3)
         open_sums(table_pass, 3)
+        for m in range(0, 2):
+            finish(2, m, scale_direct(2, m, sums[2, m])[:])
         quantize((3,), fourth)
         close_sums(dense_pass, 3)
-        for m in range(0, 4):
+        for m in range(2, 4):
             finish(2, m, scale_direct(2, m, sums[2, m])[:])
-        for m in range(N_TILES):
-            for lo, hi in ((0, CHUNK),) if m < N_TILES - 1 else ((0, 256), (256, 512)):
-                finish(3, m, scale_direct(3, m, sums[3, m], lo, hi)[:], lo, hi)
+        for m in range(0, 4):
+            finish(3, m, scale_direct(3, m, sums[3, m])[:])

@@ -297,5 +297,6 @@ def tile_list_tabts_silu_kernel(tc, tab_words, tab_scales, w4_words, w4_scales, 
         close_sums(dense_pass, 3)
         for m in range(2, 4):
             finish(2, m, scale_direct(2, m, sums[2, m])[:])
-        for m in range(0, 4):
-            finish(3, m, scale_direct(3, m, sums[3, m])[:])
+        for m in range(N_TILES):
+            for lo, hi in ((0, CHUNK),) if m < N_TILES - 1 else ((0, 256), (256, 512)):
+                finish(3, m, scale_direct(3, m, sums[3, m], lo, hi)[:], lo, hi)

@@ -23,8 +23,9 @@ N_CHUNKS = S // CHUNK
 N_TILES = M // P
 BLOCKS = CHUNK // P
 HALF = CHUNK // 2
+SHARE = 384
 TS_PER_PARTITION = T // P
-VECTOR_TILES = 24
+VECTOR_TILES = 25
 SCALAR_TILES = 24
 VECTOR_WIDE_TILES = 4
 SCALAR_WIDE_TILES = 1
@@ -92,14 +93,14 @@ def tile_list_tabts_silu_kernel(tc, tab_words, tab_scales, w4_words, w4_scales, 
             nc.sync.dma_start(tab_w[:], tab_words[0].rearrange("p t i -> p (t i)").bitcast(I32))
 
         def ts_window():
-            for g in range(T // CHUNK):
+            starts = list(range(0, TS_PER_PARTITION - 2, BLOCKS)) + [TS_PER_PARTITION - 2, TS_PER_PARTITION]
+            for lo, hi in zip(starts, starts[1:]):
                 turned = bank("turned")
-                for a in range(BLOCKS):
-                    col = g * BLOCKS + a
-                    nc.tensor.transpose(turned[:, a * P : (a + 1) * P], ts_cols[:, col : col + 1].to_broadcast([P, P]), ident[:])
+                for a in range(hi - lo):
+                    nc.tensor.transpose(turned[:, a * P : (a + 1) * P], ts_cols[:, lo + a : lo + a + 1].to_broadcast([P, P]), ident[:])
                 nc.scalar.copy(
-                    ts_all[:].rearrange("q (p a) -> q p a", p=P)[:, :, g * BLOCKS : (g + 1) * BLOCKS],
-                    turned[:].rearrange("q (a p) -> q p a", p=P),
+                    ts_all[:].rearrange("q (p a) -> q p a", p=P)[:, :, lo:hi],
+                    turned[:, 0 : (hi - lo) * P].rearrange("q (a p) -> q p a", p=P),
                 )
 
         def listed(i, n=1):
@@ -237,16 +238,16 @@ def tile_list_tabts_silu_kernel(tc, tab_words, tab_scales, w4_words, w4_scales, 
         identity()
         nc.gpsimd.memset(w4_s[:], 0)
         nc.gpsimd.memset(b_rows[:], 0.0)
+        load_planes(nc.gpsimd, w4_s, w4_scales[0])
         nc.scalar.activation(warm[:], ones[:, 0:1], ACT.Silu, bias=ones[:, 1:2])
-        nc.sync.dma_start(offsets[:], offs)
         nc.sync.dma_start(ts_cols[:], ts[0].rearrange("(p a) -> p a", p=P))
+        nc.sync.dma_start(offsets[:], offs)
         nc.sync.dma_start(w4_w[:], w4_words[0].bitcast(I32))
         load_planes(nc.sync, tab_s, tab_scales[0])
         load_rows(u_raw, u)
         load_c(0)
         nc.sync.dma_start(b_rows[0:N_TILES, :], b.rearrange("(m p) -> m p", p=P))
         load_words()
-        load_planes(nc.sync, w4_s, w4_scales[0])
         ts_window()
         first = kept([P, M + CHUNK, PACK], BF16, "first")
         round_on_gpsimd(first[:, 0:M, :], u_raw[:])
@@ -255,7 +256,8 @@ def tile_list_tabts_silu_kernel(tc, tab_words, tab_scales, w4_words, w4_scales, 
         load_c(2)
         load_c(3)
         pick_ts(0, 2)
-        round_rows(nc.scalar.copy, first[:, M : M + CHUNK, :], c_raw[0][:])
+        round_rows(nc.scalar.copy, first[:, M : M + SHARE, :], c_raw[0][:, :, 0:SHARE])
+        round_on_gpsimd(first[:, M + SHARE : M + CHUNK, :], c_raw[0][:, :, SHARE:CHUNK])
         ts_to_partitions(0)
         turn_bias()
         quantize(("u", 0), first)
@@ -266,27 +268,35 @@ def tile_list_tabts_silu_kernel(tc, tab_words, tab_scales, w4_words, w4_scales, 
         for a in range(BLOCKS):
             scale_turned(0, a, sums[0, a])
         pick_words(1)
-        open_sums(table_pass, 1, range(1, N_TILES))
-        second = kept([P, CHUNK, PACK], BF16, "second", "handed")
-        round_rows(nc.vector.tensor_copy, second[:], c_raw[1][:])
-        quantize((1,), second)
+        open_sums(table_pass, 1)
+        c1_right = kept([P, HALF, PACK], BF16, "c1_right", "handed")
+        round_on_gpsimd(c1_right[:], c_raw[1][:, :, HALF:CHUNK])
+        pick_words(2)
+        open_sums(table_pass, 2, range(2))
+        c1_left = by_vector([P, HALF, PACK], BF16, "c1_left")
+        round_rows(nc.vector.tensor_copy, c1_left[:], c_raw[1][:, :, 0:HALF])
+        quantize_part(1, c1_right, HALF, CHUNK)
+        quantize_part(1, c1_left, 0, HALF)
         right = kept([P, HALF, PACK], BF16, "right", "handed")
         round_on_gpsimd(right[:], c_raw[2][:, :, HALF:CHUNK])
         left = by_scalar([P, HALF, PACK], BF16, "left")
         round_rows(nc.scalar.copy, left[:], c_raw[2][:, :, 0:HALF])
-        open_sums(dense_pass, 1, [0])
-        close_sums(table_pass, 1, [0])
-        for m in range(N_TILES):
+        for m in range(2):
             finish(0, m, turn_back(0, m)[:])
-        close_sums(dense_pass, 1, range(1, N_TILES))
-        pick_words(2)
+        close_sums(dense_pass, 1)
+        for m in range(2, N_TILES):
+            finish(0, m, turn_back(0, m)[:])
         pick_ts(3)
+        products = [scale_direct(1, 0, sums[1, 0])]
         quantize_part(2, left, 0, HALF)
         quantize_part(2, right, HALF, CHUNK)
         fourth = kept([P, CHUNK, PACK], BF16, "fourth", "handed")
         round_on_gpsimd(fourth[:], c_raw[3][:])
+        products.extend(scale_direct(1, m, sums[1, m]) for m in range(1, N_TILES))
         for m in range(N_TILES):
-            finish(1, m, scale_direct(1, m, sums[1, m])[:])
+            finish(1, m, products[m][:])
+        close_sums(dense_pass, 2, range(2))
+        for m in range(2, N_TILES):
             open_sums(table_pass, 2, [m])
             close_sums(dense_pass, 2, [m])
         pick_words(3)

@@ -238,7 +238,6 @@ def tile_list_tabts_silu_kernel(tc, tab_words, tab_scales, w4_words, w4_scales, 
         identity()
         nc.gpsimd.memset(w4_s[:], 0)
         nc.gpsimd.memset(b_rows[:], 0.0)
-        load_planes(nc.gpsimd, w4_s, w4_scales[0])
         nc.scalar.activation(warm[:], ones[:, 0:1], ACT.Silu, bias=ones[:, 1:2])
         nc.sync.dma_start(ts_cols[:], ts[0].rearrange("(p a) -> p a", p=P))
         nc.sync.dma_start(offsets[:], offs)
@@ -248,6 +247,7 @@ def tile_list_tabts_silu_kernel(tc, tab_words, tab_scales, w4_words, w4_scales, 
         load_c(0)
         nc.sync.dma_start(b_rows[0:N_TILES, :], b.rearrange("(m p) -> m p", p=P))
         load_words()
+        load_planes(nc.sync, w4_s, w4_scales[0])
         ts_window()
         first = kept([P, M + CHUNK, PACK], BF16, "first")
         round_on_gpsimd(first[:, 0:M, :], u_raw[:])

@@ -93,14 +93,14 @@ def tile_list_tabts_silu_kernel(tc, tab_words, tab_scales, w4_words, w4_scales, 
             nc.sync.dma_start(tab_w[:], tab_words[0].rearrange("p t i -> p (t i)").bitcast(I32))
 
         def ts_window():
-            starts = list(range(0, TS_PER_PARTITION - 2, BLOCKS)) + [TS_PER_PARTITION - 2, TS_PER_PARTITION]
-            for lo, hi in zip(starts, starts[1:]):
+            for g in range(T // CHUNK):
                 turned = bank("turned")
-                for a in range(hi - lo):
-                    nc.tensor.transpose(turned[:, a * P : (a + 1) * P], ts_cols[:, lo + a : lo + a + 1].to_broadcast([P, P]), ident[:])
+                for a in range(BLOCKS):
+                    col = g * BLOCKS + a
+                    nc.tensor.transpose(turned[:, a * P : (a + 1) * P], ts_cols[:, col : col + 1].to_broadcast([P, P]), ident[:])
                 nc.scalar.copy(
-                    ts_all[:].rearrange("q (p a) -> q p a", p=P)[:, :, lo:hi],
-                    turned[:, 0 : (hi - lo) * P].rearrange("q (a p) -> q p a", p=P),
+                    ts_all[:].rearrange("q (p a) -> q p a", p=P)[:, :, g * BLOCKS : (g + 1) * BLOCKS],
+                    turned[:].rearrange("q (a p) -> q p a", p=P),
                 )
 
         def listed(i, n=1):

@@ -25,7 +25,7 @@ BLOCKS = CHUNK // P
 HALF = CHUNK // 2
 SHARE = 384
 TS_PER_PARTITION = T // P
-VECTOR_TILES = 25
+VECTOR_TILES = 24
 SCALAR_TILES = 24
 VECTOR_WIDE_TILES = 4
 SCALAR_WIDE_TILES = 1
@@ -269,11 +269,11 @@ def tile_list_tabts_silu_kernel(tc, tab_words, tab_scales, w4_words, w4_scales, 
             scale_turned(0, a, sums[0, a])
         pick_words(1)
         open_sums(table_pass, 1)
-        c1_right = kept([P, HALF, PACK], BF16, "c1_right", "handed")
+        c1_right = kept([P, HALF, PACK], BF16, "c1_right")
         round_on_gpsimd(c1_right[:], c_raw[1][:, :, HALF:CHUNK])
         pick_words(2)
         open_sums(table_pass, 2, range(2))
-        c1_left = by_vector([P, HALF, PACK], BF16, "c1_left")
+        c1_left = kept([P, HALF, PACK], BF16, "c1_left", "handed")
         round_rows(nc.vector.tensor_copy, c1_left[:], c_raw[1][:, :, 0:HALF])
         quantize_part(1, c1_right, HALF, CHUNK)
         quantize_part(1, c1_left, 0, HALF)

@@ -23,6 +23,8 @@ N_CHUNKS = S // CHUNK
 N_TILES = M // P
 BLOCKS = CHUNK // P
 HALF = CHUNK // 2
+EDGE = 128
+CUT = 160
 SHARE = 384
 TS_PER_PARTITION = T // P
 VECTOR_TILES = 24
@@ -268,38 +270,39 @@ def tile_list_tabts_silu_kernel(tc, tab_words, tab_scales, w4_words, w4_scales, 
         for a in range(BLOCKS):
             scale_turned(0, a, sums[0, a])
         pick_words(1)
-        open_sums(table_pass, 1)
-        c1_right = kept([P, HALF, PACK], BF16, "c1_right")
-        round_on_gpsimd(c1_right[:], c_raw[1][:, :, HALF:CHUNK])
+        open_sums(table_pass, 1, range(2))
+        second = kept([P, CHUNK, PACK], BF16, "second", "handed")
+        round_on_gpsimd(second[:, CUT:CHUNK, :], c_raw[1][:, :, CUT:CHUNK])
         pick_words(2)
         open_sums(table_pass, 2, range(2))
-        c1_left = kept([P, HALF, PACK], BF16, "c1_left", "handed")
-        round_rows(nc.vector.tensor_copy, c1_left[:], c_raw[1][:, :, 0:HALF])
-        quantize_part(1, c1_right, HALF, CHUNK)
-        quantize_part(1, c1_left, 0, HALF)
+        pick_ts(3)
+        round_rows(nc.vector.tensor_copy, second[:, 0:CUT, :], c_raw[1][:, :, 0:CUT])
+        quantize((1,), second)
         right = kept([P, HALF, PACK], BF16, "right", "handed")
         round_on_gpsimd(right[:], c_raw[2][:, :, HALF:CHUNK])
         left = by_scalar([P, HALF, PACK], BF16, "left")
         round_rows(nc.scalar.copy, left[:], c_raw[2][:, :, 0:HALF])
-        for m in range(2):
+        for m in range(N_TILES):
             finish(0, m, turn_back(0, m)[:])
-        close_sums(dense_pass, 1)
+        close_sums(dense_pass, 1, range(2))
         for m in range(2, N_TILES):
-            finish(0, m, turn_back(0, m)[:])
-        pick_ts(3)
+            open_sums(dense_pass, 1, [m])
+            close_sums(table_pass, 1, [m])
+        pick_words(3)
         products = [scale_direct(1, 0, sums[1, 0])]
         quantize_part(2, left, 0, HALF)
         quantize_part(2, right, HALF, CHUNK)
         fourth = kept([P, CHUNK, PACK], BF16, "fourth", "handed")
-        round_on_gpsimd(fourth[:], c_raw[3][:])
+        round_on_gpsimd(fourth[:, EDGE:CHUNK, :], c_raw[3][:, :, EDGE:CHUNK])
         products.extend(scale_direct(1, m, sums[1, m]) for m in range(1, N_TILES))
-        for m in range(N_TILES):
+        finish(1, 0, products[0][:])
+        round_rows(nc.scalar.copy, fourth[:, 0:EDGE, :], c_raw[3][:, :, 0:EDGE])
+        for m in range(1, N_TILES):
             finish(1, m, products[m][:])
         close_sums(dense_pass, 2, range(2))
         for m in range(2, N_TILES):
             open_sums(table_pass, 2, [m])
             close_sums(dense_pass, 2, [m])
-        pick_words(3)
         open_sums(table_pass, 3)
         for m in range(0, 2):
             finish(2, m, scale_direct(2, m, sums[2, m])[:])

@@ -37,7 +37,7 @@ def tile_list_tabts_silu_kernel(tc, tab_words, tab_scales, w4_words, w4_scales, 
     nc = tc.nc
     with ExitStack() as ctx:
         keep = ctx.enter_context(tc.tile_pool(name="keep", bufs=1))
-        banks = ctx.enter_context(tc.psum_pool(name="banks", bufs=8))
+        banks = ctx.enter_context(tc.psum_pool(name="banks", bufs=4))
 
         def kept(shape, dtype, name, tag=None):
             return keep.tile(shape, dtype, name=name, tag=tag or name, align_bytes=64)
@@ -51,7 +51,7 @@ def tile_list_tabts_silu_kernel(tc, tab_words, tab_scales, w4_words, w4_scales, 
             return keep.tile(shape, dtype, name=name, tag=tag, bufs=bufs, align_bytes=64)
 
         def bank(name, half="upper"):
-            return banks.tile([P, CHUNK], F32, name=name, tag="bank")
+            return banks.tile([P, CHUNK], F32, name=name, tag=half)
 
         offsets = kept([P, S // 16], U16, "offsets")
         tab_s = kept([P, T // 4], I32, "tab_s")
@@ -269,13 +269,12 @@ def tile_list_tabts_silu_kernel(tc, tab_words, tab_scales, w4_words, w4_scales, 
         close_sums(turned_table_pass, 0)
         for a in range(BLOCKS):
             scale_turned(0, a, sums[0, a])
+        pick_ts(3)
         pick_words(1)
-        open_sums(table_pass, 1, range(2))
+        open_sums(table_pass, 1)
         second = kept([P, CHUNK, PACK], BF16, "second", "handed")
         round_on_gpsimd(second[:, CUT:CHUNK, :], c_raw[1][:, :, CUT:CHUNK])
         pick_words(2)
-        open_sums(table_pass, 2, range(2))
-        pick_ts(3)
         round_rows(nc.vector.tensor_copy, second[:, 0:CUT, :], c_raw[1][:, :, 0:CUT])
         quantize((1,), second)
         right = kept([P, HALF, PACK], BF16, "right", "handed")
@@ -284,10 +283,8 @@ def tile_list_tabts_silu_kernel(tc, tab_words, tab_scales, w4_words, w4_scales, 
         round_rows(nc.scalar.copy, left[:], c_raw[2][:, :, 0:HALF])
         for m in range(N_TILES):
             finish(0, m, turn_back(0, m)[:])
-        close_sums(dense_pass, 1, range(2))
-        for m in range(2, N_TILES):
-            open_sums(dense_pass, 1, [m])
-            close_sums(table_pass, 1, [m])
+        close_sums(dense_pass, 1)
+        open_sums(table_pass, 2, half="lower")
         pick_words(3)
         products = [scale_direct(1, 0, sums[1, 0])]
         quantize_part(2, left, 0, HALF)
@@ -299,10 +296,7 @@ def tile_list_tabts_silu_kernel(tc, tab_words, tab_scales, w4_words, w4_scales, 
         round_rows(nc.scalar.copy, fourth[:, 0:EDGE, :], c_raw[3][:, :, 0:EDGE])
         for m in range(1, N_TILES):
             finish(1, m, products[m][:])
-        close_sums(dense_pass, 2, range(2))
-        for m in range(2, N_TILES):
-            open_sums(table_pass, 2, [m])
-            close_sums(dense_pass, 2, [m])
+        close_sums(dense_pass, 2)
         open_sums(table_pass, 3)
         for m in range(0, 2):
             finish(2, m, scale_direct(2, m, sums[2, m])[:])

@@ -125,7 +125,7 @@ def tile_list_tabts_silu_kernel(tc, tab_words, tab_scales, w4_words, w4_scales, 
                 picked_t[i + k] = picked[:, k * CHUNK : (k + 1) * CHUNK]
 
         def round_on_gpsimd(dst, raw):
-            nc.gpsimd.tensor_scalar(dst, raw.rearrange("p i w -> p w i"), 1.0, 0.0, ALU.mult, ALU.add)
+            nc.gpsimd.tensor_scalar(dst.rearrange("p (g e) i -> p g i e", e=4), raw.rearrange("p i (g e) -> p g i e", e=4), 1.0, 0.0, ALU.mult, ALU.add)
 
         def round_rows(copy, dst, raw):
             copy(dst.rearrange("p (g e) i -> p g i e", e=4), raw.rearrange("p i (g e) -> p g i e", e=4))

@@ -23,14 +23,9 @@ N_CHUNKS = S // CHUNK
 N_TILES = M // P
 BLOCKS = CHUNK // P
 HALF = CHUNK // 2
-EDGE = 128
-CUT = 160
-SHARE = 384
 TS_PER_PARTITION = T // P
-VECTOR_TILES = 24
-SCALAR_TILES = 24
-VECTOR_WIDE_TILES = 4
-SCALAR_WIDE_TILES = 1
+VECTOR_TILES = 30
+SCALAR_TILES = 26
 
 
 def tile_list_tabts_silu_kernel(tc, tab_words, tab_scales, w4_words, w4_scales, c, u, ts, b, offs, out):
@@ -42,13 +37,11 @@ def tile_list_tabts_silu_kernel(tc, tab_words, tab_scales, w4_words, w4_scales, 
         def kept(shape, dtype, name, tag=None):
             return keep.tile(shape, dtype, name=name, tag=tag or name, align_bytes=64)
 
-        def by_vector(shape, dtype, name, wide=False):
-            tag, bufs = ("by_vector_wide", VECTOR_WIDE_TILES) if wide else ("by_vector", VECTOR_TILES)
-            return keep.tile(shape, dtype, name=name, tag=tag, bufs=bufs, align_bytes=64)
+        def by_vector(shape, dtype, name):
+            return keep.tile(shape, dtype, name=name, tag="by_vector", bufs=VECTOR_TILES, align_bytes=64)
 
-        def by_scalar(shape, dtype, name, wide=False):
-            tag, bufs = ("by_scalar_wide", SCALAR_WIDE_TILES) if wide else ("by_scalar", SCALAR_TILES)
-            return keep.tile(shape, dtype, name=name, tag=tag, bufs=bufs, align_bytes=64)
+        def by_scalar(shape, dtype, name):
+            return keep.tile(shape, dtype, name=name, tag="by_scalar", bufs=SCALAR_TILES, align_bytes=64)
 
         def bank(name, half="upper"):
             return banks.tile([P, CHUNK], F32, name=name, tag=half)
@@ -69,9 +62,10 @@ def tile_list_tabts_silu_kernel(tc, tab_words, tab_scales, w4_words, w4_scales, 
         tab_w = kept([P, T], I32, "tab_w")
         u_raw = kept([P, PACK, M], F32, "u_raw")
         c_raw = [kept([P, PACK, CHUNK], F32, "c_raw%d" % i) for i in range(N_CHUNKS)]
+        planes = kept([P, S // 4], I32, "planes", "ramp")
         w4_bytes = w4_w[:].bitcast(U8)
         w4_plane = w4_s[:].bitcast(U8)
-        codes, scales, words, picked_s, picked_t, ts_col, blocks, small, sums, rounded = {}, {}, {}, {}, {}, {}, {}, {}, {}, {}
+        codes, pieces, words, picked_s, picked_t, ts_col, blocks, small, sums = {}, {}, {}, {}, {}, {}, {}, {}, {}
 
         def identity():
             nc.gpsimd.memset(ones[:], 1.0)
@@ -105,24 +99,26 @@ def tile_list_tabts_silu_kernel(tc, tab_words, tab_scales, w4_words, w4_scales, 
                     turned[:].rearrange("q (a p) -> q p a", p=P),
                 )
 
-        def listed(i, n=1):
-            return offsets[:, i * (CHUNK // 16) : (i + n) * (CHUNK // 16)]
+        def listed(i):
+            return offsets[:, i * (CHUNK // 16) : (i + 1) * (CHUNK // 16)]
 
-        def pick_scales(i, n):
-            plane = by_vector([P, n * CHUNK], U8, "plane%d" % i, True)
-            nc.vector.tensor_copy(plane[:], tab_s[:].bitcast(U8).indirect(listed(i, n)))
-            for k in range(n):
-                picked_s[i + k] = plane[:, k * CHUNK : (k + 1) * CHUNK]
+        def pick_scales():
+            small["rows"] = by_vector([P, S], U8, "rows")
+            nc.vector.tensor_copy(small["rows"][:], tab_s[:].bitcast(U8).indirect(offsets[:]))
 
-        def pick_words(i, wide=False):
-            words[i] = by_vector([P, CHUNK], U32, "words%d" % i, wide)
+        def place_scales(queue):
+            for r in range(4):
+                queue.dma_start(planes[r:P:32, :], small["rows"][8 * r : P : 32, :].bitcast(I32))
+            for i in range(N_CHUNKS):
+                picked_s[i] = planes[:].bitcast(U8)[:, i * CHUNK : (i + 1) * CHUNK]
+
+        def pick_words(i):
+            words[i] = by_vector([P, CHUNK], U32, "words%d" % i)
             nc.vector.tensor_copy(words[i][:], tab_w[:].bitcast(U32).indirect(listed(i)))
 
-        def pick_ts(i, n=1, wide=False):
-            picked = by_vector([P, n * CHUNK], F32, "picked%d" % i, wide or n > 1)
-            nc.vector.tensor_copy(picked[:], ts_all[:].indirect(listed(i, n)))
-            for k in range(n):
-                picked_t[i + k] = picked[:, k * CHUNK : (k + 1) * CHUNK]
+        def pick_ts(i):
+            picked_t[i] = by_vector([P, CHUNK], F32, "picked%d" % i)
+            nc.vector.tensor_copy(picked_t[i][:], ts_all[:].indirect(listed(i)))
 
         def round_on_gpsimd(dst, raw):
             nc.gpsimd.tensor_scalar(dst.rearrange("p (g e) i -> p g i e", e=4), raw.rearrange("p i (g e) -> p g i e", e=4), 1.0, 0.0, ALU.mult, ALU.add)
@@ -130,31 +126,39 @@ def tile_list_tabts_silu_kernel(tc, tab_words, tab_scales, w4_words, w4_scales, 
         def round_rows(copy, dst, raw):
             copy(dst.rearrange("p (g e) i -> p g i e", e=4), raw.rearrange("p i (g e) -> p g i e", e=4))
 
-        def quantize_part(key, rounded, lo, hi):
-            if key not in codes:
-                codes[key] = by_vector([P, CHUNK], U32, "codes_%s" % key)
-                scales[key] = kept([P, CHUNK], U8, "scales_%s" % key)
-            nc.vector.quantize_mx(out=codes[key][:, lo:hi].bitcast(FP8X4), scales=scales[key][:, lo:hi], in_=rounded[:].rearrange("p w i -> p (w i)"))
+        def round_piece(engine, key, raw, lo, hi):
+            if engine == "gpsimd":
+                piece = kept([P, hi - lo, PACK], BF16, "piece", "handed")
+                round_on_gpsimd(piece[:], raw[:, :, lo:hi])
+            elif engine == "scalar":
+                piece = by_scalar([P, hi - lo, PACK], BF16, "piece")
+                round_rows(nc.scalar.copy, piece[:], raw[:, :, lo:hi])
+            else:
+                piece = by_vector([P, hi - lo, PACK], BF16, "piece")
+                round_rows(nc.vector.tensor_copy, piece[:], raw[:, :, lo:hi])
+            pieces[key, lo] = (piece, hi)
 
-        def quantize(keys, rounded):
-            width = CHUNK * len(keys)
-            made = by_vector([P, width], U32, "codes_%s" % keys[0], len(keys) > 1)
-            plane = kept([P, width], U8, "scales_%s" % keys[0])
-            nc.vector.quantize_mx(out=made[:].bitcast(FP8X4), scales=plane[:], in_=rounded[:].rearrange("p w i -> p (w i)"))
-            for k, key in enumerate(keys):
-                codes[key] = made[:, k * CHUNK : (k + 1) * CHUNK]
-                scales[key] = plane[:, k * CHUNK : (k + 1) * CHUNK]
+        def quantize(key, lo):
+            piece, hi = pieces[key, lo]
+            made = by_vector([P, hi - lo], U32, "codes_%s" % key)
+            plane = kept([P, hi - lo], U8, "scales_%s_%d" % (key, lo))
+            nc.vector.quantize_mx(out=made[:].bitcast(FP8X4), scales=plane[:], in_=piece[:].rearrange("p w i -> p (w i)"))
+            codes.setdefault(key, []).append((lo, hi, made, plane))
 
-        def finish(i, m, src, lo=0, hi=CHUNK, wide=False):
-            result = by_scalar([P, hi - lo], F32, "result", wide)
+        def stationary(key, at):
+            lo, hi, made, plane = [part for part in codes[key] if part[0] <= at < part[1]][0]
+            return made[:, at - lo : at - lo + P].bitcast(FP8X4), plane[:, at - lo : at - lo + P]
+
+        def dense(acc, fixed, moving, first):
+            lhs, lhs_scale = fixed
+            for k, (lo, hi, made, plane) in enumerate(moving):
+                nc.tensor.matmul_mx(out=acc[:, lo:hi], lhsT=lhs, lhsT_scale=lhs_scale, rhs=made[:].bitcast(FP8X4), rhs_scale=plane[:],
+                                    start=first and k == 0, stop=not first and k == len(moving) - 1)
+
+        def finish(i, m, src, lo=0, hi=CHUNK):
+            result = by_scalar([P, hi - lo], F32, "result")
             nc.scalar.activation(result[:], src, ACT.Silu, bias=small["bias"][:, m : m + 1])
             nc.sync.dma_start(out[m * P : (m + 1) * P, i * CHUNK + lo : i * CHUNK + hi], result[:])
-
-        def finish_pair(i, m, left, right):
-            result = by_scalar([P, 2 * CHUNK], F32, "pair", True)
-            for k, src in enumerate((left, right)):
-                nc.scalar.activation(result[:, k * CHUNK : (k + 1) * CHUNK], src, ACT.Silu, bias=small["bias"][:, m : m + 1])
-            nc.sync.dma_start(out[m * P : (m + 1) * P, i * CHUNK : (i + 2) * CHUNK], result[:])
 
         def table_pass(i, m, acc, first):
             cols = slice(m * P, (m + 1) * P)
@@ -162,9 +166,7 @@ def tile_list_tabts_silu_kernel(tc, tab_words, tab_scales, w4_words, w4_scales, 
                                 rhs=words[i][:].bitcast(FP8X4), rhs_scale=picked_s[i], start=first, stop=not first)
 
         def dense_pass(i, m, acc, first):
-            cols = slice(m * P, (m + 1) * P)
-            nc.tensor.matmul_mx(out=acc[:], lhsT=codes["u"][:, cols].bitcast(FP8X4), lhsT_scale=scales["u"][:, cols],
-                                rhs=codes[i][:].bitcast(FP8X4), rhs_scale=scales[i][:], start=first, stop=not first)
+            dense(acc, stationary("u", m * P), codes[i], first)
 
         def turned_table_pass(i, a, acc, first):
             cols = slice(a * P, (a + 1) * P)
@@ -172,28 +174,7 @@ def tile_list_tabts_silu_kernel(tc, tab_words, tab_scales, w4_words, w4_scales, 
                                 rhs=w4_bytes.bitcast(FP4X4), rhs_scale=w4_plane, start=first, stop=not first)
 
         def turned_dense_pass(i, a, acc, first):
-            cols = slice(a * P, (a + 1) * P)
-            nc.tensor.matmul_mx(out=acc[:], lhsT=codes[i][:, cols].bitcast(FP8X4), lhsT_scale=scales[i][:, cols],
-                                rhs=codes["u"][:].bitcast(FP8X4), rhs_scale=scales["u"][:], start=first, stop=not first)
-
-        def turned_half(i, first_tile, half="upper"):
-            n0 = first_tile * P
-            for pair in range(BLOCKS // 2):
-                acc = bank("acc", half)
-                for k in range(2):
-                    cols = slice((2 * pair + k) * P, (2 * pair + k + 1) * P)
-                    at = k * 2 * P
-                    nc.tensor.matmul_mx(out=acc[:, at : at + 2 * P], lhsT=codes[i][:, cols].bitcast(FP8X4), lhsT_scale=scales[i][:, cols],
-                                        rhs=codes["u"][:, n0 : n0 + 2 * P].bitcast(FP8X4), rhs_scale=scales["u"][:, n0 : n0 + 2 * P], start=True, stop=False)
-                    for t in range(2):
-                        n = n0 + t * P
-                        nc.tensor.matmul_mx(out=acc[:, at + t * P : at + (t + 1) * P], lhsT=words[i][:, cols].bitcast(FP8X4), lhsT_scale=picked_s[i][:, cols],
-                                            rhs=w4_bytes[:, 2 * n : 2 * (n + P)].bitcast(FP4X4), rhs_scale=w4_plane[:, n : n + P], start=False, stop=t == 1)
-                both = by_scalar([P, CHUNK], F32, "half%d_%d" % (i, pair))
-                for k in range(2):
-                    a = 2 * pair + k
-                    nc.scalar.activation(both[:, k * 2 * P : (k + 1) * 2 * P], acc[:, k * 2 * P : (k + 1) * 2 * P], ACT.Copy, scale=ts_col[i][:, a : a + 1])
-                    blocks[i, a] = both[:, k * 2 * P : (k + 1) * 2 * P]
+            dense(acc, stationary(i, a * P), codes["u"], first)
 
         def open_sums(one_pass, i, tiles=range(N_TILES), half="upper"):
             for m in tiles:
@@ -213,97 +194,92 @@ def tile_list_tabts_silu_kernel(tc, tab_words, tab_scales, w4_words, w4_scales, 
             turned = bank("turned")
             for a in range(BLOCKS):
                 nc.tensor.transpose(turned[:, a * P : (a + 1) * P], picked_t[i][:, a * P : (a + 1) * P], ident[:])
-            ts_col[i] = kept([P, BLOCKS], F32, "ts_col%d" % i, "c_raw0" if i == 0 else None)
+            ts_col[i] = by_scalar([P, BLOCKS], F32, "ts_col%d" % i)
             nc.scalar.copy(ts_col[i][:], turned[:, 0:CHUNK:P])
 
         def turn_bias():
             turned = bank("turned")
             nc.tensor.transpose(turned[:, 0:P], b_rows[:], ident[:])
-            small["bias"] = kept([P, N_TILES], F32, "bias", "u_raw")
+            small["bias"] = by_scalar([P, N_TILES], F32, "bias")
             nc.scalar.copy(small["bias"][:], turned[:, 0:N_TILES])
 
         def scale_turned(i, a, acc):
             blocks[i, a] = by_scalar([P, M], F32, "block%d_%d" % (i, a))
             nc.scalar.activation(blocks[i, a][:], acc[:], ACT.Copy, scale=ts_col[i][:, a : a + 1])
 
-        def scale_turned_on_vector(i, a, acc):
-            blocks[i, a] = by_vector([P, M], F32, "block%d_%d" % (i, a))
-            nc.vector.tensor_scalar(blocks[i, a][:], acc[:], ts_col[i][:, a : a + 1], None, ALU.mult)
-
-        def turn_back(i, m, first_tile=0, half="lower"):
+        def turn_back(i, m, half="lower"):
             turned = bank("turned", half)
             for a in reversed(range(BLOCKS)):
-                nc.tensor.transpose(turned[:, a * P : (a + 1) * P], blocks[i, a][:, (m - first_tile) * P : (m - first_tile + 1) * P], ident[:])
+                nc.tensor.transpose(turned[:, a * P : (a + 1) * P], blocks[i, a][:, m * P : (m + 1) * P], ident[:])
             return turned
 
         nc.vector.memset(tab_s[:], 0)
         identity()
         nc.gpsimd.memset(w4_s[:], 0)
         nc.gpsimd.memset(b_rows[:], 0.0)
+        nc.gpsimd.memset(planes[:], 0)
         nc.scalar.activation(warm[:], ones[:, 0:1], ACT.Silu, bias=ones[:, 1:2])
-        nc.sync.dma_start(ts_cols[:], ts[0].rearrange("(p a) -> p a", p=P))
         nc.sync.dma_start(offsets[:], offs)
+        nc.sync.dma_start(ts_cols[:], ts[0].rearrange("(p a) -> p a", p=P))
         nc.sync.dma_start(w4_w[:], w4_words[0].bitcast(I32))
-        load_planes(nc.sync, tab_s, tab_scales[0])
+        nc.sync.dma_start(tab_s[0:P:8, :], tab_scales[0].bitcast(I32))
+        load_words()
         load_rows(u_raw, u)
         load_c(0)
-        nc.sync.dma_start(b_rows[0:N_TILES, :], b.rearrange("(m p) -> m p", p=P))
-        load_words()
-        load_planes(nc.sync, w4_s, w4_scales[0])
-        ts_window()
-        first = kept([P, M + CHUNK, PACK], BF16, "first")
-        round_on_gpsimd(first[:, 0:M, :], u_raw[:])
-        pick_scales(0, 4)
+        load_planes(nc.gpsimd, w4_s, w4_scales[0])
+        nc.gpsimd.dma_start(b_rows[0:N_TILES, :], b.rearrange("(m p) -> m p", p=P))
         load_c(1)
         load_c(2)
         load_c(3)
-        pick_ts(0, 2)
-        round_rows(nc.scalar.copy, first[:, M : M + SHARE, :], c_raw[0][:, :, 0:SHARE])
-        round_on_gpsimd(first[:, M + SHARE : M + CHUNK, :], c_raw[0][:, :, SHARE:CHUNK])
-        ts_to_partitions(0)
-        turn_bias()
-        quantize(("u", 0), first)
-        open_sums(turned_dense_pass, 0, half="lower")
-        pick_ts(2, wide=True)
+        ts_window()
+        pick_scales()
+        place_scales(nc.scalar)
         pick_words(0)
-        close_sums(turned_table_pass, 0)
+        pick_words(1)
+        pick_ts(0)
+        round_piece("scalar", "u", u_raw, 0, HALF)
+        round_piece("gpsimd", "u", u_raw, HALF, M)
+        quantize("u", 0)
+        quantize("u", HALF)
+        turn_bias()
+        pick_ts(1)
+        round_piece("scalar", 0, c_raw[0], 0, HALF)
+        round_piece("gpsimd", 0, c_raw[0], HALF, CHUNK)
+        ts_to_partitions(0)
+        open_sums(turned_table_pass, 0, half="lower")
+        quantize(0, 0)
+        quantize(0, HALF)
+        close_sums(turned_dense_pass, 0)
         for a in range(BLOCKS):
             scale_turned(0, a, sums[0, a])
-        pick_ts(3)
-        pick_words(1)
-        open_sums(table_pass, 1)
-        second = kept([P, CHUNK, PACK], BF16, "second", "handed")
-        round_on_gpsimd(second[:, CUT:CHUNK, :], c_raw[1][:, :, CUT:CHUNK])
+        open_sums(table_pass, 1, half="lower")
+        round_piece("gpsimd", 1, c_raw[1], 0, CHUNK)
         pick_words(2)
-        round_rows(nc.vector.tensor_copy, second[:, 0:CUT, :], c_raw[1][:, :, 0:CUT])
-        quantize((1,), second)
-        right = kept([P, HALF, PACK], BF16, "right", "handed")
-        round_on_gpsimd(right[:], c_raw[2][:, :, HALF:CHUNK])
-        left = by_scalar([P, HALF, PACK], BF16, "left")
-        round_rows(nc.scalar.copy, left[:], c_raw[2][:, :, 0:HALF])
+        pick_ts(2)
+        pick_ts(3)
+        quantize(1, 0)
+        round_piece("scalar", 2, c_raw[2], 0, HALF)
+        round_piece("gpsimd", 2, c_raw[2], HALF, CHUNK)
         for m in range(N_TILES):
-            finish(0, m, turn_back(0, m)[:])
+            finish(0, m, turn_back(0, m, "upper")[:])
         close_sums(dense_pass, 1)
-        open_sums(table_pass, 2, half="lower")
+        open_sums(table_pass, 2)
         pick_words(3)
         products = [scale_direct(1, 0, sums[1, 0])]
-        quantize_part(2, left, 0, HALF)
-        quantize_part(2, right, HALF, CHUNK)
-        fourth = kept([P, CHUNK, PACK], BF16, "fourth", "handed")
-        round_on_gpsimd(fourth[:, EDGE:CHUNK, :], c_raw[3][:, :, EDGE:CHUNK])
+        quantize(2, 0)
+        quantize(2, HALF)
+        round_piece("gpsimd", 3, c_raw[3], 0, CHUNK)
         products.extend(scale_direct(1, m, sums[1, m]) for m in range(1, N_TILES))
-        finish(1, 0, products[0][:])
-        round_rows(nc.scalar.copy, fourth[:, 0:EDGE, :], c_raw[3][:, :, 0:EDGE])
-        for m in range(1, N_TILES):
+        for m in range(N_TILES):
             finish(1, m, products[m][:])
         close_sums(dense_pass, 2)
-        open_sums(table_pass, 3)
+        open_sums(table_pass, 3, half="lower")
         for m in range(0, 2):
             finish(2, m, scale_direct(2, m, sums[2, m])[:])
-        quantize((3,), fourth)
+        quantize(3, 0)
         close_sums(dense_pass, 3)
         for m in range(2, 4):
             finish(2, m, scale_direct(2, m, sums[2, m])[:])
         for m in range(N_TILES):
-            for lo, hi in ((0, CHUNK),) if m < N_TILES - 1 else ((0, 256), (256, 512)):
+            for lo, hi in ((0, CHUNK),) if m < N_TILES - 1 else ((0, HALF), (HALF, CHUNK)):
                 finish(3, m, scale_direct(3, m, sums[3, m], lo, hi)[:], lo, hi)

@@ -62,7 +62,6 @@ def tile_list_tabts_silu_kernel(tc, tab_words, tab_scales, w4_words, w4_scales, 
         tab_w = kept([P, T], I32, "tab_w")
         u_raw = kept([P, PACK, M], F32, "u_raw")
         c_raw = [kept([P, PACK, CHUNK], F32, "c_raw%d" % i) for i in range(N_CHUNKS)]
-        planes = kept([P, S // 4], I32, "planes", "ramp")
         w4_bytes = w4_w[:].bitcast(U8)
         w4_plane = w4_s[:].bitcast(U8)
         codes, pieces, words, picked_s, picked_t, ts_col, blocks, small, sums = {}, {}, {}, {}, {}, {}, {}, {}, {}
@@ -105,12 +104,8 @@ def tile_list_tabts_silu_kernel(tc, tab_words, tab_scales, w4_words, w4_scales, 
         def pick_scales():
             small["rows"] = by_vector([P, S], U8, "rows")
             nc.vector.tensor_copy(small["rows"][:], tab_s[:].bitcast(U8).indirect(offsets[:]))
-
-        def place_scales(queue):
-            for r in range(4):
-                queue.dma_start(planes[r:P:32, :], small["rows"][8 * r : P : 32, :].bitcast(I32))
             for i in range(N_CHUNKS):
-                picked_s[i] = planes[:].bitcast(U8)[:, i * CHUNK : (i + 1) * CHUNK]
+                picked_s[i] = small["rows"][:, i * CHUNK : (i + 1) * CHUNK]
 
         def pick_words(i):
             words[i] = by_vector([P, CHUNK], U32, "words%d" % i)
@@ -217,23 +212,21 @@ def tile_list_tabts_silu_kernel(tc, tab_words, tab_scales, w4_words, w4_scales, 
         identity()
         nc.gpsimd.memset(w4_s[:], 0)
         nc.gpsimd.memset(b_rows[:], 0.0)
-        nc.gpsimd.memset(planes[:], 0)
         nc.scalar.activation(warm[:], ones[:, 0:1], ACT.Silu, bias=ones[:, 1:2])
         nc.sync.dma_start(offsets[:], offs)
         nc.sync.dma_start(ts_cols[:], ts[0].rearrange("(p a) -> p a", p=P))
         nc.sync.dma_start(w4_w[:], w4_words[0].bitcast(I32))
-        nc.sync.dma_start(tab_s[0:P:8, :], tab_scales[0].bitcast(I32))
+        load_planes(nc.sync, tab_s, tab_scales[0])
         load_words()
+        nc.sync.dma_start(b_rows[0:N_TILES, :], b.rearrange("(m p) -> m p", p=P))
         load_rows(u_raw, u)
         load_c(0)
-        load_planes(nc.gpsimd, w4_s, w4_scales[0])
-        nc.gpsimd.dma_start(b_rows[0:N_TILES, :], b.rearrange("(m p) -> m p", p=P))
+        load_planes(nc.sync, w4_s, w4_scales[0])
         load_c(1)
         load_c(2)
         load_c(3)
         ts_window()
         pick_scales()
-        place_scales(nc.scalar)
         pick_words(0)
         pick_words(1)
         pick_ts(0)

@@ -24,8 +24,8 @@ N_TILES = M // P
 BLOCKS = CHUNK // P
 HALF = CHUNK // 2
 TS_PER_PARTITION = T // P
-VECTOR_TILES = 30
-SCALAR_TILES = 26
+VECTOR_TILES = 36
+SCALAR_TILES = 28
 
 
 def tile_list_tabts_silu_kernel(tc, tab_words, tab_scales, w4_words, w4_scales, c, u, ts, b, offs, out):
@@ -126,18 +126,19 @@ def tile_list_tabts_silu_kernel(tc, tab_words, tab_scales, w4_words, w4_scales, 
                 piece = kept([P, hi - lo, PACK], BF16, "piece", "handed")
                 round_on_gpsimd(piece[:], raw[:, :, lo:hi])
             elif engine == "scalar":
-                piece = by_scalar([P, hi - lo, PACK], BF16, "piece")
+                piece = by_scalar([P, hi - lo, PACK], BF16, "piece") if hi - lo <= HALF else kept([P, hi - lo, PACK], BF16, "whole_%s" % key)
                 round_rows(nc.scalar.copy, piece[:], raw[:, :, lo:hi])
             else:
                 piece = by_vector([P, hi - lo, PACK], BF16, "piece")
                 round_rows(nc.vector.tensor_copy, piece[:], raw[:, :, lo:hi])
             pieces[key, lo] = (piece, hi)
 
-        def quantize(key, lo):
-            piece, hi = pieces[key, lo]
+        def quantize(key, lo, hi):
+            at = max(first for name, first in pieces if name == key and first <= lo)
+            piece = pieces[key, at][0][:, lo - at : hi - at, :]
             made = by_vector([P, hi - lo], U32, "codes_%s" % key)
             plane = kept([P, hi - lo], U8, "scales_%s_%d" % (key, lo))
-            nc.vector.quantize_mx(out=made[:].bitcast(FP8X4), scales=plane[:], in_=piece[:].rearrange("p w i -> p (w i)"))
+            nc.vector.quantize_mx(out=made[:].bitcast(FP8X4), scales=plane[:], in_=piece.rearrange("p w i -> p (w i)"))
             codes.setdefault(key, []).append((lo, hi, made, plane))
 
         def stationary(key, at):
@@ -217,62 +218,72 @@ def tile_list_tabts_silu_kernel(tc, tab_words, tab_scales, w4_words, w4_scales, 
         nc.sync.dma_start(ts_cols[:], ts[0].rearrange("(p a) -> p a", p=P))
         nc.sync.dma_start(w4_w[:], w4_words[0].bitcast(I32))
         load_planes(nc.sync, tab_s, tab_scales[0])
-        load_words()
-        nc.sync.dma_start(b_rows[0:N_TILES, :], b.rearrange("(m p) -> m p", p=P))
         load_rows(u_raw, u)
         load_c(0)
+        nc.sync.dma_start(b_rows[0:N_TILES, :], b.rearrange("(m p) -> m p", p=P))
+        load_words()
         load_planes(nc.sync, w4_s, w4_scales[0])
         load_c(1)
         load_c(2)
         load_c(3)
         ts_window()
         pick_scales()
-        pick_words(0)
-        pick_words(1)
+        products = {}
+        round_piece("gpsimd", "u", u_raw, 0, 512)
+        quantize("u", 0, 512)
+        round_piece("scalar", 0, c_raw[0], 0, 512)
         pick_ts(0)
-        round_piece("scalar", "u", u_raw, 0, HALF)
-        round_piece("gpsimd", "u", u_raw, HALF, M)
-        quantize("u", 0)
-        quantize("u", HALF)
-        turn_bias()
         pick_ts(1)
-        round_piece("scalar", 0, c_raw[0], 0, HALF)
-        round_piece("gpsimd", 0, c_raw[0], HALF, CHUNK)
+        turn_bias()
         ts_to_partitions(0)
-        open_sums(turned_table_pass, 0, half="lower")
-        quantize(0, 0)
-        quantize(0, HALF)
-        close_sums(turned_dense_pass, 0)
+        quantize(0, 0, 512)
+        open_sums(turned_dense_pass, 0, range(2), half="lower")
+        round_piece("gpsimd", 1, c_raw[1], 0, 512)
+        pick_words(0)
+        close_sums(turned_table_pass, 0, range(2))
+        for a in range(2, BLOCKS):
+            open_sums(turned_table_pass, 0, (a,), half="lower")
+            close_sums(turned_dense_pass, 0, (a,))
         for a in range(BLOCKS):
             scale_turned(0, a, sums[0, a])
+        pick_words(1)
         open_sums(table_pass, 1, half="lower")
-        round_piece("gpsimd", 1, c_raw[1], 0, CHUNK)
-        pick_words(2)
         pick_ts(2)
+        pick_words(2)
         pick_ts(3)
-        quantize(1, 0)
-        round_piece("scalar", 2, c_raw[2], 0, HALF)
-        round_piece("gpsimd", 2, c_raw[2], HALF, CHUNK)
+        quantize(1, 0, 512)
+        round_piece("scalar", 2, c_raw[2], 0, 256)
+        round_piece("gpsimd", 2, c_raw[2], 256, 512)
         for m in range(N_TILES):
             finish(0, m, turn_back(0, m, "upper")[:])
         close_sums(dense_pass, 1)
         open_sums(table_pass, 2)
         pick_words(3)
-        products = [scale_direct(1, 0, sums[1, 0])]
-        quantize(2, 0)
-        quantize(2, HALF)
-        round_piece("gpsimd", 3, c_raw[3], 0, CHUNK)
-        products.extend(scale_direct(1, m, sums[1, m]) for m in range(1, N_TILES))
-        for m in range(N_TILES):
-            finish(1, m, products[m][:])
+        products[1, 0] = scale_direct(1, 0, sums[1, 0])
+        finish(1, 0, products[1, 0][:])
+        quantize(2, 0, 256)
+        quantize(2, 256, 512)
+        round_piece("gpsimd", 3, c_raw[3], 256, 512)
         close_sums(dense_pass, 2)
+        products[1, 1] = scale_direct(1, 1, sums[1, 1])
+        round_piece("scalar", 3, c_raw[3], 0, 256)
+        finish(1, 1, products[1, 1][:])
+        products[1, 2] = scale_direct(1, 2, sums[1, 2])
+        finish(1, 2, products[1, 2][:])
+        products[1, 3] = scale_direct(1, 3, sums[1, 3])
+        finish(1, 3, products[1, 3][:])
         open_sums(table_pass, 3, half="lower")
-        for m in range(0, 2):
-            finish(2, m, scale_direct(2, m, sums[2, m])[:])
-        quantize(3, 0)
+        products[2, 0] = scale_direct(2, 0, sums[2, 0])
+        finish(2, 0, products[2, 0][:])
+        products[2, 1] = scale_direct(2, 1, sums[2, 1])
+        finish(2, 1, products[2, 1][:])
+        quantize(3, 0, 256)
+        quantize(3, 256, 512)
         close_sums(dense_pass, 3)
-        for m in range(2, 4):
-            finish(2, m, scale_direct(2, m, sums[2, m])[:])
+        products[2, 2] = scale_direct(2, 2, sums[2, 2])
+        finish(2, 2, products[2, 2][:])
+        products[2, 3] = scale_direct(2, 3, sums[2, 3])
+        finish(2, 3, products[2, 3][:])
         for m in range(N_TILES):
             for lo, hi in ((0, CHUNK),) if m < N_TILES - 1 else ((0, HALF), (HALF, CHUNK)):
                 finish(3, m, scale_direct(3, m, sums[3, m], lo, hi)[:], lo, hi)

@@ -24,8 +24,8 @@ N_TILES = M // P
 BLOCKS = CHUNK // P
 HALF = CHUNK // 2
 TS_PER_PARTITION = T // P
-VECTOR_TILES = 36
-SCALAR_TILES = 28
+VECTOR_TILES = 24
+SCALAR_TILES = 14
 
 
 def tile_list_tabts_silu_kernel(tc, tab_words, tab_scales, w4_words, w4_scales, c, u, ts, b, offs, out):
@@ -98,8 +98,8 @@ def tile_list_tabts_silu_kernel(tc, tab_words, tab_scales, w4_words, w4_scales, 
                     turned[:].rearrange("q (a p) -> q p a", p=P),
                 )
 
-        def listed(i):
-            return offsets[:, i * (CHUNK // 16) : (i + 1) * (CHUNK // 16)]
+        def listed(i, n=1):
+            return offsets[:, i * (CHUNK // 16) : (i + n) * (CHUNK // 16)]
 
         def pick_scales():
             small["rows"] = by_vector([P, S], U8, "rows")
@@ -107,13 +107,16 @@ def tile_list_tabts_silu_kernel(tc, tab_words, tab_scales, w4_words, w4_scales, 
             for i in range(N_CHUNKS):
                 picked_s[i] = small["rows"][:, i * CHUNK : (i + 1) * CHUNK]
 
-        def pick_words(i):
-            words[i] = by_vector([P, CHUNK], U32, "words%d" % i)
-            nc.vector.tensor_copy(words[i][:], tab_w[:].bitcast(U32).indirect(listed(i)))
+        def pick_words(i, n=1):
+            picked = by_vector([P, n * CHUNK], U32, "words%d" % i)
+            nc.vector.tensor_copy(picked[:], tab_w[:].bitcast(U32).indirect(listed(i, n)))
+            for k in range(n):
+                words[i + k] = picked[:, k * CHUNK : (k + 1) * CHUNK]
 
         def pick_ts(i):
-            picked_t[i] = by_vector([P, CHUNK], F32, "picked%d" % i)
-            nc.vector.tensor_copy(picked_t[i][:], ts_all[:].indirect(listed(i)))
+            picked = by_vector([P, 2 * CHUNK], F32, "picked%d" % i)
+            nc.vector.tensor_copy(picked[:], ts_all[:].indirect(listed(i, 2)))
+            picked_t[i], picked_t[i + 1] = picked[:, 0:CHUNK], picked[:, CHUNK : 2 * CHUNK]
 
         def round_on_gpsimd(dst, raw):
             nc.gpsimd.tensor_scalar(dst.rearrange("p (g e) i -> p g i e", e=4), raw.rearrange("p i (g e) -> p g i e", e=4), 1.0, 0.0, ALU.mult, ALU.add)
@@ -233,7 +236,6 @@ def tile_list_tabts_silu_kernel(tc, tab_words, tab_scales, w4_words, w4_scales, 
         quantize("u", 0, 512)
         round_piece("scalar", 0, c_raw[0], 0, 512)
         pick_ts(0)
-        pick_ts(1)
         turn_bias()
         ts_to_partitions(0)
         quantize(0, 0, 512)
@@ -246,11 +248,9 @@ def tile_list_tabts_silu_kernel(tc, tab_words, tab_scales, w4_words, w4_scales, 
             close_sums(turned_dense_pass, 0, (a,))
         for a in range(BLOCKS):
             scale_turned(0, a, sums[0, a])
-        pick_words(1)
+        pick_words(1, 2)
         open_sums(table_pass, 1, half="lower")
         pick_ts(2)
-        pick_words(2)
-        pick_ts(3)
         quantize(1, 0, 512)
         round_piece("scalar", 2, c_raw[2], 0, 256)
         round_piece("gpsimd", 2, c_raw[2], 256, 512)
@@ -263,10 +263,12 @@ def tile_list_tabts_silu_kernel(tc, tab_words, tab_scales, w4_words, w4_scales, 
         finish(1, 0, products[1, 0][:])
         quantize(2, 0, 256)
         quantize(2, 256, 512)
-        round_piece("gpsimd", 3, c_raw[3], 256, 512)
+        fourth = kept([P, CHUNK, PACK], BF16, "fourth", "handed")
+        pieces[3, 0] = (fourth, CHUNK)
+        round_on_gpsimd(fourth[:, 128:CHUNK, :], c_raw[3][:, :, 128:CHUNK])
         close_sums(dense_pass, 2)
         products[1, 1] = scale_direct(1, 1, sums[1, 1])
-        round_piece("scalar", 3, c_raw[3], 0, 256)
+        round_rows(nc.scalar.copy, fourth[:, 0:128, :], c_raw[3][:, :, 0:128])
         finish(1, 1, products[1, 1][:])
         products[1, 2] = scale_direct(1, 2, sums[1, 2])
         finish(1, 2, products[1, 2][:])
@@ -277,8 +279,7 @@ def tile_list_tabts_silu_kernel(tc, tab_words, tab_scales, w4_words, w4_scales, 
         finish(2, 0, products[2, 0][:])
         products[2, 1] = scale_direct(2, 1, sums[2, 1])
         finish(2, 1, products[2, 1][:])
-        quantize(3, 0, 256)
-        quantize(3, 256, 512)
+        quantize(3, 0, 512)
         close_sums(dense_pass, 3)
         products[2, 2] = scale_direct(2, 2, sums[2, 2])
         finish(2, 2, products[2, 2][:])

@@ -48,6 +48,7 @@ def tile_list_tabts_silu_kernel(tc, tab_words, tab_scales, w4_words, w4_scales, 
 
         offsets = kept([P, S // 16], U16, "offsets")
         tab_s = kept([P, T // 4], I32, "tab_s")
+        plane_s = kept([P, S // 4], I32, "plane_s")
         ts_cols = kept([P, TS_PER_PARTITION], F32, "ts_cols")
         ts_all = kept([P, T], F32, "ts_all")
         b_rows = kept([P, P], F32, "b_rows")
@@ -104,8 +105,10 @@ def tile_list_tabts_silu_kernel(tc, tab_words, tab_scales, w4_words, w4_scales, 
         def pick_scales():
             small["rows"] = by_vector([P, S], U8, "rows")
             nc.vector.tensor_copy(small["rows"][:], tab_s[:].bitcast(U8).indirect(offsets[:]))
+            for r in range(4):
+                nc.sync.dma_start(plane_s[r:P:32, :], small["rows"][8 * r : P : 32, :].bitcast(I32))
             for i in range(N_CHUNKS):
-                picked_s[i] = small["rows"][:, i * CHUNK : (i + 1) * CHUNK]
+                picked_s[i] = plane_s[:].bitcast(U8)[:, i * CHUNK : (i + 1) * CHUNK]
 
         def pick_words(i, n=1):
             picked = by_vector([P, n * CHUNK], U32, "words%d" % i)
@@ -214,23 +217,24 @@ def tile_list_tabts_silu_kernel(tc, tab_words, tab_scales, w4_words, w4_scales, 
 
         nc.vector.memset(tab_s[:], 0)
         identity()
+        nc.vector.memset(plane_s[:], 0)
         nc.gpsimd.memset(w4_s[:], 0)
         nc.gpsimd.memset(b_rows[:], 0.0)
         nc.scalar.activation(warm[:], ones[:, 0:1], ACT.Silu, bias=ones[:, 1:2])
         nc.sync.dma_start(offsets[:], offs)
         nc.sync.dma_start(ts_cols[:], ts[0].rearrange("(p a) -> p a", p=P))
         nc.sync.dma_start(w4_w[:], w4_words[0].bitcast(I32))
-        load_planes(nc.sync, tab_s, tab_scales[0])
+        nc.sync.dma_start(tab_s[0:P:8, :], tab_scales[0].bitcast(I32))
         load_rows(u_raw, u)
         load_c(0)
         nc.sync.dma_start(b_rows[0:N_TILES, :], b.rearrange("(m p) -> m p", p=P))
-        load_words()
         load_planes(nc.sync, w4_s, w4_scales[0])
+        load_words()
+        pick_scales()
         load_c(1)
         load_c(2)
         load_c(3)
         ts_window()
-        pick_scales()
         products = {}
         round_piece("gpsimd", "u", u_raw, 0, 512)
         quantize("u", 0, 512)

@@ -32,19 +32,19 @@ def tile_list_tabts_silu_kernel(tc, tab_words, tab_scales, w4_words, w4_scales, 
     nc = tc.nc
     with ExitStack() as ctx:
         keep = ctx.enter_context(tc.tile_pool(name="keep", bufs=1))
-        banks = ctx.enter_context(tc.psum_pool(name="banks", bufs=4))
+        banks = ctx.enter_context(tc.psum_pool(name="banks", bufs=8))
 
         def kept(shape, dtype, name, tag=None):
-            return keep.tile(shape, dtype, name=name, tag=tag or name, align_bytes=64)
+            return keep.tile(shape, dtype, name=name, tag=tag or name, align_bytes=512)
 
         def by_vector(shape, dtype, name):
-            return keep.tile(shape, dtype, name=name, tag="by_vector", bufs=VECTOR_TILES, align_bytes=64)
+            return keep.tile(shape, dtype, name=name, tag="by_vector", bufs=VECTOR_TILES, align_bytes=512)
 
         def by_scalar(shape, dtype, name):
-            return keep.tile(shape, dtype, name=name, tag="by_scalar", bufs=SCALAR_TILES, align_bytes=64)
+            return keep.tile(shape, dtype, name=name, tag="by_scalar", bufs=SCALAR_TILES, align_bytes=512)
 
         def bank(name, half="upper"):
-            return banks.tile([P, CHUNK], F32, name=name, tag=half)
+            return banks.tile([P, CHUNK], F32, name=name, tag="ring")
 
         offsets = kept([P, S // 16], U16, "offsets")
         tab_s = kept([P, T // 4], I32, "tab_s")
@@ -62,7 +62,8 @@ def tile_list_tabts_silu_kernel(tc, tab_words, tab_scales, w4_words, w4_scales, 
         w4_s = kept([P, M // 4], I32, "w4_s")
         tab_w = kept([P, T], I32, "tab_w")
         u_raw = kept([P, PACK, M], F32, "u_raw")
-        c_raw = [kept([P, PACK, CHUNK], F32, "c_raw%d" % i) for i in range(N_CHUNKS)]
+        c_raw = [kept([P, PACK, CHUNK], F32, "c_raw%d" % i) if i != 1 else None for i in range(N_CHUNKS)]
+        c_pair = [kept([P, PACK, HALF], F32, "c_pair%d" % k) for k in range(2)]
         w4_bytes = w4_w[:].bitcast(U8)
         w4_plane = w4_s[:].bitcast(U8)
         codes, pieces, words, picked_s, picked_t, ts_col, blocks, small, sums = {}, {}, {}, {}, {}, {}, {}, {}, {}
@@ -102,11 +103,14 @@ def tile_list_tabts_silu_kernel(tc, tab_words, tab_scales, w4_words, w4_scales, 
         def listed(i, n=1):
             return offsets[:, i * (CHUNK // 16) : (i + n) * (CHUNK // 16)]
 
+        def move_scales(lo, hi):
+            for r in range(4):
+                nc.sync.dma_start(plane_s[r:P:32, lo // 4 : hi // 4], small["rows"][8 * r : P : 32, lo:hi].bitcast(I32))
+
         def pick_scales():
             small["rows"] = by_vector([P, S], U8, "rows")
             nc.vector.tensor_copy(small["rows"][:], tab_s[:].bitcast(U8).indirect(offsets[:]))
-            for r in range(4):
-                nc.sync.dma_start(plane_s[r:P:32, :], small["rows"][8 * r : P : 32, :].bitcast(I32))
+            move_scales(0, S)
             for i in range(N_CHUNKS):
                 picked_s[i] = plane_s[:].bitcast(U8)[:, i * CHUNK : (i + 1) * CHUNK]
 
@@ -222,16 +226,18 @@ def tile_list_tabts_silu_kernel(tc, tab_words, tab_scales, w4_words, w4_scales, 
         nc.gpsimd.memset(b_rows[:], 0.0)
         nc.scalar.activation(warm[:], ones[:, 0:1], ACT.Silu, bias=ones[:, 1:2])
         nc.sync.dma_start(offsets[:], offs)
-        nc.sync.dma_start(ts_cols[:], ts[0].rearrange("(p a) -> p a", p=P))
-        nc.sync.dma_start(w4_w[:], w4_words[0].bitcast(I32))
+        for half in range(2):
+            nc.sync.dma_start(ts_cols[64 * half : 64 * (half + 1), :], ts[0].rearrange("(p a) -> p a", p=P)[64 * half : 64 * (half + 1), :])
         nc.sync.dma_start(tab_s[0:P:8, :], tab_scales[0].bitcast(I32))
         load_rows(u_raw, u)
         load_c(0)
-        nc.sync.dma_start(b_rows[0:N_TILES, :], b.rearrange("(m p) -> m p", p=P))
         load_planes(nc.sync, w4_s, w4_scales[0])
         load_words()
+        nc.sync.dma_start(w4_w[:], w4_words[0].bitcast(I32))
         pick_scales()
-        load_c(1)
+        for k in range(2):
+            load_rows(c_pair[k], c[:, CHUNK + k * HALF : CHUNK + (k + 1) * HALF])
+        nc.sync.dma_start(b_rows[0:N_TILES, :], b.rearrange("(m p) -> m p", p=P))
         load_c(2)
         load_c(3)
         ts_window()
@@ -240,11 +246,13 @@ def tile_list_tabts_silu_kernel(tc, tab_words, tab_scales, w4_words, w4_scales, 
         quantize("u", 0, 512)
         round_piece("scalar", 0, c_raw[0], 0, 512)
         pick_ts(0)
-        turn_bias()
         ts_to_partitions(0)
         quantize(0, 0, 512)
         open_sums(turned_dense_pass, 0, range(2), half="lower")
-        round_piece("gpsimd", 1, c_raw[1], 0, 512)
+        second = kept([P, CHUNK, PACK], BF16, "second", "handed")
+        pieces[1, 0] = (second, CHUNK)
+        for k in range(2):
+            round_on_gpsimd(second[:, k * HALF : (k + 1) * HALF, :], c_pair[k][:])
         pick_words(0)
         close_sums(turned_table_pass, 0, range(2))
         for a in range(2, BLOCKS):
@@ -254,6 +262,7 @@ def tile_list_tabts_silu_kernel(tc, tab_words, tab_scales, w4_words, w4_scales, 
             scale_turned(0, a, sums[0, a])
         pick_words(1, 2)
         open_sums(table_pass, 1, half="lower")
+        turn_bias()
         pick_ts(2)
         quantize(1, 0, 512)
         round_piece("scalar", 2, c_raw[2], 0, 256)

@@ -17,13 +17,18 @@ ACT = mybir.ActivationFunctionType
 ALU = mybir.AluOpType
 
 P = 128
+QUADRANT = 32
 PACK = 4
+GROUP = 16
+SPREAD = P // GROUP
 CHUNK = 512
 N_CHUNKS = S // CHUNK
 N_TILES = M // P
 BLOCKS = CHUNK // P
 HALF = CHUNK // 2
 TS_PER_PARTITION = T // P
+BANKS = 8
+ALIGN = 512
 VECTOR_TILES = 24
 SCALAR_TILES = 14
 
@@ -32,21 +37,24 @@ def tile_list_tabts_silu_kernel(tc, tab_words, tab_scales, w4_words, w4_scales, 
     nc = tc.nc
     with ExitStack() as ctx:
         keep = ctx.enter_context(tc.tile_pool(name="keep", bufs=1))
-        banks = ctx.enter_context(tc.psum_pool(name="banks", bufs=8))
+        banks = ctx.enter_context(tc.psum_pool(name="banks", bufs=BANKS))
 
         def kept(shape, dtype, name, tag=None):
-            return keep.tile(shape, dtype, name=name, tag=tag or name, align_bytes=512)
+            return keep.tile(shape, dtype, name=name, tag=tag or name, align_bytes=ALIGN)
 
         def by_vector(shape, dtype, name):
-            return keep.tile(shape, dtype, name=name, tag="by_vector", bufs=VECTOR_TILES, align_bytes=512)
+            return keep.tile(shape, dtype, name=name, tag="by_vector", bufs=VECTOR_TILES, align_bytes=ALIGN)
 
         def by_scalar(shape, dtype, name):
-            return keep.tile(shape, dtype, name=name, tag="by_scalar", bufs=SCALAR_TILES, align_bytes=512)
+            return keep.tile(shape, dtype, name=name, tag="by_scalar", bufs=SCALAR_TILES, align_bytes=ALIGN)
 
-        def bank(name, half="upper"):
+        def bank(name):
             return banks.tile([P, CHUNK], F32, name=name, tag="ring")
 
-        offsets = kept([P, S // 16], U16, "offsets")
+        def handed(width, name):
+            return kept([P, width, PACK], BF16, name, "handed")
+
+        offsets = kept([P, S // GROUP], U16, "offsets")
         tab_s = kept([P, T // 4], I32, "tab_s")
         plane_s = kept([P, S // 4], I32, "plane_s")
         ts_cols = kept([P, TS_PER_PARTITION], F32, "ts_cols")
@@ -54,7 +62,7 @@ def tile_list_tabts_silu_kernel(tc, tab_words, tab_scales, w4_words, w4_scales, 
         b_rows = kept([P, P], F32, "b_rows")
         ones = kept([P, P], F32, "ones")
         ramp = kept([P, P], F32, "ramp")
-        lane = kept([P, 32], F32, "lane")
+        lane = kept([P, QUADRANT], F32, "lane")
         quadrant = kept([P, 1], F32, "quadrant")
         ident = kept([P, P], F32, "ident")
         warm = kept([P, 1], F32, "warm")
@@ -62,18 +70,18 @@ def tile_list_tabts_silu_kernel(tc, tab_words, tab_scales, w4_words, w4_scales, 
         w4_s = kept([P, M // 4], I32, "w4_s")
         tab_w = kept([P, T], I32, "tab_w")
         u_raw = kept([P, PACK, M], F32, "u_raw")
-        c_raw = [kept([P, PACK, CHUNK], F32, "c_raw%d" % i) if i != 1 else None for i in range(N_CHUNKS)]
+        c_raw = {i: kept([P, PACK, CHUNK], F32, "c_raw%d" % i) for i in (0, 2, 3)}
         c_pair = [kept([P, PACK, HALF], F32, "c_pair%d" % k) for k in range(2)]
         w4_bytes = w4_w[:].bitcast(U8)
         w4_plane = w4_s[:].bitcast(U8)
-        codes, pieces, words, picked_s, picked_t, ts_col, blocks, small, sums = {}, {}, {}, {}, {}, {}, {}, {}, {}
+        codes, pieces, words, picked_t, ts_col, blocks, sums = {}, {}, {}, {}, {}, {}, {}
 
         def identity():
             nc.gpsimd.memset(ones[:], 1.0)
-            for q in range(4):
-                nc.gpsimd.memset(quadrant[32 * q : 32 * (q + 1), :], 32.0 * q)
+            for q in range(P // QUADRANT):
+                nc.gpsimd.memset(quadrant[QUADRANT * q : QUADRANT * (q + 1), :], float(QUADRANT * q))
             nc.vector.tensor_tensor_scan(ramp[:], ones[:], ones[:], 0.0, ALU.mult, ALU.add)
-            nc.vector.transpose(lane[:], ramp[:, 0:32])
+            nc.vector.transpose(lane[:], ramp[:, 0:QUADRANT])
             nc.vector.tensor_scalar(ident[:], ramp[:], lane[:, 0:1], quadrant[:], ALU.subtract, ALU.is_equal)
 
         def load_rows(dst, src):
@@ -81,13 +89,6 @@ def tile_list_tabts_silu_kernel(tc, tab_words, tab_scales, w4_words, w4_scales, 
 
         def load_c(i):
             load_rows(c_raw[i], c[:, i * CHUNK : (i + 1) * CHUNK])
-
-        def load_planes(queue, plane, rows):
-            for r in range(4):
-                queue.dma_start(plane[r:P:32, :], rows[r:16:4, :].bitcast(I32))
-
-        def load_words():
-            nc.sync.dma_start(tab_w[:], tab_words[0].rearrange("p t i -> p (t i)").bitcast(I32))
 
         def ts_window():
             for g in range(T // CHUNK):
@@ -101,18 +102,16 @@ def tile_list_tabts_silu_kernel(tc, tab_words, tab_scales, w4_words, w4_scales, 
                 )
 
         def listed(i, n=1):
-            return offsets[:, i * (CHUNK // 16) : (i + n) * (CHUNK // 16)]
-
-        def move_scales(lo, hi):
-            for r in range(4):
-                nc.sync.dma_start(plane_s[r:P:32, lo // 4 : hi // 4], small["rows"][8 * r : P : 32, lo:hi].bitcast(I32))
+            return offsets[:, i * (CHUNK // GROUP) : (i + n) * (CHUNK // GROUP)]
 
         def pick_scales():
-            small["rows"] = by_vector([P, S], U8, "rows")
-            nc.vector.tensor_copy(small["rows"][:], tab_s[:].bitcast(U8).indirect(offsets[:]))
-            move_scales(0, S)
-            for i in range(N_CHUNKS):
-                picked_s[i] = plane_s[:].bitcast(U8)[:, i * CHUNK : (i + 1) * CHUNK]
+            rows = by_vector([P, S], U8, "rows")
+            nc.vector.tensor_copy(rows[:], tab_s[:].bitcast(U8).indirect(offsets[:]))
+            for r in range(PACK):
+                nc.sync.dma_start(plane_s[r:P:QUADRANT, :], rows[SPREAD * r : P : QUADRANT, :].bitcast(I32))
+
+        def picked_s(i):
+            return plane_s[:].bitcast(U8)[:, i * CHUNK : (i + 1) * CHUNK]
 
         def pick_words(i, n=1):
             picked = by_vector([P, n * CHUNK], U32, "words%d" % i)
@@ -128,32 +127,18 @@ def tile_list_tabts_silu_kernel(tc, tab_words, tab_scales, w4_words, w4_scales, 
         def round_on_gpsimd(dst, raw):
             nc.gpsimd.tensor_scalar(dst.rearrange("p (g e) i -> p g i e", e=4), raw.rearrange("p i (g e) -> p g i e", e=4), 1.0, 0.0, ALU.mult, ALU.add)
 
-        def round_rows(copy, dst, raw):
-            copy(dst.rearrange("p (g e) i -> p g i e", e=4), raw.rearrange("p i (g e) -> p g i e", e=4))
-
-        def round_piece(engine, key, raw, lo, hi):
-            if engine == "gpsimd":
-                piece = kept([P, hi - lo, PACK], BF16, "piece", "handed")
-                round_on_gpsimd(piece[:], raw[:, :, lo:hi])
-            elif engine == "scalar":
-                piece = by_scalar([P, hi - lo, PACK], BF16, "piece") if hi - lo <= HALF else kept([P, hi - lo, PACK], BF16, "whole_%s" % key)
-                round_rows(nc.scalar.copy, piece[:], raw[:, :, lo:hi])
-            else:
-                piece = by_vector([P, hi - lo, PACK], BF16, "piece")
-                round_rows(nc.vector.tensor_copy, piece[:], raw[:, :, lo:hi])
-            pieces[key, lo] = (piece, hi)
+        def round_on_scalar(dst, raw):
+            nc.scalar.copy(dst.rearrange("p (g e) i -> p g i e", e=4), raw.rearrange("p i (g e) -> p g i e", e=4))
 
         def quantize(key, lo, hi):
-            at = max(first for name, first in pieces if name == key and first <= lo)
-            piece = pieces[key, at][0][:, lo - at : hi - at, :]
             made = by_vector([P, hi - lo], U32, "codes_%s" % key)
             plane = kept([P, hi - lo], U8, "scales_%s_%d" % (key, lo))
-            nc.vector.quantize_mx(out=made[:].bitcast(FP8X4), scales=plane[:], in_=piece.rearrange("p w i -> p (w i)"))
+            nc.vector.quantize_mx(out=made[:].bitcast(FP8X4), scales=plane[:], in_=pieces[key, lo][:].rearrange("p w i -> p (w i)"))
             codes.setdefault(key, []).append((lo, hi, made, plane))
 
         def stationary(key, at):
-            lo, hi, made, plane = [part for part in codes[key] if part[0] <= at < part[1]][0]
-            return made[:, at - lo : at - lo + P].bitcast(FP8X4), plane[:, at - lo : at - lo + P]
+            _, _, made, plane = codes[key][0]
+            return made[:, at : at + P].bitcast(FP8X4), plane[:, at : at + P]
 
         def dense(acc, fixed, moving, first):
             lhs, lhs_scale = fixed
@@ -161,40 +146,29 @@ def tile_list_tabts_silu_kernel(tc, tab_words, tab_scales, w4_words, w4_scales, 
                 nc.tensor.matmul_mx(out=acc[:, lo:hi], lhsT=lhs, lhsT_scale=lhs_scale, rhs=made[:].bitcast(FP8X4), rhs_scale=plane[:],
                                     start=first and k == 0, stop=not first and k == len(moving) - 1)
 
-        def finish(i, m, src, lo=0, hi=CHUNK):
-            result = by_scalar([P, hi - lo], F32, "result")
-            nc.scalar.activation(result[:], src, ACT.Silu, bias=small["bias"][:, m : m + 1])
-            nc.sync.dma_start(out[m * P : (m + 1) * P, i * CHUNK + lo : i * CHUNK + hi], result[:])
-
         def table_pass(i, m, acc, first):
-            cols = slice(m * P, (m + 1) * P)
-            nc.tensor.matmul_mx(out=acc[:], lhsT=w4_bytes[:, 2 * m * P : 2 * (m + 1) * P].bitcast(FP4X4), lhsT_scale=w4_plane[:, cols],
-                                rhs=words[i][:].bitcast(FP8X4), rhs_scale=picked_s[i], start=first, stop=not first)
+            nc.tensor.matmul_mx(out=acc[:], lhsT=w4_bytes[:, 2 * m * P : 2 * (m + 1) * P].bitcast(FP4X4), lhsT_scale=w4_plane[:, m * P : (m + 1) * P],
+                                rhs=words[i][:].bitcast(FP8X4), rhs_scale=picked_s(i), start=first, stop=not first)
 
         def dense_pass(i, m, acc, first):
             dense(acc, stationary("u", m * P), codes[i], first)
 
         def turned_table_pass(i, a, acc, first):
             cols = slice(a * P, (a + 1) * P)
-            nc.tensor.matmul_mx(out=acc[:], lhsT=words[i][:, cols].bitcast(FP8X4), lhsT_scale=picked_s[i][:, cols],
+            nc.tensor.matmul_mx(out=acc[:], lhsT=words[i][:, cols].bitcast(FP8X4), lhsT_scale=picked_s(i)[:, cols],
                                 rhs=w4_bytes.bitcast(FP4X4), rhs_scale=w4_plane, start=first, stop=not first)
 
         def turned_dense_pass(i, a, acc, first):
             dense(acc, stationary(i, a * P), codes["u"], first)
 
-        def open_sums(one_pass, i, tiles=range(N_TILES), half="upper"):
+        def open_sums(one_pass, i, tiles=range(N_TILES)):
             for m in tiles:
-                sums[i, m] = bank("acc", half)
+                sums[i, m] = bank("acc")
                 one_pass(i, m, sums[i, m], True)
 
         def close_sums(one_pass, i, tiles=range(N_TILES)):
             for m in tiles:
                 one_pass(i, m, sums[i, m], False)
-
-        def scale_direct(i, m, acc, lo=0, hi=CHUNK):
-            scaled = by_vector([P, hi - lo], F32, "scaled")
-            nc.vector.tensor_tensor(scaled[:], acc[:, lo:hi], picked_t[i][:, lo:hi], ALU.mult)
-            return scaled
 
         def ts_to_partitions(i):
             turned = bank("turned")
@@ -206,18 +180,29 @@ def tile_list_tabts_silu_kernel(tc, tab_words, tab_scales, w4_words, w4_scales, 
         def turn_bias():
             turned = bank("turned")
             nc.tensor.transpose(turned[:, 0:P], b_rows[:], ident[:])
-            small["bias"] = by_scalar([P, N_TILES], F32, "bias")
-            nc.scalar.copy(small["bias"][:], turned[:, 0:N_TILES])
+            columns = by_scalar([P, N_TILES], F32, "bias")
+            nc.scalar.copy(columns[:], turned[:, 0:N_TILES])
+            return columns
 
-        def scale_turned(i, a, acc):
+        def scale_turned(i, a):
             blocks[i, a] = by_scalar([P, M], F32, "block%d_%d" % (i, a))
-            nc.scalar.activation(blocks[i, a][:], acc[:], ACT.Copy, scale=ts_col[i][:, a : a + 1])
+            nc.scalar.activation(blocks[i, a][:], sums[i, a][:], ACT.Copy, scale=ts_col[i][:, a : a + 1])
 
-        def turn_back(i, m, half="lower"):
-            turned = bank("turned", half)
+        def turn_back(i, m):
+            turned = bank("turned")
             for a in reversed(range(BLOCKS)):
                 nc.tensor.transpose(turned[:, a * P : (a + 1) * P], blocks[i, a][:, m * P : (m + 1) * P], ident[:])
             return turned
+
+        def product(i, m, lo=0, hi=CHUNK):
+            scaled = by_vector([P, hi - lo], F32, "scaled")
+            nc.vector.tensor_tensor(scaled[:], sums[i, m][:, lo:hi], picked_t[i][:, lo:hi], ALU.mult)
+            return scaled
+
+        def finish(i, m, src, lo=0, hi=CHUNK):
+            result = by_scalar([P, hi - lo], F32, "result")
+            nc.scalar.activation(result[:], src[:], ACT.Silu, bias=bias[:, m : m + 1])
+            nc.sync.dma_start(out[m * P : (m + 1) * P, i * CHUNK + lo : i * CHUNK + hi], result[:])
 
         nc.vector.memset(tab_s[:], 0)
         identity()
@@ -225,14 +210,18 @@ def tile_list_tabts_silu_kernel(tc, tab_words, tab_scales, w4_words, w4_scales, 
         nc.gpsimd.memset(w4_s[:], 0)
         nc.gpsimd.memset(b_rows[:], 0.0)
         nc.scalar.activation(warm[:], ones[:, 0:1], ACT.Silu, bias=ones[:, 1:2])
+
         nc.sync.dma_start(offsets[:], offs)
+        ts_row = ts[0].rearrange("(p a) -> p a", p=P)
         for half in range(2):
-            nc.sync.dma_start(ts_cols[64 * half : 64 * (half + 1), :], ts[0].rearrange("(p a) -> p a", p=P)[64 * half : 64 * (half + 1), :])
-        nc.sync.dma_start(tab_s[0:P:8, :], tab_scales[0].bitcast(I32))
+            part = slice(half * P // 2, (half + 1) * P // 2)
+            nc.sync.dma_start(ts_cols[part, :], ts_row[part, :])
+        nc.sync.dma_start(tab_s[0:P:SPREAD, :], tab_scales[0].bitcast(I32))
         load_rows(u_raw, u)
         load_c(0)
-        load_planes(nc.sync, w4_s, w4_scales[0])
-        load_words()
+        for r in range(PACK):
+            nc.sync.dma_start(w4_s[r:P:QUADRANT, :], w4_scales[0][r:GROUP:PACK, :].bitcast(I32))
+        nc.sync.dma_start(tab_w[:], tab_words[0].rearrange("p t i -> p (t i)").bitcast(I32))
         nc.sync.dma_start(w4_w[:], w4_words[0].bitcast(I32))
         pick_scales()
         for k in range(2):
@@ -240,64 +229,59 @@ def tile_list_tabts_silu_kernel(tc, tab_words, tab_scales, w4_words, w4_scales, 
         nc.sync.dma_start(b_rows[0:N_TILES, :], b.rearrange("(m p) -> m p", p=P))
         load_c(2)
         load_c(3)
+
         ts_window()
-        products = {}
-        round_piece("gpsimd", "u", u_raw, 0, 512)
-        quantize("u", 0, 512)
-        round_piece("scalar", 0, c_raw[0], 0, 512)
+        pieces["u", 0] = handed(M, "piece")
+        round_on_gpsimd(pieces["u", 0][:], u_raw[:])
+        quantize("u", 0, M)
+        pieces[0, 0] = kept([P, CHUNK, PACK], BF16, "whole_0")
+        round_on_scalar(pieces[0, 0][:], c_raw[0][:])
         pick_ts(0)
         ts_to_partitions(0)
-        quantize(0, 0, 512)
-        open_sums(turned_dense_pass, 0, range(2), half="lower")
-        second = kept([P, CHUNK, PACK], BF16, "second", "handed")
-        pieces[1, 0] = (second, CHUNK)
+        quantize(0, 0, CHUNK)
+
+        open_sums(turned_dense_pass, 0, range(2))
+        pieces[1, 0] = handed(CHUNK, "second")
         for k in range(2):
-            round_on_gpsimd(second[:, k * HALF : (k + 1) * HALF, :], c_pair[k][:])
+            round_on_gpsimd(pieces[1, 0][:, k * HALF : (k + 1) * HALF, :], c_pair[k][:])
         pick_words(0)
         close_sums(turned_table_pass, 0, range(2))
         for a in range(2, BLOCKS):
-            open_sums(turned_table_pass, 0, (a,), half="lower")
+            open_sums(turned_table_pass, 0, (a,))
             close_sums(turned_dense_pass, 0, (a,))
         for a in range(BLOCKS):
-            scale_turned(0, a, sums[0, a])
+            scale_turned(0, a)
+
         pick_words(1, 2)
-        open_sums(table_pass, 1, half="lower")
-        turn_bias()
-        pick_ts(2)
-        quantize(1, 0, 512)
-        round_piece("scalar", 2, c_raw[2], 0, 256)
-        round_piece("gpsimd", 2, c_raw[2], 256, 512)
+        open_sums(table_pass, 1)
+        bias = turn_bias()
+        pick_words(3)
+        quantize(1, 0, CHUNK)
+        pieces[2, 0] = by_scalar([P, HALF, PACK], BF16, "piece")
+        round_on_scalar(pieces[2, 0][:], c_raw[2][:, :, 0:HALF])
+        pieces[2, HALF] = handed(HALF, "piece")
+        round_on_gpsimd(pieces[2, HALF][:], c_raw[2][:, :, HALF:CHUNK])
         for m in range(N_TILES):
-            finish(0, m, turn_back(0, m, "upper")[:])
+            finish(0, m, turn_back(0, m))
         close_sums(dense_pass, 1)
         open_sums(table_pass, 2)
-        pick_words(3)
-        products[1, 0] = scale_direct(1, 0, sums[1, 0])
-        finish(1, 0, products[1, 0][:])
-        quantize(2, 0, 256)
-        quantize(2, 256, 512)
-        fourth = kept([P, CHUNK, PACK], BF16, "fourth", "handed")
-        pieces[3, 0] = (fourth, CHUNK)
-        round_on_gpsimd(fourth[:, 128:CHUNK, :], c_raw[3][:, :, 128:CHUNK])
+        pick_ts(2)
+
+        quantize(2, 0, HALF)
+        quantize(2, HALF, CHUNK)
+        pieces[3, 0] = handed(CHUNK, "fourth")
+        round_on_gpsimd(pieces[3, 0][:], c_raw[3][:])
         close_sums(dense_pass, 2)
-        products[1, 1] = scale_direct(1, 1, sums[1, 1])
-        round_rows(nc.scalar.copy, fourth[:, 0:128, :], c_raw[3][:, :, 0:128])
-        finish(1, 1, products[1, 1][:])
-        products[1, 2] = scale_direct(1, 2, sums[1, 2])
-        finish(1, 2, products[1, 2][:])
-        products[1, 3] = scale_direct(1, 3, sums[1, 3])
-        finish(1, 3, products[1, 3][:])
-        open_sums(table_pass, 3, half="lower")
-        products[2, 0] = scale_direct(2, 0, sums[2, 0])
-        finish(2, 0, products[2, 0][:])
-        products[2, 1] = scale_direct(2, 1, sums[2, 1])
-        finish(2, 1, products[2, 1][:])
-        quantize(3, 0, 512)
-        close_sums(dense_pass, 3)
-        products[2, 2] = scale_direct(2, 2, sums[2, 2])
-        finish(2, 2, products[2, 2][:])
-        products[2, 3] = scale_direct(2, 3, sums[2, 3])
-        finish(2, 3, products[2, 3][:])
         for m in range(N_TILES):
-            for lo, hi in ((0, CHUNK),) if m < N_TILES - 1 else ((0, HALF), (HALF, CHUNK)):
-                finish(3, m, scale_direct(3, m, sums[3, m], lo, hi)[:], lo, hi)
+            finish(1, m, product(1, m))
+        open_sums(table_pass, 3)
+        for m in range(2):
+            finish(2, m, product(2, m))
+        quantize(3, 0, CHUNK)
+        close_sums(dense_pass, 3)
+        for m in range(2, N_TILES):
+            finish(2, m, product(2, m))
+        for m in range(N_TILES - 1):
+            finish(3, m, product(3, m))
+        for lo in (0, HALF):
+            finish(3, N_TILES - 1, product(3, N_TILES - 1, lo, lo + HALF), lo, lo + HALF)

@@ -71,7 +71,8 @@ def tile_list_tabts_silu_kernel(tc, tab_words, tab_scales, w4_words, w4_scales, 
         tab_w = kept([P, T], I32, "tab_w")
         u_raw = kept([P, PACK, M], F32, "u_raw")
         c_raw = {i: kept([P, PACK, CHUNK], F32, "c_raw%d" % i) for i in (0, 2, 3)}
-        c_pair = [kept([P, PACK, HALF], F32, "c_pair%d" % k) for k in range(2)]
+        cuts = ((0, P), (P, HALF), (HALF, CHUNK))
+        c_part = [kept([P, PACK, hi - lo], F32, "c_part%d" % lo) for lo, hi in cuts]
         w4_bytes = w4_w[:].bitcast(U8)
         w4_plane = w4_s[:].bitcast(U8)
         codes, pieces, words, picked_t, ts_col, blocks, sums = {}, {}, {}, {}, {}, {}, {}
@@ -224,8 +225,8 @@ def tile_list_tabts_silu_kernel(tc, tab_words, tab_scales, w4_words, w4_scales, 
         nc.sync.dma_start(tab_w[:], tab_words[0].rearrange("p t i -> p (t i)").bitcast(I32))
         nc.sync.dma_start(w4_w[:], w4_words[0].bitcast(I32))
         pick_scales()
-        for k in range(2):
-            load_rows(c_pair[k], c[:, CHUNK + k * HALF : CHUNK + (k + 1) * HALF])
+        for part, (lo, hi) in zip(c_part, cuts):
+            load_rows(part, c[:, CHUNK + lo : CHUNK + hi])
         nc.sync.dma_start(b_rows[0:N_TILES, :], b.rearrange("(m p) -> m p", p=P))
         load_c(2)
         load_c(3)
@@ -242,8 +243,8 @@ def tile_list_tabts_silu_kernel(tc, tab_words, tab_scales, w4_words, w4_scales, 
 
         open_sums(turned_dense_pass, 0, range(2))
         pieces[1, 0] = handed(CHUNK, "second")
-        for k in range(2):
-            round_on_gpsimd(pieces[1, 0][:, k * HALF : (k + 1) * HALF, :], c_pair[k][:])
+        for part, (lo, hi) in zip(c_part, cuts):
+            round_on_gpsimd(pieces[1, 0][:, lo:hi, :], part[:])
         pick_words(0)
         close_sums(turned_table_pass, 0, range(2))
         for a in range(2, BLOCKS):

@@ -71,7 +71,7 @@ def tile_list_tabts_silu_kernel(tc, tab_words, tab_scales, w4_words, w4_scales, 
         tab_w = kept([P, T], I32, "tab_w")
         u_raw = kept([P, PACK, M], F32, "u_raw")
         c_raw = {i: kept([P, PACK, CHUNK], F32, "c_raw%d" % i) for i in (0, 2, 3)}
-        cuts = ((0, P), (P, HALF), (HALF, CHUNK))
+        cuts = [(a * P, (a + 1) * P) for a in range(BLOCKS)]
         c_part = [kept([P, PACK, hi - lo], F32, "c_part%d" % lo) for lo, hi in cuts]
         w4_bytes = w4_w[:].bitcast(U8)
         w4_plane = w4_s[:].bitcast(U8)

@@ -205,7 +205,8 @@ def tile_list_tabts_silu_kernel(tc, tab_words, tab_scales, w4_words, w4_scales, 
             nc.scalar.activation(result[:], src[:], ACT.Silu, bias=bias[:, m : m + 1])
             nc.sync.dma_start(out[m * P : (m + 1) * P, i * CHUNK + lo : i * CHUNK + hi], result[:])
 
-        nc.vector.memset(tab_s[:], 0)
+        nc.vector.memset(tab_s[:, 0 : T // 8], 0)
+        nc.gpsimd.memset(tab_s[:, T // 8 : T // 4], 0)
         identity()
         nc.vector.memset(plane_s[:], 0)
         nc.gpsimd.memset(w4_s[:], 0)
@@ -213,10 +214,7 @@ def tile_list_tabts_silu_kernel(tc, tab_words, tab_scales, w4_words, w4_scales, 
         nc.scalar.activation(warm[:], ones[:, 0:1], ACT.Silu, bias=ones[:, 1:2])
 
         nc.sync.dma_start(offsets[:], offs)
-        ts_row = ts[0].rearrange("(p a) -> p a", p=P)
-        for half in range(2):
-            part = slice(half * P // 2, (half + 1) * P // 2)
-            nc.sync.dma_start(ts_cols[part, :], ts_row[part, :])
+        nc.sync.dma_start(ts_cols[:], ts[0].rearrange("(p a) -> p a", p=P))
         nc.sync.dma_start(tab_s[0:P:SPREAD, :], tab_scales[0].bitcast(I32))
         load_rows(u_raw, u)
         load_c(0)

@@ -60,10 +60,10 @@ def tile_list_tabts_silu_kernel(tc, tab_words, tab_scales, w4_words, w4_scales, 
         ts_cols = kept([P, TS_PER_PARTITION], F32, "ts_cols")
         ts_all = kept([P, T], F32, "ts_all")
         b_rows = kept([P, P], F32, "b_rows")
-        ones = kept([P, P], F32, "ones")
+        constants = kept([P, P + 1], F32, "constants")
+        ones, quadrant = constants[:, 0:P], constants[:, P : P + 1]
         ramp = kept([P, P], F32, "ramp")
         lane = kept([P, QUADRANT], F32, "lane")
-        quadrant = kept([P, 1], F32, "quadrant")
         ident = kept([P, P], F32, "ident")
         warm = kept([P, 1], F32, "warm")
         w4_w = kept([P, 2 * M // 4], I32, "w4_w")
@@ -78,7 +78,7 @@ def tile_list_tabts_silu_kernel(tc, tab_words, tab_scales, w4_words, w4_scales, 
         codes, pieces, words, picked_t, ts_col, blocks, sums = {}, {}, {}, {}, {}, {}, {}
 
         def identity():
-            nc.gpsimd.memset(ones[:], 1.0)
+            nc.vector.memset(constants[:], 1.0)
             for q in range(P // QUADRANT):
                 nc.gpsimd.memset(quadrant[QUADRANT * q : QUADRANT * (q + 1), :], float(QUADRANT * q))
             nc.vector.tensor_tensor_scan(ramp[:], ones[:], ones[:], 0.0, ALU.mult, ALU.add)
@@ -205,8 +205,8 @@ def tile_list_tabts_silu_kernel(tc, tab_words, tab_scales, w4_words, w4_scales, 
             nc.scalar.activation(result[:], src[:], ACT.Silu, bias=bias[:, m : m + 1])
             nc.sync.dma_start(out[m * P : (m + 1) * P, i * CHUNK + lo : i * CHUNK + hi], result[:])
 
-        nc.vector.memset(tab_s[:, 0 : T // 8], 0)
-        nc.gpsimd.memset(tab_s[:, T // 8 : T // 4], 0)
+        for half in range(2):
+            nc.vector.memset(tab_s[:, half * T // 8 : (half + 1) * T // 8], 0)
         identity()
         nc.vector.memset(plane_s[:], 0)
         nc.gpsimd.memset(w4_s[:], 0)
@@ -215,7 +215,9 @@ def tile_list_tabts_silu_kernel(tc, tab_words, tab_scales, w4_words, w4_scales, 
 
         nc.sync.dma_start(offsets[:], offs)
         nc.sync.dma_start(ts_cols[:], ts[0].rearrange("(p a) -> p a", p=P))
-        nc.sync.dma_start(tab_s[0:P:SPREAD, :], tab_scales[0].bitcast(I32))
+        for half in range(2):
+            cols = slice(half * T // 8, (half + 1) * T // 8)
+            nc.sync.dma_start(tab_s[0:P:SPREAD, cols], tab_scales[0].bitcast(I32)[:, cols])
         load_rows(u_raw, u)
         load_c(0)
         for r in range(PACK):

@@ -56,18 +56,18 @@ def tile_list_tabts_silu_kernel(tc, tab_words, tab_scales, w4_words, w4_scales, 
 
         offsets = kept([P, S // GROUP], U16, "offsets")
         tab_s = kept([P, T // 4], I32, "tab_s")
-        plane_s = kept([P, S // 4], I32, "plane_s")
         ts_cols = kept([P, TS_PER_PARTITION], F32, "ts_cols")
         ts_all = kept([P, T], F32, "ts_all")
-        b_rows = kept([P, P], F32, "b_rows")
         constants = kept([P, P + 1], F32, "constants")
         ones, quadrant = constants[:, 0:P], constants[:, P : P + 1]
         ramp = kept([P, P], F32, "ramp")
         lane = kept([P, QUADRANT], F32, "lane")
-        ident = kept([P, P], F32, "ident")
+        ident, plane_s, w4_s, b_rows = [
+            keep.tile(shape, dtype, name=name, tag="set_up", bufs=4, align_bytes=ALIGN)
+            for shape, dtype, name in (([P, P], F32, "ident"), ([P, S // 4], I32, "plane_s"), ([P, M // 4], I32, "w4_s"), ([P, P], F32, "b_rows"))
+        ]
         warm = kept([P, 1], F32, "warm")
         w4_w = kept([P, 2 * M // 4], I32, "w4_w")
-        w4_s = kept([P, M // 4], I32, "w4_s")
         tab_w = kept([P, T], I32, "tab_w")
         u_raw = kept([P, PACK, M], F32, "u_raw")
         c_raw = {i: kept([P, PACK, CHUNK], F32, "c_raw%d" % i) for i in (0, 2, 3)}
@@ -209,8 +209,8 @@ def tile_list_tabts_silu_kernel(tc, tab_words, tab_scales, w4_words, w4_scales, 
             nc.vector.memset(tab_s[:, half * T // 8 : (half + 1) * T // 8], 0)
         identity()
         nc.vector.memset(plane_s[:], 0)
-        nc.gpsimd.memset(w4_s[:], 0)
-        nc.gpsimd.memset(b_rows[:], 0.0)
+        nc.vector.memset(w4_s[:], 0)
+        nc.vector.memset(b_rows[:], 0.0)
         nc.scalar.activation(warm[:], ones[:, 0:1], ACT.Silu, bias=ones[:, 1:2])
 
         nc.sync.dma_start(offsets[:], offs)

@@ -262,9 +262,12 @@ def tile_list_tabts_silu_kernel(tc, tab_words, tab_scales, w4_words, w4_scales, 
         round_on_scalar(pieces[2, 0][:], c_raw[2][:, :, 0:HALF])
         pieces[2, HALF] = handed(HALF, "piece")
         round_on_gpsimd(pieces[2, HALF][:], c_raw[2][:, :, HALF:CHUNK])
-        for m in range(N_TILES):
+        for m in range(2):
             finish(0, m, turn_back(0, m))
-        close_sums(dense_pass, 1)
+        close_sums(dense_pass, 1, range(2))
+        for m in range(2, N_TILES):
+            finish(0, m, turn_back(0, m))
+        close_sums(dense_pass, 1, range(2, N_TILES))
         open_sums(table_pass, 2)
         pick_ts(2)
 

@@ -109,7 +109,7 @@ def tile_list_tabts_silu_kernel(tc, tab_words, tab_scales, w4_words, w4_scales, 
             rows = by_vector([P, S], U8, "rows")
             nc.vector.tensor_copy(rows[:], tab_s[:].bitcast(U8).indirect(offsets[:]))
             for r in range(PACK):
-                nc.sync.dma_start(plane_s[r:P:QUADRANT, :], rows[SPREAD * r : P : QUADRANT, :].bitcast(I32))
+                nc.sync.dma_start(plane_s[r:P:QUADRANT, :], rows[P - GROUP + r : P : PACK, :].bitcast(I32))
 
         def picked_s(i):
             return plane_s[:].bitcast(U8)[:, i * CHUNK : (i + 1) * CHUNK]
@@ -205,8 +205,7 @@ def tile_list_tabts_silu_kernel(tc, tab_words, tab_scales, w4_words, w4_scales, 
             nc.scalar.activation(result[:], src[:], ACT.Silu, bias=bias[:, m : m + 1])
             nc.sync.dma_start(out[m * P : (m + 1) * P, i * CHUNK + lo : i * CHUNK + hi], result[:])
 
-        for half in range(2):
-            nc.vector.memset(tab_s[:, half * T // 8 : (half + 1) * T // 8], 0)
+        nc.vector.memset(tab_s[0 : P - GROUP, :], 0)
         identity()
         nc.vector.memset(plane_s[:], 0)
         nc.vector.memset(w4_s[:], 0)
@@ -215,9 +214,7 @@ def tile_list_tabts_silu_kernel(tc, tab_words, tab_scales, w4_words, w4_scales, 
 
         nc.sync.dma_start(offsets[:], offs)
         nc.sync.dma_start(ts_cols[:], ts[0].rearrange("(p a) -> p a", p=P))
-        for half in range(2):
-            cols = slice(half * T // 8, (half + 1) * T // 8)
-            nc.sync.dma_start(tab_s[0:P:SPREAD, cols], tab_scales[0].bitcast(I32)[:, cols])
+        nc.sync.dma_start(tab_s[P - GROUP : P, :], tab_scales[0].bitcast(I32))
         load_rows(u_raw, u)
         load_c(0)
         for r in range(PACK):

@@ -26,11 +26,12 @@ N_CHUNKS = S // CHUNK
 N_TILES = M // P
 BLOCKS = CHUNK // P
 HALF = CHUNK // 2
+SHARE = 128
 TS_PER_PARTITION = T // P
 BANKS = 8
 ALIGN = 512
-VECTOR_TILES = 24
-SCALAR_TILES = 14
+VECTOR_TILES = 23
+SCALAR_TILES = 16
 
 
 def tile_list_tabts_silu_kernel(tc, tab_words, tab_scales, w4_words, w4_scales, c, u, ts, b, offs, out):
@@ -51,8 +52,10 @@ def tile_list_tabts_silu_kernel(tc, tab_words, tab_scales, w4_words, w4_scales, 
         def bank(name):
             return banks.tile([P, CHUNK], F32, name=name, tag="ring")
 
-        def handed(width, name):
-            return kept([P, width, PACK], BF16, name, "handed")
+        strip = kept([P, (SHARE + CHUNK) * PACK], BF16, "strip")
+
+        def handed(first):
+            return strip[:, first * PACK : (first + CHUNK) * PACK].rearrange("p (w i) -> p w i", i=PACK)
 
         offsets = kept([P, S // GROUP], U16, "offsets")
         tab_s = kept([P, T // 4], I32, "tab_s")
@@ -69,9 +72,11 @@ def tile_list_tabts_silu_kernel(tc, tab_words, tab_scales, w4_words, w4_scales, 
         warm = kept([P, 1], F32, "warm")
         w4_w = kept([P, 2 * M // 4], I32, "w4_w")
         tab_w = kept([P, T], I32, "tab_w")
-        u_raw = kept([P, PACK, M], F32, "u_raw")
-        c_raw = {i: kept([P, PACK, CHUNK], F32, "c_raw%d" % i) for i in (0, 2, 3)}
-        cuts = [(a * P, (a + 1) * P) for a in range(BLOCKS)]
+        u_half = [kept([P, PACK, M // 2], F32, "u_half%d" % h) for h in range(2)]
+        c_raw = {0: kept([P, PACK, CHUNK], F32, "c_raw0")}
+        c_share = {i: kept([P, PACK, SHARE], F32, "c_share%d" % i) for i in (2, 3)}
+        c_rest = {i: kept([P, PACK, CHUNK - SHARE], F32, "c_rest%d" % i) for i in (2, 3)}
+        cuts = [(0, HALF), (HALF, CHUNK)]
         c_part = [kept([P, PACK, hi - lo], F32, "c_part%d" % lo) for lo, hi in cuts]
         w4_bytes = w4_w[:].bitcast(U8)
         w4_plane = w4_s[:].bitcast(U8)
@@ -120,10 +125,11 @@ def tile_list_tabts_silu_kernel(tc, tab_words, tab_scales, w4_words, w4_scales, 
             for k in range(n):
                 words[i + k] = picked[:, k * CHUNK : (k + 1) * CHUNK]
 
-        def pick_ts(i):
-            picked = by_vector([P, 2 * CHUNK], F32, "picked%d" % i)
-            nc.vector.tensor_copy(picked[:], ts_all[:].indirect(listed(i, 2)))
-            picked_t[i], picked_t[i + 1] = picked[:, 0:CHUNK], picked[:, CHUNK : 2 * CHUNK]
+        def pick_ts(i, n=1):
+            picked = by_vector([P, n * CHUNK], F32, "picked%d" % i)
+            nc.vector.tensor_copy(picked[:], ts_all[:].indirect(listed(i, n)))
+            for k in range(n):
+                picked_t[i + k] = picked[:, k * CHUNK : (k + 1) * CHUNK]
 
         def round_on_gpsimd(dst, raw):
             nc.gpsimd.tensor_scalar(dst.rearrange("p (g e) i -> p g i e", e=4), raw.rearrange("p i (g e) -> p g i e", e=4), 1.0, 0.0, ALU.mult, ALU.add)
@@ -189,9 +195,9 @@ def tile_list_tabts_silu_kernel(tc, tab_words, tab_scales, w4_words, w4_scales, 
             blocks[i, a] = by_scalar([P, M], F32, "block%d_%d" % (i, a))
             nc.scalar.activation(blocks[i, a][:], sums[i, a][:], ACT.Copy, scale=ts_col[i][:, a : a + 1])
 
-        def turn_back(i, m):
+        def turn_back(i, m, order=None):
             turned = bank("turned")
-            for a in reversed(range(BLOCKS)):
+            for a in order or reversed(range(BLOCKS)):
                 nc.tensor.transpose(turned[:, a * P : (a + 1) * P], blocks[i, a][:, m * P : (m + 1) * P], ident[:])
             return turned
 
@@ -205,75 +211,81 @@ def tile_list_tabts_silu_kernel(tc, tab_words, tab_scales, w4_words, w4_scales, 
             nc.scalar.activation(result[:], src[:], ACT.Silu, bias=bias[:, m : m + 1])
             nc.sync.dma_start(out[m * P : (m + 1) * P, i * CHUNK + lo : i * CHUNK + hi], result[:])
 
-        nc.vector.memset(tab_s[0 : P - GROUP, :], 0)
         identity()
+        nc.vector.memset(tab_s[0 : P - GROUP, :], 0)
         nc.vector.memset(plane_s[:], 0)
         nc.vector.memset(w4_s[:], 0)
         nc.vector.memset(b_rows[:], 0.0)
         nc.scalar.activation(warm[:], ones[:, 0:1], ACT.Silu, bias=ones[:, 1:2])
 
-        nc.sync.dma_start(offsets[:], offs)
         nc.sync.dma_start(ts_cols[:], ts[0].rearrange("(p a) -> p a", p=P))
+        nc.sync.dma_start(offsets[:], offs)
         nc.sync.dma_start(tab_s[P - GROUP : P, :], tab_scales[0].bitcast(I32))
-        load_rows(u_raw, u)
+        for h in range(2):
+            load_rows(u_half[h], u[:, h * (M // 2) : (h + 1) * (M // 2)])
         load_c(0)
         for r in range(PACK):
             nc.sync.dma_start(w4_s[r:P:QUADRANT, :], w4_scales[0][r:GROUP:PACK, :].bitcast(I32))
+        nc.sync.dma_start(b_rows[0:N_TILES, :], b.rearrange("(m p) -> m p", p=P))
         nc.sync.dma_start(tab_w[:], tab_words[0].rearrange("p t i -> p (t i)").bitcast(I32))
         nc.sync.dma_start(w4_w[:], w4_words[0].bitcast(I32))
         pick_scales()
         for part, (lo, hi) in zip(c_part, cuts):
             load_rows(part, c[:, CHUNK + lo : CHUNK + hi])
-        nc.sync.dma_start(b_rows[0:N_TILES, :], b.rearrange("(m p) -> m p", p=P))
-        load_c(2)
-        load_c(3)
+        load_rows(c_share[2], c[:, 3 * CHUNK - SHARE : 3 * CHUNK])
+        load_rows(c_rest[2], c[:, 2 * CHUNK : 3 * CHUNK - SHARE])
+        load_rows(c_share[3], c[:, 3 * CHUNK : 3 * CHUNK + SHARE])
+        load_rows(c_rest[3], c[:, 3 * CHUNK + SHARE : 4 * CHUNK])
 
         ts_window()
-        pieces["u", 0] = handed(M, "piece")
-        round_on_gpsimd(pieces["u", 0][:], u_raw[:])
+        pieces["u", 0] = handed(0)
+        for h in range(2):
+            round_on_gpsimd(pieces["u", 0][:, h * (M // 2) : (h + 1) * (M // 2), :], u_half[h][:])
         quantize("u", 0, M)
-        pieces[0, 0] = kept([P, CHUNK, PACK], BF16, "whole_0")
-        round_on_scalar(pieces[0, 0][:], c_raw[0][:])
-        pick_ts(0)
+        pieces[0, 0] = handed(0)
+        round_on_gpsimd(pieces[0, 0][:, 0:HALF, :], c_raw[0][:, :, 0:HALF])
+        round_on_scalar(pieces[0, 0][:, HALF:CHUNK, :], c_raw[0][:, :, HALF:CHUNK])
+        bias = turn_bias()
+        pick_ts(0, 2)
         ts_to_partitions(0)
         quantize(0, 0, CHUNK)
 
-        open_sums(turned_dense_pass, 0, range(2))
-        pieces[1, 0] = handed(CHUNK, "second")
+        open_sums(turned_dense_pass, 0)
+        pick_ts(2)
+        pieces[1, 0] = handed(0)
         for part, (lo, hi) in zip(c_part, cuts):
             round_on_gpsimd(pieces[1, 0][:, lo:hi, :], part[:])
         pick_words(0)
-        close_sums(turned_table_pass, 0, range(2))
-        for a in range(2, BLOCKS):
-            open_sums(turned_table_pass, 0, (a,))
-            close_sums(turned_dense_pass, 0, (a,))
+        close_sums(turned_table_pass, 0)
         for a in range(BLOCKS):
             scale_turned(0, a)
 
-        pick_words(1, 2)
-        open_sums(table_pass, 1)
-        bias = turn_bias()
-        pick_words(3)
+        pick_words(1)
+        open_sums(table_pass, 1, (0, 1))
+        pick_words(2, 2)
         quantize(1, 0, CHUNK)
-        pieces[2, 0] = by_scalar([P, HALF, PACK], BF16, "piece")
-        round_on_scalar(pieces[2, 0][:], c_raw[2][:, :, 0:HALF])
-        pieces[2, HALF] = handed(HALF, "piece")
-        round_on_gpsimd(pieces[2, HALF][:], c_raw[2][:, :, HALF:CHUNK])
-        for m in range(2):
-            finish(0, m, turn_back(0, m))
-        close_sums(dense_pass, 1, range(2))
+        pieces[2, 0] = handed(SHARE)
+        round_on_gpsimd(pieces[2, 0][:, 0 : CHUNK - SHARE, :], c_rest[2][:])
+        round_on_scalar(pieces[2, 0][:, CHUNK - SHARE : CHUNK, :], c_share[2][:])
+        finish(0, 0, turn_back(0, 0, (1, 0, 2, 3)))
+        open_sums(table_pass, 1, (2, 3))
+        finish(0, 1, turn_back(0, 1))
+        close_sums(dense_pass, 1, (0, 1))
         for m in range(2, N_TILES):
             finish(0, m, turn_back(0, m))
-        close_sums(dense_pass, 1, range(2, N_TILES))
-        open_sums(table_pass, 2)
-        pick_ts(2)
 
-        quantize(2, 0, HALF)
-        quantize(2, HALF, CHUNK)
-        pieces[3, 0] = handed(CHUNK, "fourth")
-        round_on_gpsimd(pieces[3, 0][:], c_raw[3][:])
+        close_sums(dense_pass, 1, (2, 3))
+        open_sums(table_pass, 2)
+
+        pick_ts(3)
+        for m in range(2):
+            finish(1, m, product(1, m))
+        pieces[3, 0] = handed(0)
+        round_on_scalar(pieces[3, 0][:, 0:SHARE, :], c_share[3][:])
+        quantize(2, 0, CHUNK)
+        round_on_gpsimd(pieces[3, 0][:, SHARE:CHUNK, :], c_rest[3][:])
         close_sums(dense_pass, 2)
-        for m in range(N_TILES):
+        for m in range(2, N_TILES):
             finish(1, m, product(1, m))
         open_sums(table_pass, 3)
         for m in range(2):

@@ -20,18 +20,19 @@ P = 128
 QUADRANT = 32
 PACK = 4
 GROUP = 16
-SPREAD = P // GROUP
 CHUNK = 512
 N_CHUNKS = S // CHUNK
 N_TILES = M // P
 BLOCKS = CHUNK // P
 HALF = CHUNK // 2
-SHARE = 128
+STEP = 64
+EARLY = 3
+SHARE = 160
 TS_PER_PARTITION = T // P
 BANKS = 8
 ALIGN = 512
 VECTOR_TILES = 23
-SCALAR_TILES = 16
+SCALAR_TILES = 13
 
 
 def tile_list_tabts_silu_kernel(tc, tab_words, tab_scales, w4_words, w4_scales, c, u, ts, b, offs, out):
@@ -52,11 +53,7 @@ def tile_list_tabts_silu_kernel(tc, tab_words, tab_scales, w4_words, w4_scales, 
         def bank(name):
             return banks.tile([P, CHUNK], F32, name=name, tag="ring")
 
-        strip = kept([P, (SHARE + CHUNK) * PACK], BF16, "strip")
-
-        def handed(first):
-            return strip[:, first * PACK : (first + CHUNK) * PACK].rearrange("p (w i) -> p w i", i=PACK)
-
+        strip = kept([P, SHARE + CHUNK, PACK], BF16, "strip")
         offsets = kept([P, S // GROUP], U16, "offsets")
         tab_s = kept([P, T // 4], I32, "tab_s")
         ts_cols = kept([P, TS_PER_PARTITION], F32, "ts_cols")
@@ -73,14 +70,14 @@ def tile_list_tabts_silu_kernel(tc, tab_words, tab_scales, w4_words, w4_scales, 
         w4_w = kept([P, 2 * M // 4], I32, "w4_w")
         tab_w = kept([P, T], I32, "tab_w")
         u_half = [kept([P, PACK, M // 2], F32, "u_half%d" % h) for h in range(2)]
-        c_raw = {0: kept([P, PACK, CHUNK], F32, "c_raw0")}
+        c_raw = {i: kept([P, PACK, CHUNK], F32, "c_raw%d" % i) for i in (0,)}
+        c_half = {(1, h): kept([P, PACK, HALF], F32, "c_half1_%d" % h) for h in range(2)}
         c_share = {i: kept([P, PACK, SHARE], F32, "c_share%d" % i) for i in (2, 3)}
         c_rest = {i: kept([P, PACK, CHUNK - SHARE], F32, "c_rest%d" % i) for i in (2, 3)}
-        cuts = [(0, HALF), (HALF, CHUNK)]
-        c_part = [kept([P, PACK, hi - lo], F32, "c_part%d" % lo) for lo, hi in cuts]
         w4_bytes = w4_w[:].bitcast(U8)
         w4_plane = w4_s[:].bitcast(U8)
-        codes, pieces, words, picked_t, ts_col, blocks, sums = {}, {}, {}, {}, {}, {}, {}
+        codes, pieces, words, ts_col, blocks, sums, back = {}, {}, {}, {}, {}, {}, {}
+        picked_t = []
 
         def identity():
             nc.vector.memset(constants[:], 1.0)
@@ -92,6 +89,9 @@ def tile_list_tabts_silu_kernel(tc, tab_words, tab_scales, w4_words, w4_scales, 
 
         def load_rows(dst, src):
             nc.sync.dma_start(dst[:], src.rearrange("(p i) j -> p i j", i=PACK))
+
+        def load_half(i, h):
+            load_rows(c_half[i, h], c[:, i * CHUNK + h * HALF : i * CHUNK + (h + 1) * HALF])
 
         def load_c(i):
             load_rows(c_raw[i], c[:, i * CHUNK : (i + 1) * CHUNK])
@@ -107,8 +107,8 @@ def tile_list_tabts_silu_kernel(tc, tab_words, tab_scales, w4_words, w4_scales, 
                     turned[:].rearrange("q (a p) -> q p a", p=P),
                 )
 
-        def listed(i, n=1):
-            return offsets[:, i * (CHUNK // GROUP) : (i + n) * (CHUNK // GROUP)]
+        def listed(lo, hi):
+            return offsets[:, lo // GROUP : hi // GROUP]
 
         def pick_scales():
             rows = by_vector([P, S], U8, "rows")
@@ -121,15 +121,18 @@ def tile_list_tabts_silu_kernel(tc, tab_words, tab_scales, w4_words, w4_scales, 
 
         def pick_words(i, n=1):
             picked = by_vector([P, n * CHUNK], U32, "words%d" % i)
-            nc.vector.tensor_copy(picked[:], tab_w[:].bitcast(U32).indirect(listed(i, n)))
+            nc.vector.tensor_copy(picked[:], tab_w[:].bitcast(U32).indirect(listed(i * CHUNK, (i + n) * CHUNK)))
             for k in range(n):
                 words[i + k] = picked[:, k * CHUNK : (k + 1) * CHUNK]
 
-        def pick_ts(i, n=1):
-            picked = by_vector([P, n * CHUNK], F32, "picked%d" % i)
-            nc.vector.tensor_copy(picked[:], ts_all[:].indirect(listed(i, n)))
-            for k in range(n):
-                picked_t[i + k] = picked[:, k * CHUNK : (k + 1) * CHUNK]
+        def pick_ts(lo, hi):
+            picked = by_vector([P, hi - lo], F32, "picked%d" % lo)
+            nc.vector.tensor_copy(picked[:], ts_all[:].indirect(listed(lo, hi)))
+            picked_t.append((lo, hi, picked))
+
+        def picked_ts(lo, hi):
+            first, _, picked = [piece for piece in picked_t if piece[0] <= lo and hi <= piece[1]][0]
+            return picked[:, lo - first : hi - first]
 
         def round_on_gpsimd(dst, raw):
             nc.gpsimd.tensor_scalar(dst.rearrange("p (g e) i -> p g i e", e=4), raw.rearrange("p i (g e) -> p g i e", e=4), 1.0, 0.0, ALU.mult, ALU.add)
@@ -137,15 +140,15 @@ def tile_list_tabts_silu_kernel(tc, tab_words, tab_scales, w4_words, w4_scales, 
         def round_on_scalar(dst, raw):
             nc.scalar.copy(dst.rearrange("p (g e) i -> p g i e", e=4), raw.rearrange("p i (g e) -> p g i e", e=4))
 
-        def quantize(key, lo, hi):
+        def quantize(key, lo, hi, tag=None):
             made = by_vector([P, hi - lo], U32, "codes_%s" % key)
-            plane = kept([P, hi - lo], U8, "scales_%s_%d" % (key, lo))
+            plane = kept([P, hi - lo], U8, "scales_%s_%d" % (key, lo), tag)
             nc.vector.quantize_mx(out=made[:].bitcast(FP8X4), scales=plane[:], in_=pieces[key, lo][:].rearrange("p w i -> p (w i)"))
             codes.setdefault(key, []).append((lo, hi, made, plane))
 
         def stationary(key, at):
-            _, _, made, plane = codes[key][0]
-            return made[:, at : at + P].bitcast(FP8X4), plane[:, at : at + P]
+            lo, _, made, plane = [piece for piece in codes[key] if piece[0] <= at < piece[1]][0]
+            return made[:, at - lo : at - lo + P].bitcast(FP8X4), plane[:, at - lo : at - lo + P]
 
         def dense(acc, fixed, moving, first):
             lhs, lhs_scale = fixed
@@ -159,6 +162,10 @@ def tile_list_tabts_silu_kernel(tc, tab_words, tab_scales, w4_words, w4_scales, 
 
         def dense_pass(i, m, acc, first):
             dense(acc, stationary("u", m * P), codes[i], first)
+
+        def narrow_dense_pass(i, m, acc, first):
+            _, _, made, plane = codes[i][0]
+            dense(acc, stationary("u", m * P), [(lo, hi, made[:, lo:hi], plane[:, lo:hi]) for lo, hi in ((P, HALF), (HALF, CHUNK))], first)
 
         def turned_table_pass(i, a, acc, first):
             cols = slice(a * P, (a + 1) * P)
@@ -177,12 +184,15 @@ def tile_list_tabts_silu_kernel(tc, tab_words, tab_scales, w4_words, w4_scales, 
             for m in tiles:
                 one_pass(i, m, sums[i, m], False)
 
-        def ts_to_partitions(i):
+        def ts_to_partitions(first, n):
             turned = bank("turned")
-            for a in range(BLOCKS):
-                nc.tensor.transpose(turned[:, a * P : (a + 1) * P], picked_t[i][:, a * P : (a + 1) * P], ident[:])
-            ts_col[i] = by_scalar([P, BLOCKS], F32, "ts_col%d" % i)
-            nc.scalar.copy(ts_col[i][:], turned[:, 0:CHUNK:P])
+            for a in range(n):
+                nc.tensor.transpose(turned[:, a * STEP : a * STEP + P], picked_ts((first + a) * P, (first + a + 1) * P), ident[:])
+            for lo, hi in ((0, EARLY), (EARLY, n)):
+                columns = kept([P, hi - lo], F32, "ts_col%d" % lo)
+                nc.scalar.copy(columns[:], turned[:, lo * STEP : hi * STEP : STEP])
+                for a in range(lo, hi):
+                    ts_col[divmod(first + a, BLOCKS)] = columns[:, a - lo : a - lo + 1]
 
         def turn_bias():
             turned = bank("turned")
@@ -193,23 +203,40 @@ def tile_list_tabts_silu_kernel(tc, tab_words, tab_scales, w4_words, w4_scales, 
 
         def scale_turned(i, a):
             blocks[i, a] = by_scalar([P, M], F32, "block%d_%d" % (i, a))
-            nc.scalar.activation(blocks[i, a][:], sums[i, a][:], ACT.Copy, scale=ts_col[i][:, a : a + 1])
+            nc.scalar.activation(blocks[i, a][:], sums[i, a][:], ACT.Copy, scale=ts_col[i, a])
 
-        def turn_back(i, m, order=None):
-            turned = bank("turned")
-            for a in order or reversed(range(BLOCKS)):
-                nc.tensor.transpose(turned[:, a * P : (a + 1) * P], blocks[i, a][:, m * P : (m + 1) * P], ident[:])
-            return turned
+        def scale_turned_on_vector(i, a):
+            blocks[i, a] = by_vector([P, M], F32, "block%d_%d" % (i, a))
+            nc.vector.tensor_scalar(blocks[i, a][:], sums[i, a][:], ts_col[i, a], None, ALU.mult)
+
+        def turn_back(i, m, order):
+            if (i, m) not in back:
+                back[i, m] = bank("turned")
+            for a in order:
+                nc.tensor.transpose(back[i, m][:, a * P : (a + 1) * P], blocks[i, a][:, m * P : (m + 1) * P], ident[:])
+            return back[i, m]
 
         def product(i, m, lo=0, hi=CHUNK):
             scaled = by_vector([P, hi - lo], F32, "scaled")
-            nc.vector.tensor_tensor(scaled[:], sums[i, m][:, lo:hi], picked_t[i][:, lo:hi], ALU.mult)
+            nc.vector.tensor_tensor(scaled[:], sums[i, m][:, lo:hi], picked_ts(i * CHUNK + lo, i * CHUNK + hi), ALU.mult)
             return scaled
 
-        def finish(i, m, src, lo=0, hi=CHUNK):
-            result = by_scalar([P, hi - lo], F32, "result")
+        def finish(i, m, src, lo=0, hi=CHUNK, result=None):
+            result = by_scalar([P, hi - lo], F32, "result") if result is None else result
             nc.scalar.activation(result[:], src[:], ACT.Silu, bias=bias[:, m : m + 1])
             nc.sync.dma_start(out[m * P : (m + 1) * P, i * CHUNK + lo : i * CHUNK + hi], result[:])
+
+        def turn_back_block(i, a):
+            turned = bank("turned")
+            for m in range(N_TILES):
+                nc.tensor.transpose(turned[:, m * P : (m + 1) * P], blocks[i, a][:, m * P : (m + 1) * P], ident[:])
+            return turned
+
+        def finish_split(i, m, turned, src):
+            result = by_scalar([P, CHUNK], F32, "result")
+            nc.scalar.activation(result[:, P:CHUNK], src[:], ACT.Silu, bias=bias[:, m : m + 1])
+            nc.scalar.activation(result[:, 0:P], turned[:, m * P : (m + 1) * P], ACT.Silu, bias=bias[:, m : m + 1])
+            nc.sync.dma_start(out[m * P : (m + 1) * P, i * CHUNK : (i + 1) * CHUNK], result[:])
 
         identity()
         nc.vector.memset(tab_s[0 : P - GROUP, :], 0)
@@ -230,63 +257,63 @@ def tile_list_tabts_silu_kernel(tc, tab_words, tab_scales, w4_words, w4_scales, 
         nc.sync.dma_start(tab_w[:], tab_words[0].rearrange("p t i -> p (t i)").bitcast(I32))
         nc.sync.dma_start(w4_w[:], w4_words[0].bitcast(I32))
         pick_scales()
-        for part, (lo, hi) in zip(c_part, cuts):
-            load_rows(part, c[:, CHUNK + lo : CHUNK + hi])
+        load_half(1, 0)
+        load_half(1, 1)
         load_rows(c_share[2], c[:, 3 * CHUNK - SHARE : 3 * CHUNK])
         load_rows(c_rest[2], c[:, 2 * CHUNK : 3 * CHUNK - SHARE])
         load_rows(c_share[3], c[:, 3 * CHUNK : 3 * CHUNK + SHARE])
         load_rows(c_rest[3], c[:, 3 * CHUNK + SHARE : 4 * CHUNK])
 
         ts_window()
-        pieces["u", 0] = handed(0)
+        pieces["u", 0] = pieces[0, 0] = pieces[1, 0] = strip[:, 0:CHUNK, :]
         for h in range(2):
-            round_on_gpsimd(pieces["u", 0][:, h * (M // 2) : (h + 1) * (M // 2), :], u_half[h][:])
+            round_on_gpsimd(strip[:, h * HALF : (h + 1) * HALF, :], u_half[h][:])
         quantize("u", 0, M)
-        pieces[0, 0] = handed(0)
-        round_on_gpsimd(pieces[0, 0][:, 0:HALF, :], c_raw[0][:, :, 0:HALF])
-        round_on_scalar(pieces[0, 0][:, HALF:CHUNK, :], c_raw[0][:, :, HALF:CHUNK])
+        round_on_gpsimd(strip[:, 0:HALF, :], c_raw[0][:, :, 0:HALF])
+        round_on_scalar(strip[:, HALF:CHUNK, :], c_raw[0][:, :, HALF:CHUNK])
         bias = turn_bias()
-        pick_ts(0, 2)
-        ts_to_partitions(0)
+        pick_ts(0, 1024)
+        ts_to_partitions(0, 4)
         quantize(0, 0, CHUNK)
-
         open_sums(turned_dense_pass, 0)
-        pick_ts(2)
-        pieces[1, 0] = handed(0)
-        for part, (lo, hi) in zip(c_part, cuts):
-            round_on_gpsimd(pieces[1, 0][:, lo:hi, :], part[:])
+        pick_ts(1024, 1536)
+        for h in range(2):
+            round_on_gpsimd(strip[:, h * HALF : (h + 1) * HALF, :], c_half[1, h][:])
         pick_words(0)
         close_sums(turned_table_pass, 0)
         for a in range(BLOCKS):
             scale_turned(0, a)
-
         pick_words(1)
         open_sums(table_pass, 1, (0, 1))
         pick_words(2, 2)
-        quantize(1, 0, CHUNK)
-        pieces[2, 0] = handed(SHARE)
+        for m in range(N_TILES):
+            turn_back(0, m, (1, 0))
+        for m in range(N_TILES):
+            turn_back(0, m, (2,))
+        for m in range(N_TILES):
+            turn_back(0, m, (3,))
+        open_sums(table_pass, 1, (2, 3))
+        quantize(1, 0, CHUNK, "ts_col0")
+        pieces[2, 0] = strip[:, SHARE : SHARE + CHUNK, :]
         round_on_gpsimd(pieces[2, 0][:, 0 : CHUNK - SHARE, :], c_rest[2][:])
         round_on_scalar(pieces[2, 0][:, CHUNK - SHARE : CHUNK, :], c_share[2][:])
-        finish(0, 0, turn_back(0, 0, (1, 0, 2, 3)))
-        open_sums(table_pass, 1, (2, 3))
-        finish(0, 1, turn_back(0, 1))
-        close_sums(dense_pass, 1, (0, 1))
-        for m in range(2, N_TILES):
-            finish(0, m, turn_back(0, m))
-
-        close_sums(dense_pass, 1, (2, 3))
-        open_sums(table_pass, 2)
-
-        pick_ts(3)
+        first_results = kept([P, N_TILES, CHUNK], F32, "first_results", "c_share2")
+        for m in range(4):
+            finish(0, m, back[0, m], result=first_results[:, m, :])
+        close_sums(dense_pass, 1)
+        open_sums(table_pass, 2, (0, 1, 2))
+        pick_ts(1536, 2048)
+        pieces[3, 0] = strip[:, 0:CHUNK, :]
         for m in range(2):
             finish(1, m, product(1, m))
-        pieces[3, 0] = handed(0)
         round_on_scalar(pieces[3, 0][:, 0:SHARE, :], c_share[3][:])
         quantize(2, 0, CHUNK)
         round_on_gpsimd(pieces[3, 0][:, SHARE:CHUNK, :], c_rest[3][:])
-        close_sums(dense_pass, 2)
+        close_sums(dense_pass, 2, (0, 1, 2))
         for m in range(2, N_TILES):
             finish(1, m, product(1, m))
+        open_sums(table_pass, 2, (3,))
+        close_sums(dense_pass, 2, (3,))
         open_sums(table_pass, 3)
         for m in range(2):
             finish(2, m, product(2, m))

@@ -70,10 +70,10 @@ def tile_list_tabts_silu_kernel(tc, tab_words, tab_scales, w4_words, w4_scales, 
         w4_w = kept([P, 2 * M // 4], I32, "w4_w")
         tab_w = kept([P, T], I32, "tab_w")
         u_half = [kept([P, PACK, M // 2], F32, "u_half%d" % h) for h in range(2)]
-        c_raw = {i: kept([P, PACK, CHUNK], F32, "c_raw%d" % i) for i in (0,)}
+        c_raw = {i: kept([P, PACK, CHUNK], F32, "c_raw%d" % i) for i in (0, 3)}
         c_half = {(1, h): kept([P, PACK, HALF], F32, "c_half1_%d" % h) for h in range(2)}
-        c_share = {i: kept([P, PACK, SHARE], F32, "c_share%d" % i) for i in (2, 3)}
-        c_rest = {i: kept([P, PACK, CHUNK - SHARE], F32, "c_rest%d" % i) for i in (2, 3)}
+        c_share = {i: kept([P, PACK, SHARE], F32, "c_share%d" % i) for i in (2,)}
+        c_rest = {i: kept([P, PACK, CHUNK - SHARE], F32, "c_rest%d" % i) for i in (2,)}
         w4_bytes = w4_w[:].bitcast(U8)
         w4_plane = w4_s[:].bitcast(U8)
         codes, pieces, words, ts_col, blocks, sums, back = {}, {}, {}, {}, {}, {}, {}
@@ -261,8 +261,7 @@ def tile_list_tabts_silu_kernel(tc, tab_words, tab_scales, w4_words, w4_scales, 
         load_half(1, 1)
         load_rows(c_share[2], c[:, 3 * CHUNK - SHARE : 3 * CHUNK])
         load_rows(c_rest[2], c[:, 2 * CHUNK : 3 * CHUNK - SHARE])
-        load_rows(c_share[3], c[:, 3 * CHUNK : 3 * CHUNK + SHARE])
-        load_rows(c_rest[3], c[:, 3 * CHUNK + SHARE : 4 * CHUNK])
+        load_c(3)
 
         ts_window()
         pieces["u", 0] = pieces[0, 0] = pieces[1, 0] = strip[:, 0:CHUNK, :]
@@ -306,9 +305,9 @@ def tile_list_tabts_silu_kernel(tc, tab_words, tab_scales, w4_words, w4_scales, 
         pieces[3, 0] = strip[:, 0:CHUNK, :]
         for m in range(2):
             finish(1, m, product(1, m))
-        round_on_scalar(pieces[3, 0][:, 0:SHARE, :], c_share[3][:])
+        round_on_scalar(pieces[3, 0][:, 0:SHARE, :], c_raw[3][:, :, 0:SHARE])
         quantize(2, 0, CHUNK)
-        round_on_gpsimd(pieces[3, 0][:, SHARE:CHUNK, :], c_rest[3][:])
+        round_on_gpsimd(pieces[3, 0][:, SHARE:CHUNK, :], c_raw[3][:, :, SHARE:CHUNK])
         close_sums(dense_pass, 2, (0, 1, 2))
         for m in range(2, N_TILES):
             finish(1, m, product(1, m))

@@ -58,9 +58,9 @@ def tile_list_tabts_silu_kernel(tc, tab_words, tab_scales, w4_words, w4_scales, 
         tab_s = kept([P, T // 4], I32, "tab_s")
         ts_cols = kept([P, TS_PER_PARTITION], F32, "ts_cols")
         ts_all = kept([P, T], F32, "ts_all")
-        constants = kept([P, P + 1], F32, "constants")
-        ones, quadrant = constants[:, 0:P], constants[:, P : P + 1]
-        ramp = kept([P, P], F32, "ramp")
+        constants = kept([P, P + 2], F32, "constants")
+        ones, quadrant = constants[:, 0 : P + 1], constants[:, P + 1 : P + 2]
+        ramp = kept([P, P + 1], F32, "ramp")
         lane = kept([P, QUADRANT], F32, "lane")
         ident, plane_s, w4_s, b_rows = [
             keep.tile(shape, dtype, name=name, tag="set_up", bufs=4, align_bytes=ALIGN)
@@ -81,11 +81,11 @@ def tile_list_tabts_silu_kernel(tc, tab_words, tab_scales, w4_words, w4_scales, 
 
         def identity():
             nc.vector.memset(constants[:], 1.0)
-            for q in range(P // QUADRANT):
-                nc.gpsimd.memset(quadrant[QUADRANT * q : QUADRANT * (q + 1), :], float(QUADRANT * q))
+            for q in range(1, P // QUADRANT):
+                nc.gpsimd.memset(quadrant[QUADRANT * q : QUADRANT * (q + 1), :], float(QUADRANT * q + 1))
             nc.vector.tensor_tensor_scan(ramp[:], ones[:], ones[:], 0.0, ALU.mult, ALU.add)
             nc.vector.transpose(lane[:], ramp[:, 0:QUADRANT])
-            nc.vector.tensor_scalar(ident[:], ramp[:], lane[:, 0:1], quadrant[:], ALU.subtract, ALU.is_equal)
+            nc.vector.tensor_scalar(ident[:], ramp[:, 1 : P + 1], lane[:, 0:1], quadrant[:], ALU.subtract, ALU.is_equal)
 
         def load_rows(dst, src):
             nc.sync.dma_start(dst[:], src.rearrange("(p i) j -> p i j", i=PACK))
@@ -253,9 +253,9 @@ def tile_list_tabts_silu_kernel(tc, tab_words, tab_scales, w4_words, w4_scales, 
         load_c(0)
         for r in range(PACK):
             nc.sync.dma_start(w4_s[r:P:QUADRANT, :], w4_scales[0][r:GROUP:PACK, :].bitcast(I32))
-        nc.sync.dma_start(b_rows[0:N_TILES, :], b.rearrange("(m p) -> m p", p=P))
         nc.sync.dma_start(tab_w[:], tab_words[0].rearrange("p t i -> p (t i)").bitcast(I32))
         nc.sync.dma_start(w4_w[:], w4_words[0].bitcast(I32))
+        nc.sync.dma_start(b_rows[0:N_TILES, :], b.rearrange("(m p) -> m p", p=P))
         pick_scales()
         load_half(1, 0)
         load_half(1, 1)
@@ -270,7 +270,6 @@ def tile_list_tabts_silu_kernel(tc, tab_words, tab_scales, w4_words, w4_scales, 
         quantize("u", 0, M)
         round_on_gpsimd(strip[:, 0:HALF, :], c_raw[0][:, :, 0:HALF])
         round_on_scalar(strip[:, HALF:CHUNK, :], c_raw[0][:, :, HALF:CHUNK])
-        bias = turn_bias()
         pick_ts(0, 1024)
         ts_to_partitions(0, 4)
         quantize(0, 0, CHUNK)
@@ -285,6 +284,7 @@ def tile_list_tabts_silu_kernel(tc, tab_words, tab_scales, w4_words, w4_scales, 
         pick_words(1)
         open_sums(table_pass, 1, (0, 1))
         pick_words(2, 2)
+        bias = turn_bias()
         for m in range(N_TILES):
             turn_back(0, m, (1, 0))
         for m in range(N_TILES):
@@ -296,9 +296,10 @@ def tile_list_tabts_silu_kernel(tc, tab_words, tab_scales, w4_words, w4_scales, 
         pieces[2, 0] = strip[:, SHARE : SHARE + CHUNK, :]
         round_on_gpsimd(pieces[2, 0][:, 0 : CHUNK - SHARE, :], c_rest[2][:])
         round_on_scalar(pieces[2, 0][:, CHUNK - SHARE : CHUNK, :], c_share[2][:])
-        first_results = kept([P, N_TILES, CHUNK], F32, "first_results", "c_share2")
-        for m in range(4):
-            finish(0, m, back[0, m], result=first_results[:, m, :])
+        finish(0, 0, back[0, 0])
+        first_results = kept([P, N_TILES - 1, CHUNK], F32, "first_results", "c_share2")
+        for m in range(1, N_TILES):
+            finish(0, m, back[0, m], result=first_results[:, m - 1, :])
         close_sums(dense_pass, 1)
         open_sums(table_pass, 2, (0, 1, 2))
         pick_ts(1536, 2048)
@@ -320,7 +321,5 @@ def tile_list_tabts_silu_kernel(tc, tab_words, tab_scales, w4_words, w4_scales, 
         close_sums(dense_pass, 3)
         for m in range(2, N_TILES):
             finish(2, m, product(2, m))
-        for m in range(N_TILES - 1):
+        for m in range(N_TILES):
             finish(3, m, product(3, m))
-        for lo in (0, HALF):
-            finish(3, N_TILES - 1, product(3, N_TILES - 1, lo, lo + HALF), lo, lo + HALF)

@@ -21,7 +21,6 @@ QUADRANT = 32
 PACK = 4
 GROUP = 16
 CHUNK = 512
-N_CHUNKS = S // CHUNK
 N_TILES = M // P
 BLOCKS = CHUNK // P
 HALF = CHUNK // 2
@@ -69,15 +68,15 @@ def tile_list_tabts_silu_kernel(tc, tab_words, tab_scales, w4_words, w4_scales, 
         warm = kept([P, 1], F32, "warm")
         w4_w = kept([P, 2 * M // 4], I32, "w4_w")
         tab_w = kept([P, T], I32, "tab_w")
-        u_half = [kept([P, PACK, M // 2], F32, "u_half%d" % h) for h in range(2)]
-        c_raw = {i: kept([P, PACK, CHUNK], F32, "c_raw%d" % i) for i in (0, 3)}
-        c_half = {(1, h): kept([P, PACK, HALF], F32, "c_half1_%d" % h) for h in range(2)}
-        c_share = {i: kept([P, PACK, SHARE], F32, "c_share%d" % i) for i in (2,)}
-        c_rest = {i: kept([P, PACK, CHUNK - SHARE], F32, "c_rest%d" % i) for i in (2,)}
         w4_bytes = w4_w[:].bitcast(U8)
         w4_plane = w4_s[:].bitcast(U8)
-        codes, pieces, words, ts_col, blocks, sums, back = {}, {}, {}, {}, {}, {}, {}
-        picked_t = []
+        table_plane = plane_s[:].bitcast(U8)
+        raw, codes, words, picked = {"u": [], "c": []}, {"u": [], "c": []}, [], []
+        ts_col, scaled_blocks = {}, {}
+
+        def piece(pieces, lo, hi):
+            first, last, *tiles = [x for x in pieces if x[0] <= lo and hi <= x[1]][0]
+            return [t[:, lo - first : hi - first] if len(t.shape) == 2 else t[:, :, lo - first : hi - first] for t in tiles]
 
         def identity():
             nc.vector.memset(constants[:], 1.0)
@@ -87,14 +86,11 @@ def tile_list_tabts_silu_kernel(tc, tab_words, tab_scales, w4_words, w4_scales, 
             nc.vector.transpose(lane[:], ramp[:, 0:QUADRANT])
             nc.vector.tensor_scalar(ident[:], ramp[:, 1 : P + 1], lane[:, 0:1], quadrant[:], ALU.subtract, ALU.is_equal)
 
-        def load_rows(dst, src):
-            nc.sync.dma_start(dst[:], src.rearrange("(p i) j -> p i j", i=PACK))
-
-        def load_half(i, h):
-            load_rows(c_half[i, h], c[:, i * CHUNK + h * HALF : i * CHUNK + (h + 1) * HALF])
-
-        def load_c(i):
-            load_rows(c_raw[i], c[:, i * CHUNK : (i + 1) * CHUNK])
+        def load(key, lo, hi):
+            src = {"u": u, "c": c}[key]
+            tile = kept([P, PACK, hi - lo], F32, "raw_%s%d" % (key, lo))
+            nc.sync.dma_start(tile[:], src[:, lo:hi].rearrange("(p i) j -> p i j", i=PACK))
+            raw[key].append((lo, hi, tile))
 
         def ts_window():
             for g in range(T // CHUNK):
@@ -116,127 +112,104 @@ def tile_list_tabts_silu_kernel(tc, tab_words, tab_scales, w4_words, w4_scales, 
             for r in range(PACK):
                 nc.sync.dma_start(plane_s[r:P:QUADRANT, :], rows[P - GROUP + r : P : PACK, :].bitcast(I32))
 
-        def picked_s(i):
-            return plane_s[:].bitcast(U8)[:, i * CHUNK : (i + 1) * CHUNK]
-
-        def pick_words(i, n=1):
-            picked = by_vector([P, n * CHUNK], U32, "words%d" % i)
-            nc.vector.tensor_copy(picked[:], tab_w[:].bitcast(U32).indirect(listed(i * CHUNK, (i + n) * CHUNK)))
-            for k in range(n):
-                words[i + k] = picked[:, k * CHUNK : (k + 1) * CHUNK]
+        def pick_words(lo, hi):
+            tile = by_vector([P, hi - lo], U32, "words%d" % lo)
+            nc.vector.tensor_copy(tile[:], tab_w[:].bitcast(U32).indirect(listed(lo, hi)))
+            words.append((lo, hi, tile))
 
         def pick_ts(lo, hi):
-            picked = by_vector([P, hi - lo], F32, "picked%d" % lo)
-            nc.vector.tensor_copy(picked[:], ts_all[:].indirect(listed(lo, hi)))
-            picked_t.append((lo, hi, picked))
+            tile = by_vector([P, hi - lo], F32, "picked%d" % lo)
+            nc.vector.tensor_copy(tile[:], ts_all[:].indirect(listed(lo, hi)))
+            picked.append((lo, hi, tile))
 
-        def picked_ts(lo, hi):
-            first, _, picked = [piece for piece in picked_t if piece[0] <= lo and hi <= piece[1]][0]
-            return picked[:, lo - first : hi - first]
+        def round_on_gpsimd(at, key, lo, hi):
+            dst, (src,) = strip[:, at : at + hi - lo, :], piece(raw[key], lo, hi)
+            nc.gpsimd.tensor_scalar(dst.rearrange("p (g e) i -> p g i e", e=4), src.rearrange("p i (g e) -> p g i e", e=4), 1.0, 0.0, ALU.mult, ALU.add)
 
-        def round_on_gpsimd(dst, raw):
-            nc.gpsimd.tensor_scalar(dst.rearrange("p (g e) i -> p g i e", e=4), raw.rearrange("p i (g e) -> p g i e", e=4), 1.0, 0.0, ALU.mult, ALU.add)
+        def round_on_scalar(at, key, lo, hi):
+            dst, (src,) = strip[:, at : at + hi - lo, :], piece(raw[key], lo, hi)
+            nc.scalar.copy(dst.rearrange("p (g e) i -> p g i e", e=4), src.rearrange("p i (g e) -> p g i e", e=4))
 
-        def round_on_scalar(dst, raw):
-            nc.scalar.copy(dst.rearrange("p (g e) i -> p g i e", e=4), raw.rearrange("p i (g e) -> p g i e", e=4))
+        def round_on_vector(at, key, lo, hi):
+            dst, (src,) = strip[:, at : at + hi - lo, :], piece(raw[key], lo, hi)
+            nc.vector.tensor_copy(dst.rearrange("p (g e) i -> p g i e", e=4), src.rearrange("p i (g e) -> p g i e", e=4))
 
-        def quantize(key, lo, hi, tag=None):
-            made = by_vector([P, hi - lo], U32, "codes_%s" % key)
-            plane = kept([P, hi - lo], U8, "scales_%s_%d" % (key, lo), tag)
-            nc.vector.quantize_mx(out=made[:].bitcast(FP8X4), scales=plane[:], in_=pieces[key, lo][:].rearrange("p w i -> p (w i)"))
-            codes.setdefault(key, []).append((lo, hi, made, plane))
+        def quantize(at, key, lo, hi, tag=None):
+            made = by_vector([P, hi - lo], U32, "codes_%s%d" % (key, lo))
+            plane = kept([P, hi - lo], U8, "scales_%s%d" % (key, lo), tag)
+            nc.vector.quantize_mx(out=made[:].bitcast(FP8X4), scales=plane[:], in_=strip[:, at : at + hi - lo, :].rearrange("p w i -> p (w i)"))
+            codes[key].append((lo, hi, made, plane))
 
-        def stationary(key, at):
-            lo, _, made, plane = [piece for piece in codes[key] if piece[0] <= at < piece[1]][0]
-            return made[:, at - lo : at - lo + P].bitcast(FP8X4), plane[:, at - lo : at - lo + P]
+        def operand(key, lo, hi):
+            if key == "w4":
+                return w4_bytes[:, 2 * lo : 2 * hi].bitcast(FP4X4), w4_plane[:, lo:hi]
+            if key == "table":
+                return piece(words, lo, hi)[0].bitcast(FP8X4), table_plane[:, lo:hi]
+            made, plane = piece(codes[key], lo, hi)
+            return made.bitcast(FP8X4), plane
 
-        def dense(acc, fixed, moving, first):
-            lhs, lhs_scale = fixed
-            for k, (lo, hi, made, plane) in enumerate(moving):
-                nc.tensor.matmul_mx(out=acc[:, lo:hi], lhsT=lhs, lhsT_scale=lhs_scale, rhs=made[:].bitcast(FP8X4), rhs_scale=plane[:],
-                                    start=first and k == 0, stop=not first and k == len(moving) - 1)
+        def mx(acc, fixed, moving, start, stop):
+            nc.tensor.matmul_mx(out=acc, lhsT=fixed[0], lhsT_scale=fixed[1], rhs=moving[0], rhs_scale=moving[1], start=start, stop=stop)
 
-        def table_pass(i, m, acc, first):
-            nc.tensor.matmul_mx(out=acc[:], lhsT=w4_bytes[:, 2 * m * P : 2 * (m + 1) * P].bitcast(FP4X4), lhsT_scale=w4_plane[:, m * P : (m + 1) * P],
-                                rhs=words[i][:].bitcast(FP8X4), rhs_scale=picked_s(i), start=first, stop=not first)
+        def widths(lo, hi):
+            cuts = [lo]
+            for w in (CHUNK, HALF, P):
+                if hi - cuts[-1] >= w:
+                    cuts.append(cuts[-1] + w)
+            return list(zip(cuts, cuts[1:]))
 
-        def dense_pass(i, m, acc, first):
-            dense(acc, stationary("u", m * P), codes[i], first)
+        def direct(acc, pair, m, lo, hi, start, stop):
+            parts = widths(lo, hi)
+            for k, (x, y) in enumerate(parts):
+                mx(acc[:, x - lo : y - lo], operand(pair[0], m * P, (m + 1) * P), operand(pair[1], x, y), start and k == 0, stop and k == len(parts) - 1)
 
-        def narrow_dense_pass(i, m, acc, first):
-            _, _, made, plane = codes[i][0]
-            dense(acc, stationary("u", m * P), [(lo, hi, made[:, lo:hi], plane[:, lo:hi]) for lo, hi in ((P, HALF), (HALF, CHUNK))], first)
+        def turned(acc, pair, a, start, stop):
+            mx(acc[:], operand(pair[1], a * P, (a + 1) * P), operand(pair[0], 0, M), start, stop)
 
-        def turned_table_pass(i, a, acc, first):
-            cols = slice(a * P, (a + 1) * P)
-            nc.tensor.matmul_mx(out=acc[:], lhsT=words[i][:, cols].bitcast(FP8X4), lhsT_scale=picked_s(i)[:, cols],
-                                rhs=w4_bytes.bitcast(FP4X4), rhs_scale=w4_plane, start=first, stop=not first)
+        TABLE, DENSE = ("w4", "table"), ("u", "c")
 
-        def turned_dense_pass(i, a, acc, first):
-            dense(acc, stationary(i, a * P), codes["u"], first)
-
-        def open_sums(one_pass, i, tiles=range(N_TILES)):
-            for m in tiles:
-                sums[i, m] = bank("acc")
-                one_pass(i, m, sums[i, m], True)
-
-        def close_sums(one_pass, i, tiles=range(N_TILES)):
-            for m in tiles:
-                one_pass(i, m, sums[i, m], False)
-
-        def ts_to_partitions(first, n):
-            turned = bank("turned")
+        def ts_to_partitions(first, n, early):
+            held = bank("turned")
             for a in range(n):
-                nc.tensor.transpose(turned[:, a * STEP : a * STEP + P], picked_ts((first + a) * P, (first + a + 1) * P), ident[:])
-            for lo, hi in ((0, EARLY), (EARLY, n)):
-                columns = kept([P, hi - lo], F32, "ts_col%d" % lo)
-                nc.scalar.copy(columns[:], turned[:, lo * STEP : hi * STEP : STEP])
+                nc.tensor.transpose(held[:, a * STEP : a * STEP + P], piece(picked, (first + a) * P, (first + a + 1) * P)[0], ident[:])
+            for lo, hi in ((0, early), (early, n)):
+                columns = kept([P, hi - lo], F32, "ts_col%d" % (first + lo))
+                nc.scalar.copy(columns[:], held[:, lo * STEP : hi * STEP : STEP])
                 for a in range(lo, hi):
-                    ts_col[divmod(first + a, BLOCKS)] = columns[:, a - lo : a - lo + 1]
+                    ts_col[first + a] = columns[:, a - lo : a - lo + 1]
 
         def turn_bias():
-            turned = bank("turned")
-            nc.tensor.transpose(turned[:, 0:P], b_rows[:], ident[:])
+            held = bank("turned")
+            nc.tensor.transpose(held[:, 0:P], b_rows[:], ident[:])
             columns = by_scalar([P, N_TILES], F32, "bias")
-            nc.scalar.copy(columns[:], turned[:, 0:N_TILES])
+            nc.scalar.copy(columns[:], held[:, 0:N_TILES])
             return columns
 
-        def scale_turned(i, a):
-            blocks[i, a] = by_scalar([P, M], F32, "block%d_%d" % (i, a))
-            nc.scalar.activation(blocks[i, a][:], sums[i, a][:], ACT.Copy, scale=ts_col[i, a])
+        def scale_turned(a, acc):
+            scaled_blocks[a] = by_scalar([P, M], F32, "block%d" % a)
+            nc.scalar.activation(scaled_blocks[a][:], acc[:], ACT.Copy, scale=ts_col[a])
 
-        def scale_turned_on_vector(i, a):
-            blocks[i, a] = by_vector([P, M], F32, "block%d_%d" % (i, a))
-            nc.vector.tensor_scalar(blocks[i, a][:], sums[i, a][:], ts_col[i, a], None, ALU.mult)
+        def turn_back(dst, a, m):
+            nc.tensor.transpose(dst, scaled_blocks[a][:, m * P : (m + 1) * P], ident[:])
 
-        def turn_back(i, m, order):
-            if (i, m) not in back:
-                back[i, m] = bank("turned")
-            for a in order:
-                nc.tensor.transpose(back[i, m][:, a * P : (a + 1) * P], blocks[i, a][:, m * P : (m + 1) * P], ident[:])
-            return back[i, m]
-
-        def product(i, m, lo=0, hi=CHUNK):
+        def product(acc, lo, hi):
             scaled = by_vector([P, hi - lo], F32, "scaled")
-            nc.vector.tensor_tensor(scaled[:], sums[i, m][:, lo:hi], picked_ts(i * CHUNK + lo, i * CHUNK + hi), ALU.mult)
+            nc.vector.tensor_tensor(scaled[:], acc[:, 0 : hi - lo], piece(picked, lo, hi)[0], ALU.mult)
             return scaled
 
-        def finish(i, m, src, lo=0, hi=CHUNK, result=None):
-            result = by_scalar([P, hi - lo], F32, "result") if result is None else result
-            nc.scalar.activation(result[:], src[:], ACT.Silu, bias=bias[:, m : m + 1])
-            nc.sync.dma_start(out[m * P : (m + 1) * P, i * CHUNK + lo : i * CHUNK + hi], result[:])
+        def silu(dst, src, m):
+            nc.scalar.activation(dst, src, ACT.Silu, bias=bias[:, m : m + 1])
 
-        def turn_back_block(i, a):
-            turned = bank("turned")
-            for m in range(N_TILES):
-                nc.tensor.transpose(turned[:, m * P : (m + 1) * P], blocks[i, a][:, m * P : (m + 1) * P], ident[:])
-            return turned
+        def store(m, lo, hi, src):
+            nc.sync.dma_start(out[m * P : (m + 1) * P, lo:hi], src)
 
-        def finish_split(i, m, turned, src):
-            result = by_scalar([P, CHUNK], F32, "result")
-            nc.scalar.activation(result[:, P:CHUNK], src[:], ACT.Silu, bias=bias[:, m : m + 1])
-            nc.scalar.activation(result[:, 0:P], turned[:, m * P : (m + 1) * P], ACT.Silu, bias=bias[:, m : m + 1])
-            nc.sync.dma_start(out[m * P : (m + 1) * P, i * CHUNK : (i + 1) * CHUNK], result[:])
+        def store_tiles(m, n, lo, hi, src):
+            nc.sync.dma_start(out[m * P : (m + n) * P, lo:hi].rearrange("(t p) j -> p t j", p=P), src)
+
+        def finish(m, lo, hi, src):
+            result = by_scalar([P, hi - lo], F32, "result")
+            silu(result[:], src[:], m)
+            store(m, lo, hi, result[:])
 
         identity()
         nc.vector.memset(tab_s[0 : P - GROUP, :], 0)
@@ -248,78 +221,108 @@ def tile_list_tabts_silu_kernel(tc, tab_words, tab_scales, w4_words, w4_scales, 
         nc.sync.dma_start(ts_cols[:], ts[0].rearrange("(p a) -> p a", p=P))
         nc.sync.dma_start(offsets[:], offs)
         nc.sync.dma_start(tab_s[P - GROUP : P, :], tab_scales[0].bitcast(I32))
-        for h in range(2):
-            load_rows(u_half[h], u[:, h * (M // 2) : (h + 1) * (M // 2)])
-        load_c(0)
+        load("u", 0, HALF)
+        load("u", HALF, M)
+        load("c", 0, CHUNK)
         for r in range(PACK):
             nc.sync.dma_start(w4_s[r:P:QUADRANT, :], w4_scales[0][r:GROUP:PACK, :].bitcast(I32))
         nc.sync.dma_start(tab_w[:], tab_words[0].rearrange("p t i -> p (t i)").bitcast(I32))
         nc.sync.dma_start(w4_w[:], w4_words[0].bitcast(I32))
+        load("c", 512, 640)
         nc.sync.dma_start(b_rows[0:N_TILES, :], b.rearrange("(m p) -> m p", p=P))
         pick_scales()
-        load_half(1, 0)
-        load_half(1, 1)
-        load_rows(c_share[2], c[:, 3 * CHUNK - SHARE : 3 * CHUNK])
-        load_rows(c_rest[2], c[:, 2 * CHUNK : 3 * CHUNK - SHARE])
-        load_c(3)
+        load("c", 640, 832)
+        load("c", 832, 1024)
+        load("c", 1536 - SHARE, 1536)
+        load("c", 1024, 1536 - SHARE)
+        load("c", 1536, 2048)
 
         ts_window()
-        pieces["u", 0] = pieces[0, 0] = pieces[1, 0] = strip[:, 0:CHUNK, :]
-        for h in range(2):
-            round_on_gpsimd(strip[:, h * HALF : (h + 1) * HALF, :], u_half[h][:])
-        quantize("u", 0, M)
-        round_on_gpsimd(strip[:, 0:HALF, :], c_raw[0][:, :, 0:HALF])
-        round_on_scalar(strip[:, HALF:CHUNK, :], c_raw[0][:, :, HALF:CHUNK])
+        round_on_gpsimd(0, "u", 0, HALF)
+        round_on_gpsimd(HALF, "u", HALF, M)
+        quantize(0, "u", 0, M)
+        round_on_gpsimd(0, "c", 0, HALF)
+        round_on_scalar(HALF, "c", HALF, CHUNK)
         pick_ts(0, 1024)
-        ts_to_partitions(0, 4)
-        quantize(0, 0, CHUNK)
-        open_sums(turned_dense_pass, 0)
+        ts_to_partitions(0, 4, EARLY)
+        quantize(0, "c", 0, 512)
+        sums = {}
+        for a in range(2):
+            sums[a] = bank("acc")
+            turned(sums[a], DENSE, a, True, False)
+        round_on_scalar(0, "c", 512, 640)
+        round_on_gpsimd(128, "c", 640, 832)
+        round_on_gpsimd(320, "c", 832, 1024)
         pick_ts(1024, 1536)
-        for h in range(2):
-            round_on_gpsimd(strip[:, h * HALF : (h + 1) * HALF, :], c_half[1, h][:])
-        pick_words(0)
-        close_sums(turned_table_pass, 0)
+        pick_words(0, 512)
+        for a in range(2):
+            turned(sums[a], TABLE, a, False, True)
+        for a in range(2, 4):
+            sums[a] = bank("acc")
+            turned(sums[a], DENSE, a, True, False)
+            turned(sums[a], TABLE, a, False, True)
         for a in range(BLOCKS):
-            scale_turned(0, a)
-        pick_words(1)
-        open_sums(table_pass, 1, (0, 1))
-        pick_words(2, 2)
+            scale_turned(a, sums[a])
+        pick_words(512, 1024)
+        pick_words(1024, 2048)
+        acc1 = {}
+        for m in range(2):
+            acc1[m] = bank("acc")
+            direct(acc1[m], TABLE, m, 512, 1024, True, False)
         bias = turn_bias()
+        back = {}
         for m in range(N_TILES):
-            turn_back(0, m, (1, 0))
+            back[m] = bank("turned")
+            for a in (1, 0):
+                turn_back(back[m][:, a * P : (a + 1) * P], a, m)
+        for a in (2, 3):
+            for m in range(N_TILES):
+                turn_back(back[m][:, a * P : (a + 1) * P], a, m)
+        for m in range(2, 4):
+            acc1[m] = bank("acc")
+            direct(acc1[m], TABLE, m, 512, 1024, True, False)
+        quantize(0, "c", 512, 1024, "ts_col0")
+        round_on_gpsimd(SHARE, "c", 1024, 1536 - SHARE)
+        round_on_scalar(CHUNK, "c", 1536 - SHARE, 1536)
+        first = kept([P, N_TILES, CHUNK], F32, "first", "raw_c0")
         for m in range(N_TILES):
-            turn_back(0, m, (2,))
+            silu(first[:, m, :], back[m][:], m)
+            if m % 2:
+                store_tiles(m - 1, 2, 0, CHUNK, first[:, m - 1 : m + 1, :])
         for m in range(N_TILES):
-            turn_back(0, m, (3,))
-        open_sums(table_pass, 1, (2, 3))
-        quantize(1, 0, CHUNK, "ts_col0")
-        pieces[2, 0] = strip[:, SHARE : SHARE + CHUNK, :]
-        round_on_gpsimd(pieces[2, 0][:, 0 : CHUNK - SHARE, :], c_rest[2][:])
-        round_on_scalar(pieces[2, 0][:, CHUNK - SHARE : CHUNK, :], c_share[2][:])
-        finish(0, 0, back[0, 0])
-        first_results = kept([P, N_TILES - 1, CHUNK], F32, "first_results", "c_share2")
-        for m in range(1, N_TILES):
-            finish(0, m, back[0, m], result=first_results[:, m - 1, :])
-        close_sums(dense_pass, 1)
-        open_sums(table_pass, 2, (0, 1, 2))
+            direct(acc1[m], DENSE, m, 512, 1024, False, True)
+        acc2 = {}
+        for m in range(3):
+            acc2[m] = bank("acc")
+            direct(acc2[m], TABLE, m, 1024, 1536, True, False)
         pick_ts(1536, 2048)
-        pieces[3, 0] = strip[:, 0:CHUNK, :]
         for m in range(2):
-            finish(1, m, product(1, m))
-        round_on_scalar(pieces[3, 0][:, 0:SHARE, :], c_raw[3][:, :, 0:SHARE])
-        quantize(2, 0, CHUNK)
-        round_on_gpsimd(pieces[3, 0][:, SHARE:CHUNK, :], c_raw[3][:, :, SHARE:CHUNK])
-        close_sums(dense_pass, 2, (0, 1, 2))
-        for m in range(2, N_TILES):
-            finish(1, m, product(1, m))
-        open_sums(table_pass, 2, (3,))
-        close_sums(dense_pass, 2, (3,))
-        open_sums(table_pass, 3)
-        for m in range(2):
-            finish(2, m, product(2, m))
-        quantize(3, 0, CHUNK)
-        close_sums(dense_pass, 3)
-        for m in range(2, N_TILES):
-            finish(2, m, product(2, m))
+            finish(m, 512, 1024, product(acc1[m], 512, 1024))
+            if m == 1:
+                round_on_scalar(0, "c", 1536, 1536 + 160)
+        quantize(SHARE, "c", 1024, 1536)
+        round_on_gpsimd(160, "c", 1536 + 160, 2048)
+        for m in range(3):
+            direct(acc2[m], DENSE, m, 1024, 1536, False, True)
+        for m in range(2, 4):
+            finish(m, 512, 1024, product(acc1[m], 512, 1024))
+            if m == 1:
+                round_on_scalar(0, "c", 1536, 1536 + 160)
+        acc2[3] = bank("acc")
+        direct(acc2[3], TABLE, 3, 1024, 1536, True, False)
+        direct(acc2[3], DENSE, 3, 1024, 1536, False, True)
+        acc3 = {}
         for m in range(N_TILES):
-            finish(3, m, product(3, m))
+            acc3[m] = bank("acc")
+            direct(acc3[m], TABLE, m, 1536, 2048, True, False)
+        for m in range(2):
+            finish(m, 1024, 1536, product(acc2[m], 1024, 1536))
+            if m == -3:
+                round_on_scalar(0, "c", 1536, 1536 + 160)
+        quantize(0, "c", 1536, 2048)
+        for m in range(N_TILES):
+            direct(acc3[m], DENSE, m, 1536, 2048, False, True)
+        for m in range(2, 4):
+            finish(m, 1024, 1536, product(acc2[m], 1024, 1536))
+        for m in range(N_TILES):
+            finish(m, 1536, 2048, product(acc3[m], 1536, 2048))

from contextlib import ExitStack

import concourse.mybir as mybir

K, M, T, S = 512, 512, 4096, 2048
FLOPS = 2 * 2 * K * M * S

F32 = mybir.dt.float32
BF16 = mybir.dt.bfloat16
I32 = mybir.dt.int32
U32 = mybir.dt.uint32
U16 = mybir.dt.uint16
U8 = mybir.dt.uint8
FP8X4 = mybir.dt.float8_e4m3fn_x4
FP4X4 = mybir.dt.float4_e2m1fn_x4
ACT = mybir.ActivationFunctionType
ALU = mybir.AluOpType

P = 128
QUADRANT = 32
PACK = 4
GROUP = 16
CHUNK = 512
N_TILES = M // P
BLOCKS = CHUNK // P
HALF = CHUNK // 2
STEP = 64
EARLY = 3
SHARE = 160
TS_PER_PARTITION = T // P
BANKS = 8
ALIGN = 512
VECTOR_TILES = 23
SCALAR_TILES = 13


def tile_list_tabts_silu_kernel(tc, tab_words, tab_scales, w4_words, w4_scales, c, u, ts, b, offs, out):
    nc = tc.nc
    with ExitStack() as ctx:
        keep = ctx.enter_context(tc.tile_pool(name="keep", bufs=1))
        banks = ctx.enter_context(tc.psum_pool(name="banks", bufs=BANKS))

        def kept(shape, dtype, name, tag=None):
            return keep.tile(shape, dtype, name=name, tag=tag or name, align_bytes=ALIGN)

        def by_vector(shape, dtype, name):
            return keep.tile(shape, dtype, name=name, tag="by_vector", bufs=VECTOR_TILES, align_bytes=ALIGN)

        def by_scalar(shape, dtype, name):
            return keep.tile(shape, dtype, name=name, tag="by_scalar", bufs=SCALAR_TILES, align_bytes=ALIGN)

        def bank(name):
            return banks.tile([P, CHUNK], F32, name=name, tag="ring")

        strip = kept([P, SHARE + CHUNK, PACK], BF16, "strip")
        offsets = kept([P, S // GROUP], U16, "offsets")
        tab_s = kept([P, T // 4], I32, "tab_s")
        ts_cols = kept([P, TS_PER_PARTITION], F32, "ts_cols")
        ts_all = kept([P, T], F32, "ts_all")
        constants = kept([P, P + 2], F32, "constants")
        ones, quadrant = constants[:, 0 : P + 1], constants[:, P + 1 : P + 2]
        ramp = kept([P, P + 1], F32, "ramp")
        lane = kept([P, QUADRANT], F32, "lane")
        ident, plane_s, w4_s, b_rows = [
            keep.tile(shape, dtype, name=name, tag="set_up", bufs=4, align_bytes=ALIGN)
            for shape, dtype, name in (([P, P], F32, "ident"), ([P, S // 4], I32, "plane_s"), ([P, M // 4], I32, "w4_s"), ([P, P], F32, "b_rows"))
        ]
        warm = kept([P, 1], F32, "warm")
        w4_w = kept([P, 2 * M // 4], I32, "w4_w")
        tab_w = kept([P, T], I32, "tab_w")
        w4_bytes = w4_w[:].bitcast(U8)
        w4_plane = w4_s[:].bitcast(U8)
        table_plane = plane_s[:].bitcast(U8)
        raw, codes, words, picked = {"u": [], "c": []}, {"u": [], "c": []}, [], []
        ts_col, scaled_blocks = {}, {}

        def piece(pieces, lo, hi):
            first, last, *tiles = [x for x in pieces if x[0] <= lo and hi <= x[1]][0]
            return [t[:, lo - first : hi - first] if len(t.shape) == 2 else t[:, :, lo - first : hi - first] for t in tiles]

        def identity():
            nc.vector.memset(constants[:], 1.0)
            for q in range(1, P // QUADRANT):
                nc.gpsimd.memset(quadrant[QUADRANT * q : QUADRANT * (q + 1), :], float(QUADRANT * q + 1))
            nc.vector.tensor_tensor_scan(ramp[:], ones[:], ones[:], 0.0, ALU.mult, ALU.add)
            nc.vector.transpose(lane[:], ramp[:, 0:QUADRANT])
            nc.vector.tensor_scalar(ident[:], ramp[:, 1 : P + 1], lane[:, 0:1], quadrant[:], ALU.subtract, ALU.is_equal)

        def load(key, lo, hi):
            src = {"u": u, "c": c}[key]
            tile = kept([P, PACK, hi - lo], F32, "raw_%s%d" % (key, lo))
            nc.sync.dma_start(tile[:], src[:, lo:hi].rearrange("(p i) j -> p i j", i=PACK))
            raw[key].append((lo, hi, tile))

        def ts_window():
            for g in range(T // CHUNK):
                turned = bank("turned")
                for a in range(BLOCKS):
                    col = g * BLOCKS + a
                    nc.tensor.transpose(turned[:, a * P : (a + 1) * P], ts_cols[:, col : col + 1].to_broadcast([P, P]), ident[:])
                nc.scalar.copy(
                    ts_all[:].rearrange("q (p a) -> q p a", p=P)[:, :, g * BLOCKS : (g + 1) * BLOCKS],
                    turned[:].rearrange("q (a p) -> q p a", p=P),
                )

        def listed(lo, hi):
            return offsets[:, lo // GROUP : hi // GROUP]

        def pick_scales():
            rows = by_vector([P, S], U8, "rows")
            nc.vector.tensor_copy(rows[:], tab_s[:].bitcast(U8).indirect(offsets[:]))
            for r in range(PACK):
                nc.sync.dma_start(plane_s[r:P:QUADRANT, :], rows[P - GROUP + r : P : PACK, :].bitcast(I32))

        def pick_words(lo, hi):
            tile = by_vector([P, hi - lo], U32, "words%d" % lo)
            nc.vector.tensor_copy(tile[:], tab_w[:].bitcast(U32).indirect(listed(lo, hi)))
            words.append((lo, hi, tile))

        def pick_ts(lo, hi):
            tile = by_vector([P, hi - lo], F32, "picked%d" % lo)
            nc.vector.tensor_copy(tile[:], ts_all[:].indirect(listed(lo, hi)))
            picked.append((lo, hi, tile))

        def round_on_gpsimd(at, key, lo, hi):
            dst, (src,) = strip[:, at : at + hi - lo, :], piece(raw[key], lo, hi)
            nc.gpsimd.tensor_scalar(dst.rearrange("p (g e) i -> p g i e", e=4), src.rearrange("p i (g e) -> p g i e", e=4), 1.0, 0.0, ALU.mult, ALU.add)

        def round_on_scalar(at, key, lo, hi):
            dst, (src,) = strip[:, at : at + hi - lo, :], piece(raw[key], lo, hi)
            nc.scalar.copy(dst.rearrange("p (g e) i -> p g i e", e=4), src.rearrange("p i (g e) -> p g i e", e=4))

        def round_on_vector(at, key, lo, hi):
            dst, (src,) = strip[:, at : at + hi - lo, :], piece(raw[key], lo, hi)
            nc.vector.tensor_copy(dst.rearrange("p (g e) i -> p g i e", e=4), src.rearrange("p i (g e) -> p g i e", e=4))

        def quantize(at, key, lo, hi, tag=None):
            made = by_vector([P, hi - lo], U32, "codes_%s%d" % (key, lo))
            plane = kept([P, hi - lo], U8, "scales_%s%d" % (key, lo), tag)
            nc.vector.quantize_mx(out=made[:].bitcast(FP8X4), scales=plane[:], in_=strip[:, at : at + hi - lo, :].rearrange("p w i -> p (w i)"))
            codes[key].append((lo, hi, made, plane))

        def operand(key, lo, hi):
            if key == "w4":
                return w4_bytes[:, 2 * lo : 2 * hi].bitcast(FP4X4), w4_plane[:, lo:hi]
            if key == "table":
                return piece(words, lo, hi)[0].bitcast(FP8X4), table_plane[:, lo:hi]
            made, plane = piece(codes[key], lo, hi)
            return made.bitcast(FP8X4), plane

        def mx(acc, fixed, moving, start, stop):
            nc.tensor.matmul_mx(out=acc, lhsT=fixed[0], lhsT_scale=fixed[1], rhs=moving[0], rhs_scale=moving[1], start=start, stop=stop)

        def widths(lo, hi):
            cuts = [lo]
            for w in (CHUNK, HALF, P):
                if hi - cuts[-1] >= w:
                    cuts.append(cuts[-1] + w)
            return list(zip(cuts, cuts[1:]))

        def direct(acc, pair, m, lo, hi, start, stop):
            parts = widths(lo, hi)
            for k, (x, y) in enumerate(parts):
                mx(acc[:, x - lo : y - lo], operand(pair[0], m * P, (m + 1) * P), operand(pair[1], x, y), start and k == 0, stop and k == len(parts) - 1)

        def turned(acc, pair, a, start, stop):
            mx(acc[:], operand(pair[1], a * P, (a + 1) * P), operand(pair[0], 0, M), start, stop)

        TABLE, DENSE = ("w4", "table"), ("u", "c")

        def ts_to_partitions(first, n, early):
            held = bank("turned")
            for a in range(n):
                nc.tensor.transpose(held[:, a * STEP : a * STEP + P], piece(picked, (first + a) * P, (first + a + 1) * P)[0], ident[:])
            for lo, hi in ((0, early), (early, n)):
                columns = kept([P, hi - lo], F32, "ts_col%d" % (first + lo))
                nc.scalar.copy(columns[:], held[:, lo * STEP : hi * STEP : STEP])
                for a in range(lo, hi):
                    ts_col[first + a] = columns[:, a - lo : a - lo + 1]

        def turn_bias():
            held = bank("turned")
            nc.tensor.transpose(held[:, 0:P], b_rows[:], ident[:])
            columns = by_scalar([P, N_TILES], F32, "bias")
            nc.scalar.copy(columns[:], held[:, 0:N_TILES])
            return columns

        def scale_turned(a, acc):
            scaled_blocks[a] = by_scalar([P, M], F32, "block%d" % a)
            nc.scalar.activation(scaled_blocks[a][:], acc[:], ACT.Copy, scale=ts_col[a])

        def turn_back(dst, a, m):
            nc.tensor.transpose(dst, scaled_blocks[a][:, m * P : (m + 1) * P], ident[:])

        def product(acc, lo, hi):
            scaled = by_vector([P, hi - lo], F32, "scaled")
            nc.vector.tensor_tensor(scaled[:], acc[:, 0 : hi - lo], piece(picked, lo, hi)[0], ALU.mult)
            return scaled

        def silu(dst, src, m):
            nc.scalar.activation(dst, src, ACT.Silu, bias=bias[:, m : m + 1])

        def store(m, lo, hi, src):
            nc.sync.dma_start(out[m * P : (m + 1) * P, lo:hi], src)

        def store_tiles(m, n, lo, hi, src):
            nc.sync.dma_start(out[m * P : (m + n) * P, lo:hi].rearrange("(t p) j -> p t j", p=P), src)

        def finish(m, lo, hi, src):
            result = by_scalar([P, hi - lo], F32, "result")
            silu(result[:], src[:], m)
            store(m, lo, hi, result[:])

        identity()
        nc.vector.memset(tab_s[0 : P - GROUP, :], 0)
        nc.vector.memset(plane_s[:], 0)
        nc.vector.memset(w4_s[:], 0)
        nc.vector.memset(b_rows[:], 0.0)
        nc.scalar.activation(warm[:], ones[:, 0:1], ACT.Silu, bias=ones[:, 1:2])

        nc.sync.dma_start(ts_cols[:], ts[0].rearrange("(p a) -> p a", p=P))
        nc.sync.dma_start(offsets[:], offs)
        nc.sync.dma_start(tab_s[P - GROUP : P, :], tab_scales[0].bitcast(I32))
        load("u", 0, HALF)
        load("u", HALF, M)
        load("c", 0, CHUNK)
        for r in range(PACK):
            nc.sync.dma_start(w4_s[r:P:QUADRANT, :], w4_scales[0][r:GROUP:PACK, :].bitcast(I32))
        nc.sync.dma_start(tab_w[:], tab_words[0].rearrange("p t i -> p (t i)").bitcast(I32))
        nc.sync.dma_start(w4_w[:], w4_words[0].bitcast(I32))
        load("c", 512, 640)
        nc.sync.dma_start(b_rows[0:N_TILES, :], b.rearrange("(m p) -> m p", p=P))
        pick_scales()
        load("c", 640, 832)
        load("c", 832, 1024)
        load("c", 1536 - SHARE, 1536)
        load("c", 1024, 1536 - SHARE)
        load("c", 1536, 2048)

        ts_window()
        round_on_gpsimd(0, "u", 0, HALF)
        round_on_gpsimd(HALF, "u", HALF, M)
        quantize(0, "u", 0, M)
        round_on_gpsimd(0, "c", 0, HALF)
        round_on_scalar(HALF, "c", HALF, CHUNK)
        pick_ts(0, 1024)
        ts_to_partitions(0, 4, EARLY)
        quantize(0, "c", 0, 512)
        sums = {}
        for a in range(2):
            sums[a] = bank("acc")
            turned(sums[a], DENSE, a, True, False)
        round_on_scalar(0, "c", 512, 640)
        round_on_gpsimd(128, "c", 640, 832)
        round_on_gpsimd(320, "c", 832, 1024)
        pick_ts(1024, 1536)
        pick_words(0, 512)
        for a in range(2):
            turned(sums[a], TABLE, a, False, True)
        for a in range(2, 4):
            sums[a] = bank("acc")
            turned(sums[a], DENSE, a, True, False)
            turned(sums[a], TABLE, a, False, True)
        for a in range(BLOCKS):
            scale_turned(a, sums[a])
        pick_words(512, 1024)
        pick_words(1024, 2048)
        acc1 = {}
        for m in range(2):
            acc1[m] = bank("acc")
            direct(acc1[m], TABLE, m, 512, 1024, True, False)
        bias = turn_bias()
        back = {}
        for m in range(N_TILES):
            back[m] = bank("turned")
            for a in (1, 0):
                turn_back(back[m][:, a * P : (a + 1) * P], a, m)
        for a in (2, 3):
            for m in range(N_TILES):
                turn_back(back[m][:, a * P : (a + 1) * P], a, m)
        for m in range(2, 4):
            acc1[m] = bank("acc")
            direct(acc1[m], TABLE, m, 512, 1024, True, False)
        quantize(0, "c", 512, 1024, "ts_col0")
        round_on_gpsimd(SHARE, "c", 1024, 1536 - SHARE)
        round_on_scalar(CHUNK, "c", 1536 - SHARE, 1536)
        first = kept([P, N_TILES, CHUNK], F32, "first", "raw_c0")
        for m in range(N_TILES):
            silu(first[:, m, :], back[m][:], m)
            if m % 2:
                store_tiles(m - 1, 2, 0, CHUNK, first[:, m - 1 : m + 1, :])
        for m in range(N_TILES):
            direct(acc1[m], DENSE, m, 512, 1024, False, True)
        acc2 = {}
        for m in range(3):
            acc2[m] = bank("acc")
            direct(acc2[m], TABLE, m, 1024, 1536, True, False)
        pick_ts(1536, 2048)
        for m in range(2):
            finish(m, 512, 1024, product(acc1[m], 512, 1024))
            if m == 1:
                round_on_scalar(0, "c", 1536, 1536 + 160)
        quantize(SHARE, "c", 1024, 1536)
        round_on_gpsimd(160, "c", 1536 + 160, 2048)
        for m in range(3):
            direct(acc2[m], DENSE, m, 1024, 1536, False, True)
        for m in range(2, 4):
            finish(m, 512, 1024, product(acc1[m], 512, 1024))
            if m == 1:
                round_on_scalar(0, "c", 1536, 1536 + 160)
        acc2[3] = bank("acc")
        direct(acc2[3], TABLE, 3, 1024, 1536, True, False)
        direct(acc2[3], DENSE, 3, 1024, 1536, False, True)
        acc3 = {}
        for m in range(N_TILES):
            acc3[m] = bank("acc")
            direct(acc3[m], TABLE, m, 1536, 2048, True, False)
        for m in range(2):
            finish(m, 1024, 1536, product(acc2[m], 1024, 1536))
            if m == -3:
                round_on_scalar(0, "c", 1536, 1536 + 160)
        quantize(0, "c", 1536, 2048)
        for m in range(N_TILES):
            direct(acc3[m], DENSE, m, 1536, 2048, False, True)
        for m in range(2, 4):
            finish(m, 1024, 1536, product(acc2[m], 1024, 1536))
        for m in range(N_TILES):
            finish(m, 1536, 2048, product(acc3[m], 1536, 2048))
